import numpy as np, ml_dtypes
CORES = [10,34,74,98]
N = 4
BF = ml_dtypes.bfloat16
def gentries(a):
    return np.ascontiguousarray(a.reshape(8, 16, -1).transpose(0, 2, 1)).reshape(8, -1)
def gtable(e):
    e = np.asarray(e); return np.ascontiguousarray(e.reshape(8, -1, 16).transpose(0, 2, 1)).reshape(128, -1).astype(np.int32)
C, T, G, K1, K2, SC, ST, EPS, RO, BO = 512, 1024, 256, 192, 256, 128, 192, 10, 4, 2048
H = (N - 1) * G
WB = 16 * C + H
def ghosts(a):
    r, g = np.arange(N), np.arange(8)
    return np.concatenate([a[..., (d - 1) * G:d * G][r ^ d][:, g ^ d] for d in range(1, N)], axis=-1)
def ghostly(rng, c):
    u = np.ones(16 * H, bool); u[c[c >= 16 * T] - 16 * T] = False
    i = np.flatnonzero(c < 0); c[i] = 16 * T + rng.permutation(np.flatnonzero(u))[:len(i)]
    return c
def links(rng, room, share, far):
    ct = np.full((N, 8, 16 * C), -1, np.int64); tv = np.full((N, 8, 16 * T), WB, np.int64)
    for q in range(N):
        for g in range(8):
            for d in range(1, N):
                h = (d - 1) * G + np.flatnonzero(rng.random(G) < share); s = 16 * (d - 1) * G + rng.permutation(16 * G)[:len(h)]
                ct[q, g, h] = 16 * T + s; tv[q ^ d, g ^ d, s] = 16 * C + h
    for q in range(N):
        for g in range(8):
            o = rng.permutation(np.flatnonzero(ct[q, g] < 0)); nf = int(far * len(o))
            rk = np.argsort(rng.random((T, 16)), axis=1)
            own = rng.permutation(np.flatnonzero((rk < room[q, g][:, None]).reshape(-1) & (tv[q, g] == WB)))[:len(o) - nf]
            o = o[:len(own)]; ct[q, g, o] = own; tv[q, g, own] = o
            ct[q, g] = ghostly(rng, ct[q, g])
    return ct, tv
def stir(rng, tv, share):
    for q in range(N):
        for g in range(8):
            s = np.flatnonzero((tv[q, g] < WB) & (rng.random(16 * T) < share)); tv[q, g, s] = rng.permutation(tv[q, g, s])
    return tv
def see(x, ct):
    return np.take_along_axis(np.concatenate([x, ghosts(x)], axis=3), (ct >> 4)[:, :, None, :], 3)
def whole(rng, lo, hi, *shape):
    return rng.integers(lo, hi, shape, dtype=np.int16)
def geo(rng, ct):
    x = whole(rng, 60, 192, N, 8, 16, T); pose = np.repeat(whole(rng, -60, 61, N, 8, 16, C), 16, axis=3)
    e = (whole(rng, -64, 65, N, 8, 16, 16 * C) * whole(rng, 0, EPS + 4, N, 8, 1, 16 * C)) >> 6
    bad = rng.random((N, 8, 1, 16 * C)) < np.repeat(rng.choice(np.array([0.03, 0.1, 0.2, 0.75]), (N, 8, 1, C), p=[0.35, 0.35, 0.2, 0.1]), 16, axis=3)
    o = np.where(bad, whole(rng, 0, 256, N, 8, 16, 16 * C), see(x, ct) - pose + e)
    x0 = np.where(rng.random((N, 8, 1, T)) < 0.15, whole(rng, 0, 256, N, 8, 16, T), x + whole(rng, -2, 3, N, 8, 16, T))
    return o, x0
def pack(o, x, ct, tv):
    return {"obs": np.clip(o, 0, 255).reshape(N, 128, 16 * C).astype(np.float32).astype(BF), "x0": np.clip(x, 0, 255).reshape(N, 128, T).astype(np.float32).astype(BF),
            "ct": np.stack([gtable(a) for a in ct]), "tv": np.stack([gtable(a) for a in tv])}
def setup_inputs(rng):
    ct, tv = links(rng, np.minimum(rng.integers(2, 24, (N, 8, T)), 16), 0.6, 0.08); tv = stir(rng, tv, 0.06)
    o, x0 = geo(rng, ct)
    return pack(o, x0, ct, tv)
def setup_inputs_spread(rng):
    ct, tv = links(rng, rng.integers(1, 17, (N, 8, T)), 0.8, 0.15); tv = stir(rng, tv, 0.1)
    x = np.minimum(np.exp2(8 * rng.random((N, 8, 1, T))) * rng.random((N, 8, 16, T)), 255).astype(np.int16)
    pose = np.repeat((np.exp2(6 * rng.random((N, 8, 1, C))) * (rng.random((N, 8, 16, C)) - 0.6)).astype(np.int16), 16, axis=3)
    e = (np.exp2(6 * rng.random((N, 8, 1, 16 * C), dtype=np.float32)) * (rng.random((N, 8, 16, 16 * C), dtype=np.float32) - 0.5)).astype(np.int16)
    o = see(x, ct) - pose + e; o = np.where(rng.random((N, 8, 1, 16 * C)) < 0.1, whole(rng, 0, 256, N, 8, 16, 16 * C), o)
    x = np.where(rng.random((N, 8, 1, T)) < 0.1, whole(rng, 0, 256, N, 8, 16, T), x)
    return pack(o, x, ct, tv)
def setup_inputs_ends(rng):
    a = 16 * (C // 3); top = 16 * (T + H); sl = np.concatenate([np.arange(a), np.arange(16 * T - a, 16 * T), np.arange(top - (16 * C - 2 * a), top)])
    ct = np.zeros((N, 8, 16 * C), np.int64); tv = np.full((N, 8, 16 * T), WB, np.int64)
    for q in range(N):
        for g in range(8):
            p = rng.permutation(16 * C); j = int(np.argmin(p)); p[j] = p[0]; p[0] = 0
            ct[q, g, p] = sl; tv[q, g, sl[:2 * a]] = p[:2 * a]
            s = 1 + rng.permutation(2 * a - 1)[:H // 2]; tv[q, g, sl[s]] = WB - 1 - rng.permutation(H // 2)[:len(s)]
    rk = np.argsort(rng.random((N, 8, 16)), axis=2)[..., None]
    x = (255 * (rng.random((N, 8, 16, T)) < np.where(rk == 0, 0.875, np.where(rk == 1, 0.125, 0.5)))).astype(np.int16)
    s = see(x, ct); pf = rng.choice(np.array([0.0, 0.0, 0.05, 0.1, 0.15, 0.8]), (N, 8, 1, 16 * C))
    o = np.where(rng.random(s.shape, dtype=np.float32) < pf, 255 - s, s)
    cs = np.repeat(rng.random((N, 8, 16, C)) < np.where(rk == 0, 0.25, np.where(rk == 1, 0.75, 0.5)), 16, axis=3) ^ (rng.random(s.shape, dtype=np.float32) < 0.1)
    o = np.where(rk < 4, 255 * cs, o); last = 255 * (np.arange(16) == 15)
    for c in (0, C - 1):
        o[..., 16 * c:16 * c + 16] = np.where(rk == 0, last, np.where(rk == 1, 255 - last, s[..., 16 * c:16 * c + 16]))
    return pack(o, x, ct, tv)
def setup_inputs_corners(rng):
    ct = np.full((N, 8, 16 * C), -1, np.int64); tv = np.full((N, 8, 16 * T), WB, np.int64); far = np.zeros((N, 8, T), bool)
    pa = [16 * int(rng.integers(G // 16, G // 8)) + rng.permutation(16) for q in range(N)]; plant = []
    for q in range(N):
        for g in range(8):
            k = (g + q) % 8
            if 1 <= k <= 3:
                rf = k if q % 2 else 3 * K1 - C + (0, -1, 1)[k - 1]
                t = rng.permutation(T)[:(rf + 11) // 12]; far[q, g, t] = True; cs = rng.permutation(SC); s = 16 * t[:, None] + np.arange(16)
                ct[q, g, 16 * cs[:len(t)] + rng.integers(0, 16, len(t))] = 16 * t + rng.integers(0, 16, len(t))
                tv[q, g, s[:, :12].reshape(-1)[:rf]] = 16 * cs[:rf] + rng.integers(0, 16, rf)
                tv[q, g, s[:, 12:].reshape(-1)] = 16 * C + rng.permutation(H)[:4 * len(t)]
            elif 4 <= k <= 6:
                t = rng.permutation(T)[:K2 + k - 5]; s = (16 * t[:, None] + np.argsort(rng.random((len(t), 16)), axis=1))
                s = np.concatenate([s[:, 0], rng.permutation(s[:, 1:].reshape(-1))])[:8 * K1]
                p = rng.permutation(16 * K1)[:len(s)]; ct[q, g, p] = s; tv[q, g, s] = p
            elif k == 7:
                room = rng.choice(np.array([0, 1, 2, 3, 15, 16]), T); rk = np.argsort(rng.random((T, 16)), axis=1)
                s = np.flatnonzero((rk < room[:, None]).reshape(-1))[:16 * C]; p = rng.permutation(16 * C)[:len(s)]
                ct[q, g, p] = s; tv[q, g, s] = p
            elif q % 2:
                t = rng.permutation(T)[:6]; z = rng.permutation(16); a = pa[q]; f = 16 * int(rng.integers(G // 8, SC)) + rng.permutation(16)
                e = 16 * int(rng.integers(2 * K1, C)) + rng.permutation(16)[:3]; s = 16 * t[:, None] + np.argsort(rng.random((6, 16)), axis=1)
                ct[q, g, z[:10]] = s[0, :10]; ct[q, g, z[10:]] = s[1, :6]; ct[q, g, a[:10]] = s[1, 6:]; ct[q, g, f] = s[2]; ct[q, g, e] = s[3:, 0]
                s = 16 * t[:, None] + np.argsort(rng.random((6, 16)), axis=1)
                tv[q, g, s[0, :5]] = z[:5]; tv[q, g, s[1, :4]] = f[:4]; tv[q, g, s[2, 0]] = a[0]; tv[q, g, s[3, :4]] = f[4:8]; tv[q, g, s[4, :4]] = 16 * C + pa[q ^ 2][:4]
                plant.append((q, g, t, z, a, f))
            ct[q, g] = ghostly(rng, ct[q, g])
    o, x0 = geo(rng, ct); x0 = np.where(far[:, :, None, :], 255, x0)
    for q, g, t, z, a, f in plant:
        m = 80 * rng.integers(0, 2, 16); w = rng.integers(70, 100, (3, 16)); w[1] += m; w[2] += 80 - m; pose = rng.integers(-60, 61, (3, 16))
        x0[q, g][:, t[:3]] = w.T
        for p, j, c in ((z[:10], 0, 0), (z[10:], 1, 0), (a[:10], 1, 1), (f, 2, 2)):
            o[q, g][:, p] = (w[j] - pose[c])[:, None]
    return pack(o, x0, ct, tv)
def setup_inputs_crowd(rng):
    ct, tv = links(rng, np.full((N, 8, T), 16), 0.6, 0.05)
    for q in range(N):
        for g in range(0, 8, 2):
            c = (16 * rng.permutation(T)[:C, None] + np.argsort(rng.random((C, 16)), axis=1)).reshape(-1)
            tv[q, g] = WB; tv[q, g, c] = np.arange(16 * C)
            m = np.flatnonzero(rng.random(C) < 0.5); p = 16 * m + rng.integers(0, 16, len(m))
            tv[q, g, c[p]] = WB; c[p] = -1; ct[q, g] = ghostly(rng, c)
    o, x0 = geo(rng, ct)
    return pack(o, x0, ct, tv)
def setup_inputs_ties(rng):
    ct, tv = links(rng, rng.choice(np.array([1, 2, 3, 4, 8, 16]), (N, 8, T)), 0.7, 0.05)
    x = whole(rng, 80, 171, N, 8, 16, T); pose = np.repeat(whole(rng, -50, 51, N, 8, 16, C), 16, axis=3)
    nf = rng.choice(np.array([0, 5, 6, 7, 10, 16]), (N, 8, C, 1), p=[0.05, 0.15, 0.25, 0.15, 0.2, 0.2])
    m = np.where(np.argsort(rng.random((N, 8, C, 16)), axis=3) < nf, 4, 5).reshape(N, 8, 1, 16 * C)
    r = np.argsort(rng.random((N, 8, 16 * C, 16), dtype=np.float32), axis=3).transpose(0, 1, 3, 2)
    sg = 2 * whole(rng, 0, 2, N, 8, 16, 16 * C) - 1
    e = np.where(r < m, sg * (EPS + 1), np.where(rng.random(sg.shape, dtype=np.float32) < 0.8, 0, sg * EPS))
    return pack(see(x, ct) - pose + e, x, ct, tv)
def check_inputs(d):
    bad = []
    for k, hi in (("obs", 255), ("x0", 255), ("ct", 16 * (T + H) - 1), ("tv", WB)):
        v = np.asarray(d[k]).astype(np.float64)
        if not np.all((v >= 0) & (v <= hi) & (v == np.floor(v))): bad.append("range of " + k)
    s = np.sort(np.stack([gentries(a) for a in d["ct"]]), axis=-1)
    if np.any(s[..., 1:] == s[..., :-1]): bad.append("entries of ct differ")
    s = np.sort(np.stack([gentries(a) for a in d["tv"]]), axis=-1)
    if np.any((s[..., 1:] == s[..., :-1]) & (s[..., 1:] < WB)): bad.append("entries of tv that are not empty differ")
    return bad
def first(flag, start, k):
    f = np.roll(flag, -start, axis=-1); ix = np.argsort(~f, axis=-1, kind="stable")[..., :k]
    return (ix + start) % flag.shape[-1], np.take_along_axis(f, ix, -1)
def med(v, e):
    n = np.sum(e.reshape(N, 8, -1, 16), axis=3)
    s = np.sort(np.where(e[:, :, None, :], v, np.int16(9999)).reshape(N, 8, 16, -1, 16), axis=4)
    i = np.maximum((n + 1) // 2 - 1, 0)
    return np.take_along_axis(s, i[:, :, None, :, None], 4)[..., 0], n
def reference(obs, x0, ct, tv):
    o = obs.astype(np.int16).reshape(N, 8, 16, 16 * C); x = x0.astype(np.int16).reshape(N, 8, 16, T); xe = np.ones((N, 8, T), bool)
    lk = np.stack([gentries(a) for a in ct]).astype(np.int64); vw = np.stack([gentries(a) for a in tv]).astype(np.int64)
    live = np.ones((N, 8, 16 * C), bool); b = np.zeros((N, 8, 16, 16 * C), np.int16); be = np.zeros((N, 8, 16 * C), bool)
    fc = np.ones((N, 8, C), bool); ft = np.zeros((N, 8, T), bool)
    qi = np.arange(N)[:, None, None]; gi = np.arange(8)[None, :, None]; s16 = np.arange(16)
    for u in range(RO):
        ix, ok = first(fc, u * SC, K1); okp = np.repeat(ok, 16, axis=2)
        pt = (16 * ix[..., None] + s16).reshape(N, 8, 16 * K1); pt4 = pt[:, :, None, :]
        tr = np.take_along_axis(lk, pt, 2) >> 4
        wx = np.concatenate([x, ghosts(x)], axis=3); we = np.concatenate([xe, ghosts(xe)], axis=2)
        op = np.take_along_axis(o, pt4, 3); al = np.take_along_axis(live, pt, 2)
        ex = al & np.take_along_axis(we, tr, 2)
        dif = np.take_along_axis(wx, tr[:, :, None, :], 3) - op
        p, n = med(dif, ex); pp = np.repeat(p, 16, axis=3)
        fit = ex & (np.sum(np.abs(dif - pp) <= EPS, axis=2) >= 12)
        good = np.repeat(np.sum(fit.reshape(N, 8, K1, 16), axis=3) >= 6, 16, axis=2)
        al2 = al & ~(good & ex & ~fit)
        np.put_along_axis(live, pt, np.where(okp, al2, al), 2)
        np.put_along_axis(be, pt, np.where(okp, good & al2, np.take_along_axis(be, pt, 2)), 2)
        np.put_along_axis(b, pt4, np.where(okp[:, :, None, :], np.clip(pp + op, 0, 255), np.take_along_axis(b, pt4, 3)), 3)
        np.put_along_axis(fc, ix, False, 2)
        mk = np.zeros((N, 8, T + H), bool); mk[qi, gi, np.where(okp, tr, T)] = True
        ft = ft | mk[..., :T]
        ix, ok = first(ft, u * ST, K2); okp = np.repeat(ok, 16, axis=2); ix4 = ix[:, :, None, :]
        sl = (16 * ix[..., None] + s16).reshape(N, 8, 16 * K2); v = np.take_along_axis(vw, sl, 2)
        wb = np.concatenate([b, ghosts(b), np.zeros((N, 8, 16, 1), np.int16)], axis=3)
        we = np.concatenate([be, ghosts(be), np.zeros((N, 8, 1), bool)], axis=2)
        ex = np.take_along_axis(we, v, 2); bv = np.take_along_axis(wb, v[:, :, None, :], 3)
        m, n = med(bv, ex); has = n >= 3
        fit = np.sum(np.abs(bv - np.repeat(m, 16, axis=3)) <= EPS, axis=2) >= 12
        rej = okp & np.repeat(has, 16, axis=2) & ex & ~fit
        ox = np.take_along_axis(x, ix4, 3); oe = np.take_along_axis(xe, ix, 2)
        chg = ok & ((has != oe) | (has & oe & np.any(m != ox, axis=2)))
        np.put_along_axis(x, ix4, np.where((ok & has)[:, :, None, :], m, ox), 3)
        np.put_along_axis(xe, ix, np.where(ok, has, oe), 2)
        np.put_along_axis(vw, sl, np.where(rej, WB, v), 2)
        kill = np.zeros((N, 8, WB + 1), bool); kill[qi, gi, np.where(rej, v, WB)] = True
        live = live & ~kill[..., :16 * C]; be = be & ~kill[..., :16 * C]
        np.put_along_axis(ft, ix, False, 2)
        mk = np.zeros((N, 8, WB + 1), bool); mk[qi, gi, np.where(np.repeat(chg, 16, axis=2), v, WB)] = True
        fc = fc | np.any(mk[..., :16 * C].reshape(N, 8, C, 16), axis=3)
    yx = np.where(xe[:, :, None, :], x, 512).reshape(N, 128, T)
    yb = np.where(be[:, :, None, 16 * C - BO:], b[..., 16 * C - BO:], 512).reshape(N, 128, BO)
    yc = np.sum(live.reshape(N, 8, C, 16), axis=3) + 32 * fc
    yt = np.sum((vw < WB).reshape(N, 8, T, 16), axis=3) + 32 * ft
    return {"yx": yx.astype(np.float32).astype(BF), "yb": yb.astype(np.float32).astype(BF), "yc": yc.astype(np.float32), "yt": yt.astype(np.float32)}

@@ -1,0 +1,905 @@
+from concourse.bass import DstId, RemoteDMATransfer
+from concourse.mybir import AluOpType as A, ActivationFunctionType as F
+
+W1 = 96
+CH2 = [64, 96, 96]
+OHM = 32
+AS1 = (1, 1)
+AS2 = (1, 1)
+PE_SORT = max(AS1 + AS2) > 0
+TAIL1 = "ba"
+TAIL2 = "bb"
+SAMEQ_WAR = True
+TRED = True
+SMALL = True
+TWO = True
+MOVES = [30000, 30003, 30004, 30104, 30216, 30268, 30288, 30292, 30728, 30772]
+FOUND = []
+SWEEPS = 4
+TRIES = 0
+SEED = 1
+NC1 = 192 // W1
+XN, VE = 1792, 816
+OWN = 800
+OAB, OBB = 8192, 8192 + 32 * 256
+
+bf, f4, i4, u2 = "bfloat16", "float32", "int32", "uint16"
+hf = "float16"
+hs, WM = hf if PE_SORT else bf, max([W1] + CH2)
+SCRATCH = {}
+for _n, _s, _d in [
+    ("OB", [8192], bf), ("POOL", [OWN + 4 * 3072], bf), ("W2", [28800], bf), ("XW", [2064], bf),
+    ("XG", [3072], bf), ("OG", [3072], bf), ("BG", [4096], bf), ("SRC", [4096], bf),
+    ("SGA", [16, WM], bf), ("SGB", [16, WM], bf), ("SA0", [8, WM], bf), ("SA1", [8, WM], bf), ("IH", [128], hf), ("NIH", [128], hf),
+    ("SB0", [8, WM], hs), ("SC0", [8, WM], hs), ("SD0", [4, WM], hs), ("SB1", [8, WM], hs), ("SC1", [8, WM], hs), ("SD1", [4, WM], hs),
+    ("CT", [512], i4), ("TV", [1024], i4), ("TI", [1024], i4),
+    ("TRL", [768], f4), ("TA", [768], f4), ("TB", [768], f4), ("VC", [1280], f4), ("VL", [1280], bf), ("SO", [1280], f4),
+    ("IDS", [1280], bf), ("LW", [2176], bf), ("LOC", [832], bf), ("LS0", [384], bf), ("LS", [192], bf),
+    ("S", [2048], bf), ("ZC", [144], bf), ("SEL", [480], bf), ("PERM", [384], bf), ("ONE", [144], bf),
+    ("I", [128], bf), ("NI", [128], bf), ("ONES", [128], bf), ("ONES16", [128], bf), ("ONESB", [128], bf),
+    ("TRI", [128], bf), ("RK", [128], bf), ("M1", [128], bf), ("M2", [128], bf), ("OP32", [128], bf), ("OM32", [128], bf),
+    ("IP", [1136 if TRED else 16], bf), ("Z8", [248], bf), ("TM1", [128], bf), ("TM2", [128], bf),
+    ("KI", [8], i4), ("KC", [8], f4), ("MK", [16], f4), ("I16", [16], f4), ("BC", [4], f4), ("DUMP", [64], f4), ("ONEF", [64], f4),
+    ("XS", [4 * 768], bf), ("BS", [4 * 768], bf),
+    ("FC", [32], bf), ("AC", [32], bf), ("FT", [64], bf), ("AT", [64], bf), ("SCN", [64], f4), ("RP", [64], f4), ("RO", [64], f4),
+    ("OFU", [64], u2), ("CL", [16], u2), ("TL", [16], u2), ("OOU", [192], u2), ("TRU", [192], u2), ("TRG", [192], f4),
+    ("DE", [192], bf), ("U", [256], bf), ("FX", [256], bf), ("PM", [256], bf), ("FIT", [192], bf), ("MR", [192], bf), ("KL", [256], f4),
+    ("A0", [192], bf), ("B0", [192], bf), ("ABT", [512], bf), ("CS", [8, 33], f4), ("FF", [8, 32], bf),
+    ("VCU", [256], u2), ("SOU", [256], u2), ("ADU", [256], u2), ("VCF", [256], f4), ("VLG", [256], bf), ("OX", [256], bf),
+    ("EM", [256], bf), ("NH", [256], bf), ("MH", [256], bf), ("ML", [256], bf), ("X0", [256], bf), ("XQ", [256], bf),
+    ("NE", [256], bf), ("AM", [256], bf), ("SN", [256], bf), ("VA", [256], bf),
+    ("AB", [512], bf), ("DS", [128], bf), ("ASU", [128], u2),
+]:
+    SCRATCH[_n] = ("sbuf", [128] + _s, _d)
+SCRATCH["PA"] = ("psum", [128, 8, 128], f4)
+SCRATCH["PB"] = ("psum", [128, 8, 128], f4)
+BANKS = ("E0", "E1", "E2", "E3")
+for _n in BANKS:
+    SCRATCH[_n] = ("psum", [128, 512], f4)
+NDMA = 12
+SEMAPHORES = ["cv", "ca", "cp", "cg", "sent"] + ["xa%d" % u for u in range(4)] + ["ba%d" % u for u in range(4)] + ["d%d" % j for j in range(NDMA)]
+QSEM = {"v": "cv", "a": "ca", "p": "cp", "g": "cg"}
+LAT, GAT, SCA, PEC = 110.0, 1.56, 3.8, 0.5
+
+
+def meta(n):
+    return ("psum", [128, 512], f4) if n[0] == "#" else SCRATCH[n]
+
+
+def R(name, *idx, p=None):
+    return ("ref", name, tuple(slice(x[0], x[1], x[2] if len(x) > 2 else None) if isinstance(x, tuple) else x for x in idx), p)
+
+
+def IND(win, off):
+    return ("ind", win, off)
+
+
+def spans(r):
+    shp = meta(r[1])[1][1:]
+    idx = list(r[2]) + [slice(None)] * (len(shp) - len(r[2]))
+    rg = [range(*x.indices(n)) if isinstance(x, slice) else range(x, x + 1) for x, n in zip(idx, shp)]
+    if len(shp) == 1:
+        return [(rg[0][0], rg[0][-1] + 1)], len(rg[0])
+    return [(a * shp[1] + rg[1][0], a * shp[1] + rg[1][-1] + 1) for a in rg[0]], len(rg[0]) * len(rg[1])
+
+
+def is_ref(x):
+    return isinstance(x, tuple) and len(x) > 0 and x[0] in ("ref", "ind")
+
+
+def build():
+    ops, acc, banks, ndma, uses, lab = [], {}, {}, [0], [0], ["start", 0]
+
+    def add(q, calls, reads, writes, cost, kind="c", extra=(), lat=0.0, sem=None):
+        me = len(ops)
+        deps = {}
+        for e in extra:
+            deps[e] = True
+        touched = set()
+        for refs, wr in ((reads, False), (writes, True)):
+            for r in refs:
+                if r[1] not in SCRATCH and r[1][0] != "#":
+                    continue
+                lst = acc.setdefault(r[1], [])
+                for lo, hi in spans(r)[0]:
+                    for (a, b, o, w) in lst:
+                        if a < hi and lo < b and o != me and (w or wr):
+                            need = ops[o]["q"] != q or ops[o]["kind"] != "c" or kind != "c" or (w and not wr) or (SAMEQ_WAR and q != "p")
+                            deps[o] = deps.get(o, False) or need
+                    if wr:
+                        lst[:] = [t for t in lst if not (lo <= t[0] and t[1] <= hi)]
+                    lst.append((lo, hi, me, wr))
+                    if meta(r[1])[0] == "psum":
+                        for bk in range(lo // 512, (hi - 1) // 512 + 1):
+                            touched.add((r[1], bk))
+        for bk in touched:
+            st = banks.setdefault(bk, [q, [], []])
+            if st[0] != q:
+                st[0], st[1], st[2] = q, [], st[1]
+            for o in st[2]:
+                deps[o] = True
+            st[1].append(me)
+        ops.append({"q": q, "calls": calls, "deps": deps, "cost": cost, "kind": kind, "lat": lat, "sem": sem, "tag": lab[0] + str(q), "rd": lab[1],
+                    "use": max([b[0] for b in touched if b[0][0] == "#"] or [""])})
+        return me
+
+    def parts(out, ins):
+        rd, wr = [], []
+        for x in ins:
+            if is_ref(x):
+                rd += [x[1], x[2]] if x[0] == "ind" else [x]
+        if out[0] == "ind":
+            wr.append(out[1]); rd.append(out[2])
+        else:
+            wr.append(out)
+        return rd, wr
+
+    def vec(meth, out, *args):
+        rd, wr = parts(out, args)
+        full = [x for x in (out,) + args if is_ref(x) and x[0] == "ref" and spans(x)[1] > 1] or [out]
+        n = max(spans(x)[1] for x in full)
+        f = 0.5 if all(meta(x[1])[2] in (bf, u2, hf) for x in full) else 1.0
+        if meth == "tensor_tensor":
+            f = 1.0 if any(meta(x[1])[0] == "psum" for x in args[:2] if x[0] == "ref") else 2.0
+        if out[0] == "ind":
+            f = SCA
+        elif any(is_ref(x) and x[0] == "ind" for x in args):
+            f = GAT
+        return add("v", [(meth, (out,) + args, {})], rd, wr, 60 + n * f)
+
+    def tt(out, a, b, op): return vec("tensor_tensor", out, a, b, op)
+    def ts(out, a, s1, o1, s2=None, o2=None):
+        return vec("tensor_scalar", out, a, s1, s2, o1) if o2 is None else vec("tensor_scalar", out, a, s1, s2, o1, o2)
+    def cp(out, a): return vec("tensor_copy", out, a)
+    def ms(out, c): return vec("memset", out, c)
+
+    def act(out, a, func=F.Identity, bias=0.0, scale=1.0):
+        rd, wr = parts(out, (a, bias, scale))
+        return add("a", [("activation", (out, a, func), {"bias": bias, "scale": scale})], rd, wr,
+                   90 + spans(out)[1] * (GAT if a[0] == "ind" else 1.0))
+
+    def nb():
+        uses[0] += 1
+        return "#%d" % uses[0]
+
+    def mm(groups, go_on=False, close=True):
+        calls, rd, wr, cost = [], [], [], 40.0
+        for gr in groups:
+            for j, (o, l, r) in enumerate(gr):
+                calls.append(("matmul", (o, l, r, j == 0 and not go_on, j == len(gr) - 1 and close), {}))
+                rd += [l, r]; wr.append(o)
+                cost += PEC * max(min(64, spans(l)[1]), spans(r)[1])
+        return add("p", calls, rd, wr, cost)
+
+    def gp(meth, out, *args, **kw):
+        rd, wr = parts(out, args)
+        return add("g", [(meth, (out,) + args, kw)], rd, wr, 200 + 2 * spans(out)[1])
+
+    def iota(out, pat, base=0, cm=0):
+        if SCRATCH[out[1]][2] == i4:
+            return gp("iota", out, pat, base, cm)
+        return gp("iota", out, pat, base, cm, allow_small_or_imprecise_dtypes=True)
+
+    def fill(out, c): return iota(out, [[0, spans(out)[1]]], c)
+
+    def asel(out, a, pat, op, base, cm=1): return gp("affine_select", out, a, pat, op, 0.0, base, cm)
+
+    def dma(q, out, a, nbytes):
+        j = ndma[0]; ndma[0] += 1
+        return add(q, [("dma_start", (out, a), {})], [a], [out], 80.0, kind="d", lat=2400 + nbytes / 150.0, sem=("d%d" % j, 16))
+
+    def send(src, u, dst, d0, sem, extra=()):
+        s = add("g", [("send", (src, u, dst, d0, sem), {})], [R(src, (768 * u, 768 * u + 768))], [], 1200.0, kind="s", extra=extra, lat=4000.0)
+        return add(None, [], [], [R(dst, (d0, d0 + 768))], 0.0, kind="r", extra=(s,), sem=(sem, 8))
+
+    I, NI, ONES = R("I"), R("NI"), R("ONES")
+    def C(k): return R("ZC", (15 - k, 143 - k))
+    def S(k): return R("S", (128 * k, 128 * k + 128))
+    def col(name, j): return R(name, (j, j + 1))
+
+    def turn(src, s0, dst, u):
+        for bk, ds in ((nb(), (0, 1)), (nb(), (2,))):
+            mm([[(R(bk, (256 * j, 256 * j + 256)), R("PERM", (128 * d, 128 * d + 128)), R(src, (s0 + 256 * d, s0 + 256 * d + 256)))] for j, d in enumerate(ds)])
+            act(R(dst, (768 * u + 256 * ds[0], 768 * u + 256 * ds[-1] + 256)), R(bk, (0, 256 * len(ds))))
+
+    dma("s", R("XW", (256, 1280)), R("x0"), 262144)
+    dma("a", R("CT"), R("ct"), 262144)
+    dma("s", R("OB", (0, 3072)), R("obs", (0, 3072)), 1310720)
+    dma("a", R("TV"), R("tv"), 1835008)
+    dma("s", R("OB", (3072, 8192)), R("obs", (3072, 8192)), 3145728)
+    ms(R("ONE"), 1.0)
+    one = R("ONE", (0, 128))
+    asel(R("PERM", (0, 128)), one, [[-32, 4], [16, 2], [-1, 16]], A.is_equal, -16)
+    asel(R("PERM", (128, 256)), one, [[-64, 2], [32, 2], [-1, 32]], A.is_equal, -32)
+    asel(R("PERM", (256, 384)), one, [[-64, 2], [16, 4], [-1, 16]], A.is_equal, -48)
+    turn("XW", 256, "XS", 0)
+    send("XS", 0, "XW", 1280, "xa0")
+    asel(I, one, [[-1, 128]], A.is_equal, 0)
+    asel(R("TM1"), one, [[-16, 8], [0, 16]], A.is_ge, 0)
+    asel(ONES, R("TM1"), [[16, 8], [0, 16]], A.is_ge, 15, -1)
+    asel(R("TRI"), ONES, [[1, 128]], A.is_ge, 0, -1)
+    iota(R("KI", (0, 1)), [[0, 1]], 0, 1)
+    iota(R("I16"), [[1, 16]])
+    ts(R("KI", (4, 5)), R("KI", (0, 1)), 15, A.bitwise_and)
+    cp(col("KC", 0), R("KI", (4, 5)))
+    ts(R("MK"), R("I16"), col("KC", 0), A.is_equal)
+    ts(col("KC", 1), col("KC", 0), -4096.0, A.add)
+    ts(col("KC", 2), col("KC", 0), float(W1), A.mult, -784.0, A.add)
+    ts(col("KC", 3), col("MK", 2), float(OWN), A.mult)
+    ts(R("BC"), R("I16", (0, 4)), 3072.0, A.mult)
+    ts(R("BC"), R("BC"), col("MK", 3), A.mult, col("KC", 3), A.add)
+    ms(R("ZC"), 0.0)
+    cp(R("ZC", (15, 143, 16)), R("ONES", (0, 128, 16)))
+    for k in range(16):
+        act(S(k), ONES, F.Identity, 0.0, col("MK", k))
+    ts(NI, I, -1.0, A.mult)
+    if PE_SORT:
+        cp(R("IH"), I); ts(R("NIH"), I, -1.0, A.mult)
+    ts(R("TM1"), R("TRI"), 2.0, A.mult)
+    tt(R("TM1"), R("TM1"), ONES, A.subtract)
+    ts(R("TM2"), I, -64.0, A.mult)
+    tt(R("M1"), R("TM2"), R("TM1"), A.add)
+    tt(R("M2"), R("TM2"), R("TM1"), A.subtract)
+    ts(R("TM2"), I, 32.0, A.mult)
+    tt(R("OP32"), ONES, R("TM2"), A.add)
+    tt(R("OM32"), ONES, R("TM2"), A.subtract)
+    ts(R("TM2"), I, -4096.0, A.mult)
+    tt(R("TM1"), R("TRI"), ONES, A.subtract)
+    tt(R("RK"), R("TM1"), R("TM2"), A.add)
+    act(R("ONES16"), ONES, F.Identity, 0.0, 16.0)
+    act(R("ONESB"), ONES, F.Identity, 0.0, 2.0 ** 20)
+    fill(R("SEL"), 0)
+    for h in range(2):
+        asel(R("SEL", (240 * h + 112, 240 * h + 128), p=(0, 32)), R("ONE", (0, 16), p=(0, 32)), [[-1, 16]], A.is_equal, -16 * h)
+    if TRED:
+        fill(R("IP"), 0); fill(R("Z8"), 0)
+        for c in range(8):
+            act(R("IP", (112 + 128 * c, 128 + 128 * c)), R("I", (16 * c, 16 * c + 16)))
+        cp(R("Z8", (120, 128)), R("ONES", (0, 128, 16)))
+    ms(R("ONEF"), 1.0)
+    iota(R("DUMP"), [[16, 64]], 1024, 1)
+    ts(R("TI", (0, 512)), R("CT"), 4, A.logical_shift_right)
+    cp(R("TRU"), R("TI", (0, 192)))
+    cp(R("TRL", (256, 768)), R("TI", (0, 512)))
+    ts(R("TI", (512, 1024)), R("CT"), 4, A.logical_shift_right, 31, A.bitwise_and)
+    cp(R("TA", (256, 768)), R("TI", (512, 1024)))
+    ts(R("TI", (0, 512)), R("CT"), 9, A.logical_shift_right)
+    cp(R("TB", (256, 768)), R("TI", (0, 512)))
+    fill(R("TRL", (0, 256)), XN); fill(R("TA", (0, 256)), 0); fill(R("TB", (0, 256)), 99)
+    fill(R("XW", (0, 256)), 512); fill(R("XW", (2048, 2064)), 512)
+    fill(R("POOL", (0, 16)), 2048); fill(R("POOL", (784, 800)), 2048)
+    fill(R("LOC"), -1024)
+    iota(R("LOC", (768, 816)), [[1, 48]], 1)
+    iota(R("BG", (0, 1280)), [[16, 80], [0, 16]])
+    iota(R("BG", (1280, 2560)), [[0, 80], [1, 16]])
+    iota(R("BG", (2560, 2752)), [[16 * W1, NC1], [0, W1]])
+    iota(R("BG", (2752, 2944)), [[-16 * W1, NC1], [0, W1]], 16 * W1 * (NC1 - 1))
+    iota(R("BG", (2944, 3328)), [[0, 2 * NC1], [1, W1]])
+    for a, n in ((0, 512), (512, 512), (1024, 256)):
+        e = R(nb(), (0, n))
+        mm([[(e, C(0), R("BG", (a, a + n))), (e, C(1), R("BG", (1280 + a, 1280 + a + n)))]])
+        act(R("IDS", (a, a + n)), e, F.Identity, 0.0, 0.0625)
+    e = R(nb(), (0, 384))
+    mm([[(e, C(0), R("BG", (2560, 2944))), (e, C(1), R("BG", (2944, 3328)))]])
+    act(R("LS0"), e, F.Identity, 0.0, 0.0625)
+    iota(R("SO"), [[16, 1280]], 8192, 1)
+    for j in range(2):
+        e, v, t = R(nb()), R("TV", (512 * j, 512 * j + 512)), (256 + 512 * j, 768 + 512 * j)
+        ti = R("TI", (512 * j, 512 * j + 512))
+        ts(e, v, 8192.0, A.is_ge, 65536.0, A.mult)
+        act(R("AB"), e, F.Identity, float(W1), -(W1 - 1.0) / 65536.0)
+        tt(e, e, v, A.add)
+        tt(R("SO", t), e, R("SO", t), A.min)
+        ts(ti, v, 15, A.bitwise_and)
+        tt(R("VL", t), ti, R("AB"), A.mult)
+        ts(ti, v, 4, A.logical_shift_right)
+        ts(R("VC", t), ti, 256.0, A.add)
+    fill(R("VC", (0, 256)), VE); fill(R("VL", (0, 256)), 0)
+    for j in range(8):
+        iota(R("W2", (1024 * j, 1024 * j + 1024)), [[0, 1024]])
+    ms(R("FC"), 1.0); ms(R("AC", (0, 12)), 0.0); ms(R("AC", (12, 32)), 1.0)
+
+    def worklist(fl, al, n, s0, K, out, c0, c1):
+        act(R("LW", (0, K)), R("IDS", (0, K)))
+        b = nb()
+        mm([[(R(b, (0, n)), ONES, R(fl))], [(R(b, (64, 64 + n)), R("RK"), R(fl))]])
+        vec("tensor_tensor_scan", R("SCN", (s0, n)), R("ONEF", (s0, n)), R(b, (s0, n)), 4095.0, A.mult, A.add)
+        if s0:
+            vec("tensor_tensor_scan", R("SCN", (0, s0)), R("ONEF", (0, s0)), R(b, (0, s0)), col("SCN", n - 1), A.mult, A.add)
+        tt(R("RP", (0, n)), R(b, (64, 64 + n)), R("SCN", (0, n)), A.add)
+        tt(R("RO", (0, n)), R("RP", (0, n)), R("DUMP", (0, n)), A.min)
+        cp(R("OFU", (0, n)), R("RO", (0, n)))
+        ts(R(al), R("RP", (0, n)), K - 0.5, A.is_ge)
+        for c in range(c0, c1, 32):
+            d = min(c + 32, c1)
+            cp(IND(R("LW"), R("OFU", (c, d))), R("IDS", (256 + 16 * c, 256 + 16 * d)))
+        m = K // 16
+        e = R(nb(), (0, m))
+        mm([[(e, C(k), R("LW", (k, K, 16))) for k in range(16)]])
+        cp(R(out, (0, m)), e)
+
+    def median(P, SA, W, out, level, hist):
+        def q(nm):
+            return lambda a, b=None, s=None: R(nm, (a, a + 1 if b is None else b, s), (0, W))
+        z = SA[2] if TWO else "0"
+        p, a_, b_, c_, d_ = q(P), q(SA), q("SB" + z), q("SC" + z), q("SD" + z)
+        lo, hi = A.min, A.max
+        if level:
+            def other(s0, pairs):
+                for j, (x, y) in enumerate(pairs):
+                    hist[s0 + j] = hist[s0 + j] + [(I if x[0] == SA else R("IH"), R(SA if x[0] == SA else x[0] + z, x[1], (0, W))), (R("NIH"), R(y[0] + z, y[1], (0, W)))]
+                mm([[(R(P, s, (0, W)), l, r) for l, r in hist[s]] for s in range(s0, s0 + len(pairs))])
+            tt(b_(0, 4), p(0, 4), a_(0, 4), lo); other(0, [((SA, j), ("SB", j)) for j in range(4)])
+            tt(b_(4, 8), p(4, 8), a_(4, 8), hi); other(4, [((SA, j), ("SB", j)) for j in range(4, 8)])
+            tt(d_(0, 2), p(0, 2), b_(4, 6), lo); tt(c_(0, 2), p(2, 4), b_(6, 8), hi)
+            if level > 1:
+                other(0, [(("SB", 4 + j), y) for j, y in enumerate((("SD", 0), ("SD", 1), ("SC", 0), ("SC", 1)))])
+            tt(c_(6, 8), p(4, 6), b_(0, 2), lo); tt(d_(2, 4), p(6, 8), b_(2, 4), hi)
+            if level > 1:
+                other(4, [(("SB", j), y) for j, y in enumerate((("SC", 6), ("SC", 7), ("SD", 2), ("SD", 3)))])
+            else:
+                tt(p(4, 6), p(4, 6), b_(0, 2), hi); tt(p(0, 2), p(0, 2), b_(4, 6), hi)
+                tt(p(2, 4), p(2, 4), b_(6, 8), lo); tt(p(6, 8), p(6, 8), b_(2, 4), lo)
+            tt(c_(2, 4), p(4, 6), d_(0, 2), lo); tt(c_(4, 6), p(2, 4), d_(2, 4), hi)
+            if level > 2:
+                other(4, [(("SD", j), ("SC", 2 + j)) for j in range(2)]); other(2, [(("SD", 2 + j), ("SC", 4 + j)) for j in range(2)])
+            else:
+                tt(p(4, 6), p(4, 6), d_(0, 2), hi); tt(p(2, 4), p(2, 4), d_(2, 4), lo)
+            net = [
+                (b_(0, 8, 2), p(0, 8, 2), c_(0, 8, 2), lo), (b_(1, 8, 2), p(1, 8, 2), c_(1, 8, 2), hi),
+                (p(0, 8, 2), p(0, 8, 2), c_(0, 8, 2), hi), (p(1, 8, 2), p(1, 8, 2), c_(1, 8, 2), lo),
+                (c_(2, 4), p(1, 8, 4), b_(0, 8, 4), lo), (d_(0, 4), p(0, 8, 2), b_(1, 8, 2), lo),
+                (p(1, 8, 2), p(1, 8, 2), b_(0, 8, 2), hi), (p(2, 8, 4), p(2, 8, 4), b_(3, 8, 4), hi),
+                (c_(0, 2), p(3, 8, 4), d_(1, 4, 2), hi), (p(0, 8, 4), p(1, 8, 4), d_(0, 3, 2), lo), (p(3), p(3), d_(1), lo),
+                (b_(0), p(6), c_(0), hi), (b_(1), p(6), c_(0), lo), (b_(2, 4), p(0, 4, 2), c_(1, 4, 2), lo),
+                (p(5), p(4), c_(2), lo), (p(7), p(4), c_(2), hi), (b_(2), p(3), b_(2), hi),
+                (p(5, 8, 2), p(5, 8, 2), b_(0, 2), lo), (b_(4), p(5), b_(2), hi), (p(7), p(7), b_(3), hi), (out, p(7), b_(4), hi)]
+        else:
+            net = [
+                (b_(0, 4), p(4, 8), a_(4, 8), lo), (b_(4, 8), p(4, 8), a_(4, 8), hi), (p(4, 8), p(0, 4), a_(0, 4), lo), (p(0, 4), p(0, 4), a_(0, 4), hi),
+                (c_(2, 4), p(6, 8), b_(2, 4), lo), (a_(0, 4), p(0, 4), b_(4, 8), lo), (c_(0, 2), p(2, 4), b_(6, 8), hi),
+                (p(2, 4), p(4, 6), b_(0, 2), lo), (p(4, 8), p(4, 8), b_(0, 4), hi), (p(0, 2), p(0, 2), b_(4, 6), hi),
+                (c_(4, 6), p(6, 8), a_(2, 4), hi), (c_(6, 8), p(6, 8), a_(2, 4), lo), (p(6, 8), p(4, 6), a_(0, 2), lo), (p(4, 6), p(4, 6), a_(0, 2), hi),
+                (b_(0, 4), p(1, 8, 2), c_(1, 8, 2), lo), (b_(4, 8), p(1, 8, 2), c_(1, 8, 2), hi),
+                (p(1, 8, 2), p(0, 8, 2), c_(0, 8, 2), lo), (p(0, 8, 2), p(0, 8, 2), c_(0, 8, 2), hi),
+                (c_(2, 4), p(1, 8, 4), b_(0, 3, 2), lo), (a_(0, 4), p(0, 8, 2), b_(4, 8), lo),
+                (p(1, 8, 2), p(1, 8, 2), b_(0, 4), hi), (p(2, 8, 4), p(2, 8, 4), b_(5, 8, 2), hi),
+                (c_(0, 2), p(3, 8, 4), a_(1, 4, 2), hi), (p(0, 8, 4), p(1, 8, 4), a_(0, 3, 2), lo), (p(7), p(7), a_(3), lo),
+                (b_(0), p(2), c_(1), hi), (b_(1), p(2), c_(1), lo), (b_(2, 4), p(0, 8, 6), c_(0, 4, 3), lo),
+                (p(1), p(4), c_(2), lo), (p(3), p(4), c_(2), hi), (b_(2), p(7), b_(2), hi),
+                (p(1, 4, 2), p(1, 4, 2), b_(0, 2), lo), (b_(4), p(1), b_(2), hi), (p(3), p(3), b_(3), hi), (out, p(3), b_(4), hi)]
+        for o, x, y, f in net:
+            tt(o, x, y, f)
+
+    def stage(P, SA, w0, W, terms, src, thr, M, zthr, fx):
+        g, z, u, x = R(nb(), (0, W)), R(nb(), (0, W)), R("U", (w0, w0 + W)), R("FX", (w0, w0 + W))
+        mm([[(g, C(k), src(k)) for k in range(16)]])
+        if thr is None:
+            act(u, g, F.Relu, -32.0, 1.0 / 128)
+        else:
+            ts(u, g, thr, A.is_ge, 32.0, A.mult)
+        mm([[(z, R(M), u)]])
+        ts(x, z, zthr, A.is_le, fx, A.mult)
+        for h in (1, 0):
+            bk = nb()
+            mm([[(R(bk, (j * W, j * W + W)), l, r) for l, r in terms(8 + 4 * h + j) + [(S(8 + 4 * h + j), x)]] for j in range(4)])
+            act(R(SA, (4 * h, 4 * h + 4), (0, W)), R(bk, (0, 4 * W)))
+            gr = [[(R(P, 4 * h + j, (0, W)), l, r) for l, r in terms(4 * h + j) + [(S(4 * h + j), x)]] for j in range(4)]
+            mm(gr)
+
+    def fits(W, terms, mlo, mhi, tail):
+        def fill(j, m):
+            b = nb()
+            mm([[(R(b, (i * W, i * W + W)), l, r) for l, r in terms(4 * j + i) + [(NI, m)]] for i in range(4)])
+            return R(b, (0, 4 * W))
+        for j in range(4):
+            e = fill(j, mlo)
+            sa, sb = R("SGA", (4 * j, 4 * j + 4), (0, W)), R("SGB", (4 * j, 4 * j + 4), (0, W))
+            if tail in "ab":
+                act(sa, e, F.Abs)
+                if tail == "a":
+                    ts(sb, sa, 10.5, A.is_le, 2.0, A.mult)
+                else:
+                    act(sb, sa, F.Sign, 10.5, -1.0)
+                continue
+            act(sa, e, F.Sign, 10.5)
+            if mhi is not mlo:
+                e = fill(j, mhi)
+            if tail == "d":
+                ts(sb, e, 10.5, A.is_le, 2.0, A.mult)
+            else:
+                act(sb, e, F.Sign, 10.5, -1.0)
+        return [(C(k), R(s, k, (0, W))) for k in range(16) for s in (("SGB",) if tail in "ab" else ("SGA", "SGB"))], {"d": 39.0, "b": 7.0}.get(tail, 23.0)
+
+    def total(e, tm, split):
+        h = len(tm) - 4 if split else len(tm)
+        mm([[(e, l, r) for l, r in tm[:h]]], False, not split)
+        if split:
+            mm([[(e, l, r) for l, r in tm[h:]]], True)
+
+    def places(c0, n):
+        ts(R("DS", (0, n)), R("TRL", (256 + c0, 256 + c0 + n)), XN - 0.5, A.is_ge, -16384.0, A.mult)
+        e = R(nb(), (0, n))
+        mm([[(e, ONES, R("LOC", (256 + c0, 256 + c0 + n))), (e, I, R("DS", (0, n)))]])
+        ts(R("ASU", (0, n)), e, col("KC", 2), A.add, 0.0, A.max)
+
+    par = [0]
+    for u in range(4):
+        lab[:] = ["list", u]
+        if u:
+            worklist("FC", "AC", 32, 8 * u, 192, "CL", *((8, 24) if u == 1 else (0, 32)))
+            e = R(nb(), (0, 192)); cl = R("CL", (0, 12))
+            mm([[(e, R("ONES16"), R("LW", (0, 192)))]])
+            ts(R("OOU"), e, col("KC", 1), A.add, 0.0, A.max)
+            cp(R("TRU"), IND(R("TRL"), cl))
+            lab[0] = "ab"
+            act(R("A0"), IND(R("TA"), cl)); act(R("B0"), IND(R("TB"), cl))
+            lab[0] = "more"
+            act(R("TRG"), IND(R("TRL"), cl))
+            act(R("LS"), R("LS0", (192, 384) if u == 2 else (0, 192)), F.Identity, col("BC", u))
+            cp(IND(R("LOC"), cl), R("LS"))
+            og, trg = "OG", ("TRG", 0)
+        else:
+            act(R("A0"), R("TA", (256, 448))); act(R("B0"), R("TB", (256, 448)))
+            act(R("LOC", (256, 448)), R("LS0", (0, 192)), F.Identity, col("BC", 0))
+            og, trg = "OB", ("TRL", 256)
+        places(0, 48)
+        ts(R("DE"), R(trg[0], (trg[1], trg[1] + 192)), XN - 0.5, A.is_ge, -64.0, A.mult)
+        order = list(range(NC1))[::-1] if u == 2 else list(range(NC1))
+        xg = []
+        for n, c in enumerate(order):
+            w0 = c * W1; lab[0] = "x%d" % n
+            for h in range(2):
+                a, b = w0 + h * W1 // 2, w0 + (h + 1) * W1 // 2
+                gx = (R("XG", (16 * a, 16 * b)), IND(R("XW", (256, 2064)), R("TRU", (a, b))))
+                xg.append(cp(*gx) if n == 0 and (u or h) else act(*gx))
+                if u:
+                    act(R("OG", (16 * a, 16 * b)), IND(R("OB"), R("OOU", (a, b))))
+
+        def onehot():
+            b1, b2, b3, top, few = nb(), nb(), nb(), (0, 96), (0, 32)
+            lab[0] = "hot"
+            mm([[(R(b1, (128 * j, 128 * j + 128), p=top), R("A0" if j < 2 else "B0", (96 * (j % 2), 96 * (j % 2) + 96)), I)] for j in range(4)])
+            act(R("ABT", p=top), R(b1, p=top))
+            for a in range(32):
+                ts(R("W2", (OAB + 256 * a, OAB + 256 * a + 256), p=top), R("ABT", (0, 256), p=top), float(a), A.is_equal)
+            c0 = 0 if OHM else 1; lab[0] = "hotb"
+            for b in range(c0, 33):
+                o, i_ = R("W2", (OBB + 256 * b, OBB + 256 * b + 256), p=top), R("ABT", (256, 512), p=top)
+                if b <= OHM:
+                    act(o, i_, F.Sign, 0.5 - b)
+                else:
+                    ts(o, i_, b - 1.0, A.is_equal)
+            lab[0] = "flag"
+            for g in range(8):
+                mm([[(R(b2, (33 * g + c0, 33 * g + 33), p=few), R("W2", (OAB + x, OAB + 8192, 256), p=top), R("W2", (OBB + 256 * c0 + x, OBB + 256 * 33, 256), p=top))
+                     for x in [128 * h + 16 * g + k for h in range(2) for k in range(16)]]])
+            if OHM:
+                act(R("CS", p=few), R(b2, (0, 264), p=few))
+                tt(R("FF", (0, 8), (0, OHM), p=few), R("CS", (0, 8), (0, OHM), p=few), R("CS", (0, 8), (1, OHM + 1), p=few), A.is_gt)
+                if OHM < 32:
+                    ts(R("FF", (0, 8), (OHM, 32), p=few), R("CS", (0, 8), (OHM + 1, 33), p=few), 0.5, A.is_gt)
+            else:
+                for g in range(8):
+                    act(R("FF", g, p=few), R(b2, (33 * g + 1, 33 * g + 33), p=few), F.Sign)
+            e = R(b3, (0, 64))
+            gr = [(e, I, R("AT")), (e, I, R("FT"))] if u else [(e, R("SEL", (128, 256), p=few), R("ONE", (0, 64), p=few))]
+            gr += [(R(b3, (h, 64, 2)), R("SEL", (240 * h + 112 - 16 * g, 240 * h + 240 - 16 * g), p=few), R("FF", g, p=few)) for g in range(8) for h in range(2)]
+            mm([gr])
+            ts(R("FT"), e, 1.75 if u else 0.5, A.is_ge)
+            worklist("FT", "AT", 64, 12 * u, 256, "TL", 0, 64)
+            tl = R("TL")
+            cp(R("VCU"), IND(R("VC"), tl)); act(R("VLG"), IND(R("VL"), tl))
+            lab[0] = "late"
+            cp(R("SOU"), IND(R("SO"), tl)); act(R("VCF"), IND(R("VC"), tl)); act(R("OX"), IND(R("XW", (0, 1280)), tl))
+            ts(R("EM"), R("VCF"), VE - 0.5, A.is_ge, -2.0 ** 35, A.mult)
+            for w0 in range(0, 256, 64):
+                lab[0] = "loc%d" % w0
+                act(R("SRC", (16 * w0, 16 * w0 + 1024)), IND(R("LOC"), R("VCU", (w0, w0 + 64))))
+                e = R(nb(), (0, 64))
+                mm([[(e, C(k), R("SRC", (16 * w0 + k, 16 * w0 + 1024, 16))) for k in range(16)] + [(e, I, R("VLG", (w0, w0 + 64)))]])
+                ts(R("ADU", (w0, w0 + 64)), e, 0.0, A.max)
+
+        def send_b(done):
+            lab[0] = "send"
+            act(R("BG", (0, 768)), IND(R("POOL", (784, OWN + 3072 * u + 16 * W1 * done)), R("ASU", (0, 48))))
+            turn("BG", 0, "BS", u)
+            send("BS", u, "POOL", 16, "ba%d" % u, extra=xg)
+
+        def terms1(c):
+            return lambda k: [(I, R("XG", (16 * W1 * c + k, 16 * W1 * (c + 1), 16))), (NI, R(og, (16 * W1 * c + k, 16 * W1 * (c + 1), 16)))]
+
+        def pre1(n):
+            c = order[n]; pr = (par[0] + n) % 2; lab[0] = "pre1%d" % n
+            stage("PB" if pr else "PA", "SA%d" % pr, c * W1, W1, terms1(c), lambda k: terms1(c)(k)[0][1], None if n and SMALL else 6000.0, "M1", -63.5 * 32, -1024.0)
+
+        def post1(n):
+            c = order[n]; w = (c * W1, c * W1 + W1); tail = TAIL1[n == NC1 - 1]; lab[0] = "fit1%d" % n
+            pm, uu, ft, mk = R("PM", w), R("U", w), R("FIT", w), R("MR", w)
+            tm, thr = fits(W1, terms1(c), pm, pm, tail)
+            e = R(nb(), (0, W1))
+            total(e, [(NI, uu)] + tm, n == NC1 - 1)
+            ts(ft, e, thr, A.is_ge)
+            b = nb(); e, e2 = R(b, (0, W1)), R(b, (128, 128 + W1))
+            mm([[(e, R("OP32"), ft), (e, I, uu), (e, I, R("DE", w))], [(e2, R("OM32"), ft), (e2, NI, uu)]])
+            ts(mk, e, 37.5, A.is_lt, 2048.0, A.mult)
+            ts(R("KL", w), e2, 5.5, A.is_ge, float(XN), A.mult)
+            base = OWN + 3072 * u + 16 * W1 * n; lab[0] = "pool%d" % n
+            for j in range(4):
+                b = nb()
+                mm([[(R(b, (i * W1, i * W1 + W1)), l, r) for l, r in ((NI, terms1(c)(4 * j + i)[1][1]), (NI, pm), (S(4 * j + i), mk))] for i in range(4)])
+                o, e = R("POOL", (base + 4 * j * W1, base + 4 * (j + 1) * W1)), R(b, (0, 4 * W1))
+                if n == NC1 - 1 and j % 2:
+                    ts(o, e, 255.0, A.add, 0.0, A.max)
+                else:
+                    act(o, e, F.Relu, 255.0)
+            if u:
+                tt(IND(R("TRL"), R("CL", (w[0] // 16, w[1] // 16))), R("TRG", w), R("KL", w), A.max)
+            else:
+                tt(R("TRL", (256 + w[0], 256 + w[1])), R("TRL", (256 + w[0], 256 + w[1])), R("KL", w), A.max)
+
+        pre1(0)
+        if u == 1:
+            send_b(0)
+        for n in range(NC1):
+            if n + 1 < NC1:
+                pre1(n + 1)
+            pr = (par[0] + n) % 2
+            lab[0] = "med1%d" % n
+            median("PB" if pr else "PA", "SA%d" % pr, W1, R("PM", (order[n] * W1, order[n] * W1 + W1)), AS1[n > 0],
+                   [terms1(order[n])(k) + [(S(k), R("FX", (order[n] * W1, order[n] * W1 + W1)))] for k in range(8)])
+            if n == 0:
+                onehot()
+            post1(n)
+            if (u in (0, 2) and n == 0) or (u == 3 and n == NC1 - 1):
+                send_b(n + 1)
+        par[0] = (par[0] + NC1) % 2
+
+        win = R("POOL", (0, OWN + 3072 * (u + 1)))
+        st2 = [sum(CH2[:n]) for n in range(len(CH2))]
+        for n, W in enumerate(CH2):
+            for h in range(2):
+                a, b = st2[n] + h * W // 2, st2[n] + (h + 1) * W // 2; lab[0] = "b%d" % n
+                gx = (R("BG", (16 * a, 16 * b)), IND(win, R("ADU", (a, b))))
+                if n == 0 and h:
+                    cp(*gx)
+                else:
+                    act(*gx)
+
+        def terms2(n):
+            return lambda k: [(NI, R("BG", (16 * st2[n] + k, 16 * (st2[n] + CH2[n]), 16)))]
+
+        def pre2(n):
+            W, w0, pr = CH2[n], st2[n], (par[0] + n) % 2; lab[0] = "pre2%d" % n
+            stage("PB" if pr else "PA", "SA%d" % pr, w0, W, terms2(n), lambda k: terms2(n)(k)[0][1], 16000.0, "M2", -64.5 * 32, 4096.0)
+            e = R(nb(), (0, W))
+            mm([[(e, ONES, R("U", (w0, w0 + W)))]])
+            ts(R("NH", (w0, w0 + W)), e, 13.5 * 32, A.is_ge, 512.0, A.mult)
+
+        def post2(n):
+            W, w0 = CH2[n], st2[n]; lab[0] = "fit2%d" % n
+            w = (w0, w0 + W); tail = TAIL2[n == len(CH2) - 1]
+            pm, mh, ml, tf = R("PM", w), R("MH", w), R("ML", w), terms2(n)
+            act(R("X0", w), pm, F.Relu, 255.0)
+            if tail in "ab":
+                for a in range(16 * w0, 16 * w[1], 512):
+                    act(R("SRC", (a, a + 512)), R("BG", (a, a + 512)), F.Relu, 255.0, -1.0)
+                ml = mh = R("X0", w)
+                tf = lambda k: [(I, R("SRC", (16 * w0 + k, 16 * w[1], 16)))]
+            else:
+                ts(mh, pm, -255.0, A.max)
+                ts(ml, pm, -244.5, A.is_le, -1024.0, A.mult)
+                tt(ml, ml, mh, A.add)
+            tt(R("XQ", w), R("X0", w), R("NH", w), A.max)
+            if SMALL:
+                e = R(nb(), (0, W))
+                mm([[(e, I, R("XQ", w)), (e, NI, R("OX", w))]])
+                act(R("NE", w), e, F.Abs)
+            else:
+                tt(R("NE", w), R("XQ", w), R("OX", w), A.not_equal)
+            cp(IND(R("XW", (0, 1280)), R("TL", (w0 // 16, w[1] // 16))), R("XQ", w))
+            e = R(nb(), (0, W))
+            mm([[(e, R("ONESB"), R("NE", w)), (e, I, R("EM", w))]])
+            ts(R("AM", w), e, 1.0, A.max, 32.0 ** (u + 1), A.min)
+            tm, thr = fits(W, tf, ml, mh, tail)
+            e = R(nb(), (0, W))
+            total(e, [(I, R("U", w)), (I, R("NH", w))] + tm, n == len(CH2) - 1)
+            act(R("SN", w), e, F.Sign, -thr)
+            tt(R("VA", w), R("SN", w), R("AM", w), A.mult)
+            lab[0] = "back%d" % n
+            for j in range(W // 32):
+                b = nb(); a = w0 + 32 * j
+                mm([[(R(b, (k, 512, 16)), S(k), R("VA", (a, a + 32)))] for k in range(16)])
+                act(R("SRC", (16 * a, 16 * a + 512)), R(b))
+                cp(IND(R("W2"), R("SOU", (a, a + 32))), R("SRC", (16 * a, 16 * a + 512)))
+            act(R("KL", w), R("SN", w), F.Identity, VE / 2.0, -VE / 2.0)
+            tt(IND(R("VC"), R("TL", (w0 // 16, w[1] // 16))), R("VCF", w), R("KL", w), A.max)
+
+        pre2(0)
+        for n, W in enumerate(CH2):
+            if n + 1 < len(CH2):
+                pre2(n + 1)
+            if u == 3 and n == 0:
+                lab[0] = "yb"
+                places(384, 128)
+                pw = R("POOL", (784, OWN + 4 * 3072))
+                act(R("TM1"), I, F.Identity, 0.0, 256.0)
+                for j in range(4):
+                    b, w, o = R(nb()), (512 * j, 512 * j + 512), R("ASU", (32 * j, 32 * j + 32))
+                    act(R("XG", w), IND(pw, o), F.Relu, 255.0, -1.0)
+                    act(R("OG", w), IND(pw, o), F.Sign, -1000.0)
+                    mm([[(b, I, R("XG", w)), (b, R("TM1"), R("OG", w))]])
+                    act(R("OB", w), b, F.Identity, 256.0)
+            pr = (par[0] + n) % 2
+            lab[0] = "med2%d" % n
+            median("PB" if pr else "PA", "SA%d" % pr, W, R("PM", (st2[n], st2[n] + W)), AS2[n > 0],
+                   [terms2(n)(k) + [(S(k), R("FX", (st2[n], st2[n] + W)))] for k in range(8)])
+            post2(n)
+        par[0] = (par[0] + len(CH2)) % 2
+        lab[0] = "end"
+        if u < 3:
+            turn("XW", 256, "XS", u + 1)
+            send("XS", u + 1, "XW", 1280, "xa%d" % (u + 1))
+        if TRED:
+            b = nb()
+            mm([[(R(b, (8 * j, 8 * j + 8)), R("W2", (128 * j, 128 * j + 128)), R("ONES", (0, 128, 16)))] for j in range(64)])
+            act(R("AB"), R(b), F.Abs, 0.0, 1.0 / (16 * 32.0 ** (u + 1)))
+            ts(R("ABT"), R(b), 0.0, A.is_lt, float(XN), A.mult)
+            e = R(nb(), (0, 32))
+            mm([[(e, I, R("AC")), (e, I, R("FC"))] + [(e, R("Z8", (120 - 8 * m, 248 - 8 * m)), R("AB", (8 * (m % 2) + m // 2, 512, 16))) for m in range(16)]])
+            ts(R("FC"), e, 1.75, A.is_ge)
+            b = nb()
+            for h in range(4):
+                mm([[(R(b, (c, 512, 8)), R("IP", (112 + 128 * c - 16 * g, 240 + 128 * c - 16 * g)), R("ABT", (g, 512, 8))) for g in range(8)] for c in (2 * h, 2 * h + 1)])
+            if u == 3:
+                cp(R("DS"), R(b, (384, 512)))
+                ts(R("DS"), R("DS"), 512.0, A.min)
+            tt(R("TRL", (256, 768)), R(b), R("TRL", (256, 768)), A.max)
+            continue
+        for j in (1, 0):
+            w = (256 * j, 256 * j + 256); e = R(nb(), (0, 256))
+            mm([[(e, C(k), R("W2", (4096 * j + k, 4096 * j + 4096, 16))) for k in range(16)]])
+            act(R("AB", w), e, F.Abs, 0.0, 1.0 / (16 * 32.0 ** (u + 1)))
+            ts(e, e, 0.0, A.is_lt, float(XN), A.mult)
+            if u == 3 and j:
+                ts(R("DS"), R(e[1], (128, 256)), 1.0, A.is_ge, 512.0, A.mult)
+            t = R("TRL", (256 + w[0], 256 + w[1]))
+            tt(t, e, t, A.max)
+        e = R(nb(), (0, 32))
+        mm([[(e, I, R("AC")), (e, I, R("FC"))] + [(e, C(m), R("AB", (m, 512, 16))) for m in range(16)]])
+        ts(R("FC"), e, 1.75, A.is_ge)
+
+    dma("s", R("yx"), R("XW", (256, 1280)), 262144)
+    for j in range(4):
+        b, w = nb(), (512 * j, 512 * j + 512)
+        mm([[(R(b, (k, 512, 16)), S(k), R("DS", (32 * j, 32 * j + 32)))] for k in range(16)])
+        tt(R("BG", w), R(b), R("OB", w), A.max)
+        if j % 2:
+            dma("s", R("yb", (512 * j - 512, 512 * j + 512)), R("BG", (512 * j - 512, 512 * j + 512)), 262144)
+    e = R(nb(), (0, 64))
+    mm([[(e, I, R("AT")), (e, I, R("FT"))]])
+    ts(R("FT"), e, 1.75, A.is_ge, 32.0, A.mult)
+    ts(R("XG", (0, 1024)), R("VC", (256, 1280)), VE - 0.5, A.is_lt)
+    gi, g8 = R("ONES", (0, 128, 16)), (0, 8)
+    def gm(m): return R("S", (128 * m, 128 * m + 128, 16))
+    for j in range(2):
+        b = nb()
+        mm([[(R(b, p=g8), gi, R("XG", (512 * j, 512 * j + 512)))] + [(R(b, (m, 512, 16), p=g8), gm(m), R("FT", (32 * j, 32 * j + 32))) for m in range(16)]])
+        act(R("SO", (512 * j, 512 * j + 512), p=g8), R(b, p=g8))
+    dma("a", R("yt"), R("SO", (0, 1024), p=g8), 32768)
+    ts(R("AB"), R("TRL", (256, 768)), XN - 0.5, A.is_lt)
+    ts(R("AC"), R("FC"), 32.0, A.mult)
+    b = nb()
+    mm([[(R(b, p=g8), gi, R("AB"))] + [(R(b, (m, 512, 16), p=g8), gm(m), R("AC")) for m in range(16)]])
+    act(R("TA", (0, 512), p=g8), R(b, p=g8))
+    dma("a", R("yc"), R("TA", (0, 512), p=g8), 16384)
+    return ops
+
+
+def schedule(ops):
+    n = len(ops)
+    cost = [o["cost"] for o in ops]
+    pre = [[(d, (ops[d]["lat"] + LAT) if w else 0.0) for d, w in o["deps"].items()] for o in ops]
+    suc = [[] for _ in range(n)]
+    unit = {}
+    for j in range(n):
+        unit.setdefault(ops[j]["use"] or j, []).append(j)
+        for d, l in pre[j]:
+            suc[d].append((j, l))
+
+    def gap(ln, t, c):
+        k = len(ln)
+        while k and ln[k - 1][1] > t:
+            k -= 1
+        while k < len(ln) and t + c > ln[k][0]:
+            t = max(t, ln[k][1]); k += 1
+        return t, k
+
+    def sweep(key, edges, back):
+        st, lanes, bank, left, nxt = [0.0] * n, {b: [] for b in BANKS}, {}, {}, {}
+        for u, js in unit.items():
+            before = {ops[d]["use"] or d for j in js for d, l in edges[j]} - {u}
+            left[u] = len(before)
+            for v in before:
+                nxt.setdefault(v, []).append(u)
+        uk = {u: min(key[j] for j in js) for u, js in unit.items()}
+        ready = sorted((uk[u], unit[u][0], u) for u in unit if not left[u])
+        done = 0
+
+        def place(js, t0):
+            got = []
+            for j in js:
+                t = max([st[d] + cost[d] + l for d, l in edges[j]] + [t0])
+                if ops[j]["q"] is not None:
+                    ln = lanes.setdefault(ops[j]["q"], [])
+                    t, k = gap(ln, t, cost[j])
+                    ln.insert(k, (t, t + cost[j])); got.append((ln, k))
+                st[j] = t
+            return got
+        while ready:
+            u = ready.pop(0)[2]
+            js = unit[u][::-1] if back else unit[u]
+            done += len(js)
+            if isinstance(u, str):
+                best = None
+                for b in BANKS:
+                    t0 = 0.0
+                    while True:
+                        for ln, k in place(js, t0)[::-1]:
+                            ln.pop(k)
+                        a, e = min(st[j] for j in js), max(st[j] + cost[j] for j in js) + LAT
+                        t, k = gap(lanes[b], a, e - a)
+                        if t == a:
+                            break
+                        t0 = t
+                    if best is None or e < best[0]:
+                        best = (e, b, t0, a, k)
+                place(js, best[2])
+                lanes[best[1]].insert(best[4], (best[3], best[0])); bank[u] = best[1]
+            else:
+                place(js, 0.0)
+            for v in nxt.get(u, []):
+                left[v] -= 1
+                if not left[v]:
+                    ready.append((uk[v], unit[v][0], v))
+            ready.sort()
+        assert done == n
+        return st, bank
+
+    tail = [0.0] * n
+    for j in range(n - 1, -1, -1):
+        tail[j] = cost[j] + max([tail[x] + l for x, l in suc[j]] or [ops[j]["lat"]])
+    key = [-t for t in tail]
+    best = None
+    for it in range(2 * SWEEPS):
+        if it == SWEEPS:
+            key = list(range(n))
+        st, bank = sweep(key, pre, False)
+        end = max(st[j] + cost[j] + ops[j]["lat"] for j in range(n))
+        if best is None or end < best[0]:
+            best = (end, st, bank)
+        bk = sweep([-st[j] - cost[j] for j in range(n)], suc, True)[0]
+        key = [-bk[j] - cost[j] for j in range(n)]
+    seed, tags = SEED, sorted({o["tag"] for o in ops})
+    FOUND[:] = []
+    for it in MOVES + list(range(SEED, SEED + TRIES)):
+        sh, seed, was = {}, it * 2654435761 % 2147483648, best[0]
+        FOUND.append(it)
+        for _ in range(1 + it % 3):
+            seed = (seed * 1103515245 + 12345) % 2147483648
+            sh[tags[(seed >> 8) % len(tags)]] = ((seed >> 16) % 33 - 16) * (150 if it % 2 else 600)
+        rd = it // 7 % 8
+        key = [best[1][j] + (sh.get(ops[j]["tag"], 0) if rd > 3 or ops[j]["rd"] == rd else 0) for j in range(n)]
+        for again in range(2):
+            st, bank = sweep(key, pre, False)
+            end = max(st[j] + cost[j] + ops[j]["lat"] for j in range(n))
+            if end < best[0] - 20:
+                best = (end, st, bank)
+            if again or end > best[0] + 4000 or it % 4:
+                break
+            bk = sweep([-st[j] - cost[j] for j in range(n)], suc, True)[0]
+            key = [-bk[j] - cost[j] for j in range(n)]
+        if best[0] == was:
+            FOUND.pop()
+    end, st, bank = best
+    last = {}
+    for u in sorted(bank, key=lambda u: min(st[j] for j in unit[u])):
+        for d in last.get(bank[u], []):
+            for j in unit[u]:
+                ops[j]["deps"][d] = ops[j]["deps"].get(d, False) or ops[j]["q"] != ops[d]["q"] or ops[j]["q"] != "p"
+        last[bank[u]] = unit[u]
+    return sorted(range(n), key=lambda j: (st[j], j)), st, bank
+
+
+def plan():
+    ops = build()
+    order, start, bank = schedule(ops)
+    cnt, known, snap, out = {}, {}, {}, []
+    used = set()
+    for o in ops:
+        for d, w in o["deps"].items():
+            if w and o["kind"] != "r":
+                used.add(d)
+    for j in order:
+        o = ops[j]; q = o["q"]
+        if o["kind"] == "r":
+            snap[j] = {}
+            continue
+        kn = known.setdefault(q, {})
+        waits = {}
+        for d in sorted((d for d, w in o["deps"].items() if w), key=lambda d: -start[d]):
+            s, v = ops[d]["sem"]
+            if kn.get(s, 0) < v:
+                waits[s] = max(waits.get(s, 0), v)
+                kn[s] = v
+                for s2, v2 in snap[d].items():
+                    kn[s2] = max(kn.get(s2, 0), v2)
+        if o["kind"] == "c" and j in used:
+            cnt[q] = cnt.get(q, 0) + 1
+            o["sem"] = (QSEM[q], cnt[q])
+        snap[j] = dict(kn)
+        out.append((q, waits, o["calls"], o["sem"], o["kind"]))
+    fin = [(QSEM[q], c) for q, c in cnt.items()] + [o["sem"] for o in ops if o["kind"] in ("d", "r")]
+    fin.append(("sent", 8 * sum(o["kind"] == "s" for o in ops)))
+    return out, fin, bank
+
+
+PLAN = []
+
+
+def rank_program(g, core, T, topo):
+    rank = T.rank_of(core)
+    if rank is None:
+        return
+    if not PLAN:
+        PLAN.append(plan())
+    prog, fin, bank = PLAN[0]
+    eng = {"v": g.vector, "a": g.scalar, "p": g.tensor, "s": g.sync, "g": g}
+
+    def ap(x):
+        if not is_ref(x):
+            return x
+        if x[0] == "ind":
+            return ap(x[1]).indirect(ap(x[2]))
+        t = T[bank.get(x[1], x[1])]
+        return t[(slice(None) if x[3] is None else slice(x[3][0], x[3][1]),) + (x[2] or (slice(0, t.shape[1]),))]
+
+    def send(src, u, dst, d0, sem):
+        trs = []
+        for d in range(1, 4):
+            to = T.cores[rank ^ d]
+            assert topo.may_write(core, to)
+            e = topo.engines(core, to)
+            use = (e[0:3:2], e[4:7:2], e[1:8:2])[d - 1]
+            rid, pid, _ = topo.addr(to)
+            a = 256 * (d - 1)
+            trs.append(RemoteDMATransfer(dst_ids=[DstId(rid=rid, pnc=pid)], dma_engine_mask=sum(1 << x for x in use), remote_sem=T.sem[sem],
+                                         src=T[src][:, 768 * u + a:768 * u + a + 256], dst=T[dst][:, d0 + a:d0 + a + 256]))
+        g.remote_dma_fused(trs, local_sem=T.sem.sent)
+
+    for q, waits, calls, sem, kind in prog:
+        e = eng[q]
+        for s, v in waits.items():
+            e.wait_ge(T.sem[s], v)
+        for meth, args, kw in calls:
+            if meth == "send":
+                send(*args)
+                continue
+            a = [ap(x) for x in args]
+            k = {n: ap(x) for n, x in kw.items()}
+            if meth == "matmul": r = e.matmul(*a)
+            elif meth == "activation": r = e.activation(*a, **k)
+            elif meth == "tensor_tensor": r = e.tensor_tensor(*a)
+            elif meth == "tensor_scalar": r = e.tensor_scalar(*a)
+            elif meth == "tensor_copy": r = e.tensor_copy(*a)
+            elif meth == "memset": r = e.memset(*a)
+            elif meth == "tensor_tensor_scan": r = e.tensor_tensor_scan(*a)
+            elif meth == "iota": r = e.iota(*a, **k)
+            elif meth == "affine_select": r = e.affine_select(*a)
+            else: r = e.dma_start(*a)
+        if kind == "d":
+            r.then_inc(T.sem[sem[0]], 16)
+        elif kind == "c" and sem is not None:
+            r.then_inc(T.sem[sem[0]], 1)
+    for s, v in fin:
+        g.wait_ge(T.sem[s], v)

@@ -1,54 +1,62 @@
+import math
 from concourse.bass import DstId, RemoteDMATransfer
 from concourse.mybir import AluOpType as A, ActivationFunctionType as F
 
-W1 = 96
-CH2 = [64, 96, 96]
-OHM = 32
+CH1 = [[(0, None, 64), (64, None, 128)],
+       [(192, None, 128), (None, 0, 64)],
+       [(384, None, 64), (None, 64, 64), (None, 0, 64)],
+       [(None, 0, 64), (None, 64, 128)]]
+SENDB = [1, 0, 2, 1]
+CH2 = [96, 96, 64]
+FIT1 = ("bbbb", "vbvb")
+FIT2 = ("bbbb", "vbvb")
+CLIP = "aaa"
+GX = ("va", "aa")
+GB = ("av", "aa")
+GL = "aaaa"
+POOLQ = ("aa", "av")
 AS1 = (1, 1)
 AS2 = (1, 1)
-PE_SORT = max(AS1 + AS2) > 0
-TAIL1 = "ba"
-TAIL2 = "bb"
-SAMEQ_WAR = True
-TRED = True
-SMALL = True
-TWO = True
-MOVES = [30000, 30003, 30004, 30104, 30216, 30268, 30288, 30292, 30728, 30772]
+MOVES = []
 FOUND = []
 SWEEPS = 4
-TRIES = 0
+TRIES = 2000
 SEED = 1
-NC1 = 192 // W1
 XN, VE = 1792, 816
 OWN = 800
-OAB, OBB = 8192, 8192 + 32 * 256
+OAB, OBB, P0 = 0, 6144, 9216
+DB = 3904
+DEAD = 16384.0
+MAGIC = 1.5 * 2.0 ** 28
+LN2 = math.log(2.0)
 
 bf, f4, i4, u2 = "bfloat16", "float32", "int32", "uint16"
 hf = "float16"
-hs, WM = hf if PE_SORT else bf, max([W1] + CH2)
+WM = 128
 SCRATCH = {}
 for _n, _s, _d in [
-    ("OB", [8192], bf), ("POOL", [OWN + 4 * 3072], bf), ("W2", [28800], bf), ("XW", [2064], bf),
+    ("OB", [8192], bf), ("POOL", [OWN + 4 * 3072], bf), ("W2", [P0 + 8192], bf), ("XW", [2064], bf),
     ("XG", [3072], bf), ("OG", [3072], bf), ("BG", [4096], bf), ("SRC", [4096], bf),
     ("SGA", [16, WM], bf), ("SGB", [16, WM], bf), ("SA0", [8, WM], bf), ("SA1", [8, WM], bf), ("IH", [128], hf), ("NIH", [128], hf),
-    ("SB0", [8, WM], hs), ("SC0", [8, WM], hs), ("SD0", [4, WM], hs), ("SB1", [8, WM], hs), ("SC1", [8, WM], hs), ("SD1", [4, WM], hs),
-    ("CT", [512], i4), ("TV", [1024], i4), ("TI", [1024], i4),
-    ("TRL", [768], f4), ("TA", [768], f4), ("TB", [768], f4), ("VC", [1280], f4), ("VL", [1280], bf), ("SO", [1280], f4),
-    ("IDS", [1280], bf), ("LW", [2176], bf), ("LOC", [832], bf), ("LS0", [384], bf), ("LS", [192], bf),
+    ("SB0", [8, WM], hf), ("SC0", [8, WM], hf), ("SD0", [4, WM], hf), ("SB1", [8, WM], hf), ("SC1", [8, WM], hf), ("SD1", [4, WM], hf),
+    ("CT", [512], i4), ("TV", [1024], i4), ("TI", [1024], i4), ("SO", [1280], i4), ("DUMP2", [256], i4), ("TRL", [768], i4),
+    ("TA", [768], bf), ("TZ", [768], bf), ("DD", [768], bf), ("VC", [1280], f4), ("VL", [1280], bf), ("TR0", [448], u2),
+    ("IDS", [1280], f4), ("LW", [2176], f4), ("LWB", [256], bf), ("LOC", [832], bf), ("LS0", [192], bf), ("LS", [192], bf),
     ("S", [2048], bf), ("ZC", [144], bf), ("SEL", [480], bf), ("PERM", [384], bf), ("ONE", [144], bf),
     ("I", [128], bf), ("NI", [128], bf), ("ONES", [128], bf), ("ONES16", [128], bf), ("ONESB", [128], bf),
+    ("I15", [128], bf), ("NI15", [128], bf), ("IQ", [128], bf), ("IPM", [128], bf), ("SCL", [128], bf),
     ("TRI", [128], bf), ("RK", [128], bf), ("M1", [128], bf), ("M2", [128], bf), ("OP32", [128], bf), ("OM32", [128], bf),
-    ("IP", [1136 if TRED else 16], bf), ("Z8", [248], bf), ("TM1", [128], bf), ("TM2", [128], bf),
-    ("KI", [8], i4), ("KC", [8], f4), ("MK", [16], f4), ("I16", [16], f4), ("BC", [4], f4), ("DUMP", [64], f4), ("ONEF", [64], f4),
+    ("TM1", [128], bf), ("TM2", [128], bf),
+    ("KI", [8], i4), ("KC", [8], f4), ("KT", [16], f4), ("MK", [16], f4), ("I16", [16], f4), ("BC", [4], f4), ("DUMP", [64], f4), ("ONEF", [64], f4),
     ("XS", [4 * 768], bf), ("BS", [4 * 768], bf),
     ("FC", [32], bf), ("AC", [32], bf), ("FT", [64], bf), ("AT", [64], bf), ("SCN", [64], f4), ("RP", [64], f4), ("RO", [64], f4),
-    ("OFU", [64], u2), ("CL", [16], u2), ("TL", [16], u2), ("OOU", [192], u2), ("TRU", [192], u2), ("TRG", [192], f4),
-    ("DE", [192], bf), ("U", [256], bf), ("FX", [256], bf), ("PM", [256], bf), ("FIT", [192], bf), ("MR", [192], bf), ("KL", [256], f4),
-    ("A0", [192], bf), ("B0", [192], bf), ("ABT", [512], bf), ("CS", [8, 33], f4), ("FF", [8, 32], bf),
+    ("OFU", [64], u2), ("CL", [16], u2), ("TL", [16], u2), ("OOU", [192], u2), ("TRU", [192], u2),
+    ("DE", [192], bf), ("U", [256], bf), ("FX", [256], bf), ("PM", [256], bf), ("FIT", [192], bf), ("MR", [192], bf), ("KL", [192], bf), ("KV", [256], f4),
+    ("A0", [192], bf), ("B0", [192], bf), ("ABT", [384], bf), ("CI", [128], i4), ("CJ", [8, 32], i4), ("FF", [8, 32], bf),
     ("VCU", [256], u2), ("SOU", [256], u2), ("ADU", [256], u2), ("VCF", [256], f4), ("VLG", [256], bf), ("OX", [256], bf),
-    ("EM", [256], bf), ("NH", [256], bf), ("MH", [256], bf), ("ML", [256], bf), ("X0", [256], bf), ("XQ", [256], bf),
+    ("EM", [256], bf), ("NH", [256], bf), ("X1", [256], bf), ("X0", [256], bf), ("XQ", [256], bf),
     ("NE", [256], bf), ("AM", [256], bf), ("SN", [256], bf), ("VA", [256], bf),
-    ("AB", [512], bf), ("DS", [128], bf), ("ASU", [128], u2),
+    ("AB", [512], bf), ("DS", [128], bf), ("ASU", [128], u2), ("YF", [1024], f4),
 ]:
     SCRATCH[_n] = ("sbuf", [128] + _s, _d)
 SCRATCH["PA"] = ("psum", [128, 8, 128], f4)
@@ -104,7 +112,7 @@ def build():
                 for lo, hi in spans(r)[0]:
                     for (a, b, o, w) in lst:
                         if a < hi and lo < b and o != me and (w or wr):
-                            need = ops[o]["q"] != q or ops[o]["kind"] != "c" or kind != "c" or (w and not wr) or (SAMEQ_WAR and q != "p")
+                            need = ops[o]["q"] != q or ops[o]["kind"] != "c" or kind != "c" or (w and not wr) or q != "p"
                             deps[o] = deps.get(o, False) or need
                     if wr:
                         lst[:] = [t for t in lst if not (lo <= t[0] and t[1] <= hi)]
@@ -155,8 +163,12 @@ def build():
 
     def act(out, a, func=F.Identity, bias=0.0, scale=1.0):
         rd, wr = parts(out, (a, bias, scale))
+        if out[0] == "ind":
+            return add("a", [("activation", (out, a, func), {})], rd, wr, 90 + spans(a)[1] * SCA)
         return add("a", [("activation", (out, a, func), {"bias": bias, "scale": scale})], rd, wr,
                    90 + spans(out)[1] * (GAT if a[0] == "ind" else 1.0))
+
+    def move(q, out, a): return cp(out, a) if q == "v" else act(out, a)
 
     def nb():
         uses[0] += 1
@@ -192,7 +204,7 @@ def build():
         s = add("g", [("send", (src, u, dst, d0, sem), {})], [R(src, (768 * u, 768 * u + 768))], [], 1200.0, kind="s", extra=extra, lat=4000.0)
         return add(None, [], [], [R(dst, (d0, d0 + 768))], 0.0, kind="r", extra=(s,), sem=(sem, 8))
 
-    I, NI, ONES = R("I"), R("NI"), R("ONES")
+    I, NI, ONES, I15, NI15 = R("I"), R("NI"), R("ONES"), R("I15"), R("NI15")
     def C(k): return R("ZC", (15 - k, 143 - k))
     def S(k): return R("S", (128 * k, 128 * k + 128))
     def col(name, j): return R(name, (j, j + 1))
@@ -215,6 +227,7 @@ def build():
     turn("XW", 256, "XS", 0)
     send("XS", 0, "XW", 1280, "xa0")
     asel(I, one, [[-1, 128]], A.is_equal, 0)
+    asel(R("IPM"), one, [[-8, 2], [-16, 8], [-1, 8]], A.is_equal, 0)
     asel(R("TM1"), one, [[-16, 8], [0, 16]], A.is_ge, 0)
     asel(ONES, R("TM1"), [[16, 8], [0, 16]], A.is_ge, 15, -1)
     asel(R("TRI"), ONES, [[1, 128]], A.is_ge, 0, -1)
@@ -223,18 +236,31 @@ def build():
     ts(R("KI", (4, 5)), R("KI", (0, 1)), 15, A.bitwise_and)
     cp(col("KC", 0), R("KI", (4, 5)))
     ts(R("MK"), R("I16"), col("KC", 0), A.is_equal)
-    ts(col("KC", 1), col("KC", 0), -4096.0, A.add)
-    ts(col("KC", 2), col("KC", 0), float(W1), A.mult, -784.0, A.add)
+    ts(col("KC", 1), col("KC", 0), -4352.0, A.add)
+    ts(col("KC", 2), col("KC", 0), 64.0, A.mult, -784.0, A.add)
     ts(col("KC", 3), col("MK", 2), float(OWN), A.mult)
     ts(R("BC"), R("I16", (0, 4)), 3072.0, A.mult)
     ts(R("BC"), R("BC"), col("MK", 3), A.mult, col("KC", 3), A.add)
+    modes = sorted(set(FIT1 + FIT2))
+    for j, m in enumerate(modes):
+        ms(col("KT", 2 * j), 11.5)
+        for k in range(16):
+            if m[k // 4] == "b" and len(set(m)) > 1:
+                ts(col("KT", 2 * j), col("MK", k), -4.5, A.mult, col("KT", 2 * j), A.add)
+        if len(set(m)) > 1:
+            ts(col("KT", 2 * j + 1), col("KT", 2 * j), -1.0, A.mult)
+
+    def bound(m, neg):
+        if "b" in m and len(set(m)) > 1:
+            return col("KT", 2 * modes.index(m) + neg)
+        return (7.0 if "b" in m else 11.5) * (-1.0 if neg else 1.0)
     ms(R("ZC"), 0.0)
     cp(R("ZC", (15, 143, 16)), R("ONES", (0, 128, 16)))
     for k in range(16):
         act(S(k), ONES, F.Identity, 0.0, col("MK", k))
     ts(NI, I, -1.0, A.mult)
-    if PE_SORT:
-        cp(R("IH"), I); ts(R("NIH"), I, -1.0, A.mult)
+    cp(R("IH"), I); ts(R("NIH"), I, -1.0, A.mult)
+    ts(I15, I, 1.5, A.mult); ts(NI15, I, -1.5, A.mult); ts(R("IQ"), I, 1.0 / 32, A.mult)
     ts(R("TM1"), R("TRI"), 2.0, A.mult)
     tt(R("TM1"), R("TM1"), ONES, A.subtract)
     ts(R("TM2"), I, -64.0, A.mult)
@@ -247,169 +273,167 @@ def build():
     tt(R("TM1"), R("TRI"), ONES, A.subtract)
     tt(R("RK"), R("TM1"), R("TM2"), A.add)
     act(R("ONES16"), ONES, F.Identity, 0.0, 16.0)
-    act(R("ONESB"), ONES, F.Identity, 0.0, 2.0 ** 20)
+    act(R("ONESB"), ONES, F.Identity, 0.0, 2.0 ** 34)
     fill(R("SEL"), 0)
     for h in range(2):
         asel(R("SEL", (240 * h + 112, 240 * h + 128), p=(0, 32)), R("ONE", (0, 16), p=(0, 32)), [[-1, 16]], A.is_equal, -16 * h)
-    if TRED:
-        fill(R("IP"), 0); fill(R("Z8"), 0)
-        for c in range(8):
-            act(R("IP", (112 + 128 * c, 128 + 128 * c)), R("I", (16 * c, 16 * c + 16)))
-        cp(R("Z8", (120, 128)), R("ONES", (0, 128, 16)))
     ms(R("ONEF"), 1.0)
     iota(R("DUMP"), [[16, 64]], 1024, 1)
-    ts(R("TI", (0, 512)), R("CT"), 4, A.logical_shift_right)
-    cp(R("TRU"), R("TI", (0, 192)))
-    cp(R("TRL", (256, 768)), R("TI", (0, 512)))
+    iota(R("DUMP2"), [[16, 256]], DB, 1)
+    ts(R("TRL", (256, 768)), R("CT"), 4, A.logical_shift_right)
+    cp(R("TR0", (0, 192)), R("TRL", (256, 448)))
+    cp(R("TR0", (192, 448)), R("TRL", (448, 704)))
     ts(R("TI", (512, 1024)), R("CT"), 4, A.logical_shift_right, 31, A.bitwise_and)
     cp(R("TA", (256, 768)), R("TI", (512, 1024)))
-    ts(R("TI", (0, 512)), R("CT"), 9, A.logical_shift_right)
-    cp(R("TB", (256, 768)), R("TI", (0, 512)))
-    fill(R("TRL", (0, 256)), XN); fill(R("TA", (0, 256)), 0); fill(R("TB", (0, 256)), 99)
+    ts(R("TI", (0, 512)), R("CT"), 16384.0, A.add)
+    ts(R("TI", (0, 512)), R("TI", (0, 512)), 9, A.logical_shift_right, 63, A.bitwise_and)
+    cp(R("AB"), R("TI", (0, 512)))
+    act(R("TZ", (256, 768)), R("AB"), F.Exp, -334.0 * LN2, 7.0 * LN2)
+    iota(R("VCF", (0, 128)), [[0, 8], [-14, 16]], 110)
+    act(R("SCL"), R("VCF", (0, 128)), F.Exp, 0.0, LN2)
+    fill(R("TRL", (0, 256)), XN); fill(R("TA", (0, 256)), 0); fill(R("TZ", (0, 256)), 0); ms(R("DD"), 0.0)
     fill(R("XW", (0, 256)), 512); fill(R("XW", (2048, 2064)), 512)
     fill(R("POOL", (0, 16)), 2048); fill(R("POOL", (784, 800)), 2048)
     fill(R("LOC"), -1024)
     iota(R("LOC", (768, 816)), [[1, 48]], 1)
     iota(R("BG", (0, 1280)), [[16, 80], [0, 16]])
-    iota(R("BG", (1280, 2560)), [[0, 80], [1, 16]])
-    iota(R("BG", (2560, 2752)), [[16 * W1, NC1], [0, W1]])
-    iota(R("BG", (2752, 2944)), [[-16 * W1, NC1], [0, W1]], 16 * W1 * (NC1 - 1))
-    iota(R("BG", (2944, 3328)), [[0, 2 * NC1], [1, W1]])
+    iota(R("BG", (1280, 2560)), [[0, 80], [1, 16]], 16)
+    iota(R("BG", (2560, 2752)), [[1024, 3], [0, 64]])
+    iota(R("BG", (2752, 2944)), [[0, 3], [1, 64]])
     for a, n in ((0, 512), (512, 512), (1024, 256)):
         e = R(nb(), (0, n))
         mm([[(e, C(0), R("BG", (a, a + n))), (e, C(1), R("BG", (1280 + a, 1280 + a + n)))]])
         act(R("IDS", (a, a + n)), e, F.Identity, 0.0, 0.0625)
-    e = R(nb(), (0, 384))
-    mm([[(e, C(0), R("BG", (2560, 2944))), (e, C(1), R("BG", (2944, 3328)))]])
+    e = R(nb(), (0, 192))
+    mm([[(e, C(0), R("BG", (2560, 2752))), (e, C(1), R("BG", (2752, 2944)))]])
     act(R("LS0"), e, F.Identity, 0.0, 0.0625)
-    iota(R("SO"), [[16, 1280]], 8192, 1)
+    lab[0] = "views"
     for j in range(2):
         e, v, t = R(nb()), R("TV", (512 * j, 512 * j + 512)), (256 + 512 * j, 768 + 512 * j)
         ti = R("TI", (512 * j, 512 * j + 512))
-        ts(e, v, 8192.0, A.is_ge, 65536.0, A.mult)
-        act(R("AB"), e, F.Identity, float(W1), -(W1 - 1.0) / 65536.0)
-        tt(e, e, v, A.add)
-        tt(R("SO", t), e, R("SO", t), A.min)
+        ts(e, v, 8192.0, A.is_lt, 63.0, A.mult)
+        act(R("AB"), e, F.Identity, 1.0)
         ts(ti, v, 15, A.bitwise_and)
         tt(R("VL", t), ti, R("AB"), A.mult)
+        ts(ti, v, 8192.0, A.add)
+        ts(R("SO", t), ti, 16383, A.bitwise_and)
         ts(ti, v, 4, A.logical_shift_right)
         ts(R("VC", t), ti, 256.0, A.add)
-    fill(R("VC", (0, 256)), VE); fill(R("VL", (0, 256)), 0)
+    fill(R("VC", (0, 256)), VE); fill(R("VL", (0, 256)), 0); fill(R("SO", (0, 256)), 0)
+    lab[0] = "zero"
     for j in range(8):
-        iota(R("W2", (1024 * j, 1024 * j + 1024)), [[0, 1024]])
+        fill(R("W2", (P0 + 1024 * j, P0 + 1024 * j + 1024)), 0)
+    lab[0] = "start"
     ms(R("FC"), 1.0); ms(R("AC", (0, 12)), 0.0); ms(R("AC", (12, 32)), 1.0)
 
-    def worklist(fl, al, n, s0, K, out, c0, c1):
+    def worklist(fl, al, n, segs, K, out, fixed=None, turned=False):
+        c0, c1 = min(s[0] for s in segs), max(s[1] for s in segs)
+        w = (c0, c1)
         act(R("LW", (0, K)), R("IDS", (0, K)))
+        if fixed:
+            ms(R("SCN", fixed), 8000.0)
         b = nb()
-        mm([[(R(b, (0, n)), ONES, R(fl))], [(R(b, (64, 64 + n)), R("RK"), R(fl))]])
-        vec("tensor_tensor_scan", R("SCN", (s0, n)), R("ONEF", (s0, n)), R(b, (s0, n)), 4095.0, A.mult, A.add)
-        if s0:
-            vec("tensor_tensor_scan", R("SCN", (0, s0)), R("ONEF", (0, s0)), R(b, (0, s0)), col("SCN", n - 1), A.mult, A.add)
-        tt(R("RP", (0, n)), R(b, (64, 64 + n)), R("SCN", (0, n)), A.add)
-        tt(R("RO", (0, n)), R("RP", (0, n)), R("DUMP", (0, n)), A.min)
-        cp(R("OFU", (0, n)), R("RO", (0, n)))
-        ts(R(al), R("RP", (0, n)), K - 0.5, A.is_ge)
-        for c in range(c0, c1, 32):
-            d = min(c + 32, c1)
-            cp(IND(R("LW"), R("OFU", (c, d))), R("IDS", (256 + 16 * c, 256 + 16 * d)))
+        mm([[(R(b, w), ONES, R(fl, w))], [(R(b, (64 + c0, 64 + c1)), R("RK"), R(fl, w))]])
+        for j, s in enumerate(segs):
+            vec("tensor_tensor_scan", R("SCN", s), R("ONEF", s), R(b, s), col("SCN", segs[j - 1][1] - 1) if j and not turned else 4095.0, A.mult, A.add)
+        tt(R("RP", w), R(b, (64 + c0, 64 + c1)), R("SCN", w), A.add)
+        if turned:
+            s, t = segs
+            ts(col("KC", 4), col("SCN", s[1] - 1), -1.0, A.mult, K + 4094.5, A.add)
+            ts(R("RO", s), R("RP", s), col("KC", 4), A.add, 0.5, A.add)
+            tt(R("RO", s), R("RO", s), R("DUMP", s), A.min)
+            tt(R("RO", t), R("RP", t), R("DUMP", t), A.min)
+            cp(R("OFU", w), R("RO", w))
+            ts(R(al, s), R("RP", s), K - 0.5, A.is_ge)
+            ts(R(al, t), R("RP", t), col("KC", 4), A.is_ge)
+            segs = segs[::-1]
+        else:
+            tt(R("RO", w), R("RP", w), R("DUMP", w), A.min)
+            cp(R("OFU", w), R("RO", w))
+            ts(R(al, w), R("RP", w), K - 0.5, A.is_ge)
+            segs = sorted(segs)
+            segs = [segs[0]] + segs[1:] if fixed else [w]
+        if fixed:
+            ms(R(al, fixed), 0.0)
+        for s in segs:
+            for c in range(s[0], s[1], 32):
+                d = min(c + 32, s[1])
+                act(IND(R("LW"), R("OFU", (c, d))), R("IDS", (256 + 16 * c, 256 + 16 * d)), F.Silu)
         m = K // 16
+        act(R("LWB", (0, K)), R("LW", (0, K)))
         e = R(nb(), (0, m))
-        mm([[(e, C(k), R("LW", (k, K, 16))) for k in range(16)]])
-        cp(R(out, (0, m)), e)
+        mm([[(e, C(k), R("LWB", (k, K, 16))) for k in range(16)]])
+        ts(R(out, (0, m)), e, -16.0, A.add)
 
     def median(P, SA, W, out, level, hist):
         def q(nm):
             return lambda a, b=None, s=None: R(nm, (a, a + 1 if b is None else b, s), (0, W))
-        z = SA[2] if TWO else "0"
+        z = SA[2]
         p, a_, b_, c_, d_ = q(P), q(SA), q("SB" + z), q("SC" + z), q("SD" + z)
         lo, hi = A.min, A.max
         if level:
-            def other(s0, pairs):
-                for j, (x, y) in enumerate(pairs):
-                    hist[s0 + j] = hist[s0 + j] + [(I if x[0] == SA else R("IH"), R(SA if x[0] == SA else x[0] + z, x[1], (0, W))), (R("NIH"), R(y[0] + z, y[1], (0, W)))]
-                mm([[(R(P, s, (0, W)), l, r) for l, r in hist[s]] for s in range(s0, s0 + len(pairs))])
-            tt(b_(0, 4), p(0, 4), a_(0, 4), lo); other(0, [((SA, j), ("SB", j)) for j in range(4)])
-            tt(b_(4, 8), p(4, 8), a_(4, 8), hi); other(4, [((SA, j), ("SB", j)) for j in range(4, 8)])
-            tt(d_(0, 2), p(0, 2), b_(4, 6), lo); tt(c_(0, 2), p(2, 4), b_(6, 8), hi)
-            if level > 1:
-                other(0, [(("SB", 4 + j), y) for j, y in enumerate((("SD", 0), ("SD", 1), ("SC", 0), ("SC", 1)))])
-            tt(c_(6, 8), p(4, 6), b_(0, 2), lo); tt(d_(2, 4), p(6, 8), b_(2, 4), hi)
-            if level > 1:
-                other(4, [(("SB", j), y) for j, y in enumerate((("SC", 6), ("SC", 7), ("SD", 2), ("SD", 3)))])
-            else:
-                tt(p(4, 6), p(4, 6), b_(0, 2), hi); tt(p(0, 2), p(0, 2), b_(4, 6), hi)
-                tt(p(2, 4), p(2, 4), b_(6, 8), lo); tt(p(6, 8), p(6, 8), b_(2, 4), lo)
-            tt(c_(2, 4), p(4, 6), d_(0, 2), lo); tt(c_(4, 6), p(2, 4), d_(2, 4), hi)
-            if level > 2:
-                other(4, [(("SD", j), ("SC", 2 + j)) for j in range(2)]); other(2, [(("SD", 2 + j), ("SC", 4 + j)) for j in range(2)])
-            else:
-                tt(p(4, 6), p(4, 6), d_(0, 2), hi); tt(p(2, 4), p(2, 4), d_(2, 4), lo)
-            net = [
-                (b_(0, 8, 2), p(0, 8, 2), c_(0, 8, 2), lo), (b_(1, 8, 2), p(1, 8, 2), c_(1, 8, 2), hi),
-                (p(0, 8, 2), p(0, 8, 2), c_(0, 8, 2), hi), (p(1, 8, 2), p(1, 8, 2), c_(1, 8, 2), lo),
-                (c_(2, 4), p(1, 8, 4), b_(0, 8, 4), lo), (d_(0, 4), p(0, 8, 2), b_(1, 8, 2), lo),
-                (p(1, 8, 2), p(1, 8, 2), b_(0, 8, 2), hi), (p(2, 8, 4), p(2, 8, 4), b_(3, 8, 4), hi),
-                (c_(0, 2), p(3, 8, 4), d_(1, 4, 2), hi), (p(0, 8, 4), p(1, 8, 4), d_(0, 3, 2), lo), (p(3), p(3), d_(1), lo),
-                (b_(0), p(6), c_(0), hi), (b_(1), p(6), c_(0), lo), (b_(2, 4), p(0, 4, 2), c_(1, 4, 2), lo),
-                (p(5), p(4), c_(2), lo), (p(7), p(4), c_(2), hi), (b_(2), p(3), b_(2), hi),
-                (p(5, 8, 2), p(5, 8, 2), b_(0, 2), lo), (b_(4), p(5), b_(2), hi), (p(7), p(7), b_(3), hi), (out, p(7), b_(4), hi)]
+            def other(s0):
+                mm([[(R(P, s, (0, W)), l, r) for l, r in hist[s] + [(I, R(SA, s, (0, W))), (R("NIH"), R("SB" + z, s, (0, W)))]] for s in range(s0, s0 + 4)])
+            tt(b_(0, 4), p(0, 4), a_(0, 4), lo); other(0)
+            tt(b_(4, 8), p(4, 8), a_(4, 8), hi); other(4)
         else:
-            net = [
-                (b_(0, 4), p(4, 8), a_(4, 8), lo), (b_(4, 8), p(4, 8), a_(4, 8), hi), (p(4, 8), p(0, 4), a_(0, 4), lo), (p(0, 4), p(0, 4), a_(0, 4), hi),
-                (c_(2, 4), p(6, 8), b_(2, 4), lo), (a_(0, 4), p(0, 4), b_(4, 8), lo), (c_(0, 2), p(2, 4), b_(6, 8), hi),
-                (p(2, 4), p(4, 6), b_(0, 2), lo), (p(4, 8), p(4, 8), b_(0, 4), hi), (p(0, 2), p(0, 2), b_(4, 6), hi),
-                (c_(4, 6), p(6, 8), a_(2, 4), hi), (c_(6, 8), p(6, 8), a_(2, 4), lo), (p(6, 8), p(4, 6), a_(0, 2), lo), (p(4, 6), p(4, 6), a_(0, 2), hi),
-                (b_(0, 4), p(1, 8, 2), c_(1, 8, 2), lo), (b_(4, 8), p(1, 8, 2), c_(1, 8, 2), hi),
-                (p(1, 8, 2), p(0, 8, 2), c_(0, 8, 2), lo), (p(0, 8, 2), p(0, 8, 2), c_(0, 8, 2), hi),
-                (c_(2, 4), p(1, 8, 4), b_(0, 3, 2), lo), (a_(0, 4), p(0, 8, 2), b_(4, 8), lo),
-                (p(1, 8, 2), p(1, 8, 2), b_(0, 4), hi), (p(2, 8, 4), p(2, 8, 4), b_(5, 8, 2), hi),
-                (c_(0, 2), p(3, 8, 4), a_(1, 4, 2), hi), (p(0, 8, 4), p(1, 8, 4), a_(0, 3, 2), lo), (p(7), p(7), a_(3), lo),
-                (b_(0), p(2), c_(1), hi), (b_(1), p(2), c_(1), lo), (b_(2, 4), p(0, 8, 6), c_(0, 4, 3), lo),
-                (p(1), p(4), c_(2), lo), (p(3), p(4), c_(2), hi), (b_(2), p(7), b_(2), hi),
-                (p(1, 4, 2), p(1, 4, 2), b_(0, 2), lo), (b_(4), p(1), b_(2), hi), (p(3), p(3), b_(3), hi), (out, p(3), b_(4), hi)]
+            tt(b_(0, 4), p(0, 4), a_(0, 4), lo); tt(b_(4, 8), p(4, 8), a_(4, 8), hi)
+            tt(p(0, 4), p(0, 4), a_(0, 4), hi); tt(p(4, 8), p(4, 8), a_(4, 8), lo)
+        net = [
+            (d_(0, 2), p(0, 2), b_(4, 6), lo), (c_(0, 2), p(2, 4), b_(6, 8), hi), (c_(6, 8), p(4, 6), b_(0, 2), lo), (d_(2, 4), p(6, 8), b_(2, 4), hi),
+            (p(4, 6), p(4, 6), b_(0, 2), hi), (p(0, 2), p(0, 2), b_(4, 6), hi), (p(2, 4), p(2, 4), b_(6, 8), lo), (p(6, 8), p(6, 8), b_(2, 4), lo),
+            (c_(2, 4), p(4, 6), d_(0, 2), lo), (c_(4, 6), p(2, 4), d_(2, 4), hi), (p(4, 6), p(4, 6), d_(0, 2), hi), (p(2, 4), p(2, 4), d_(2, 4), lo),
+            (b_(0, 8, 2), p(0, 8, 2), c_(0, 8, 2), lo), (b_(1, 8, 2), p(1, 8, 2), c_(1, 8, 2), hi),
+            (p(0, 8, 2), p(0, 8, 2), c_(0, 8, 2), hi), (p(1, 8, 2), p(1, 8, 2), c_(1, 8, 2), lo),
+            (c_(2, 4), p(1, 8, 4), b_(0, 8, 4), lo), (d_(0, 4), p(0, 8, 2), b_(1, 8, 2), lo),
+            (p(1, 8, 2), p(1, 8, 2), b_(0, 8, 2), hi), (p(2, 8, 4), p(2, 8, 4), b_(3, 8, 4), hi),
+            (c_(0, 2), p(3, 8, 4), d_(1, 4, 2), hi), (p(0, 8, 4), p(1, 8, 4), d_(0, 3, 2), lo), (p(3), p(3), d_(1), lo),
+            (b_(0), p(6), c_(0), hi), (b_(1), p(6), c_(0), lo), (b_(2, 4), p(0, 4, 2), c_(1, 4, 2), lo),
+            (p(5), p(4), c_(2), lo), (p(7), p(4), c_(2), hi), (b_(2), p(3), b_(2), hi),
+            (p(5, 8, 2), p(5, 8, 2), b_(0, 2), lo), (b_(4), p(5), b_(2), hi), (p(7), p(7), b_(3), hi), (out, p(7), b_(4), hi)]
         for o, x, y, f in net:
             tt(o, x, y, f)
 
-    def stage(P, SA, w0, W, terms, src, thr, M, zthr, fx):
+    def stage(P, SA, w0, W, terms, src, first, dead):
         g, z, u, x = R(nb(), (0, W)), R(nb(), (0, W)), R("U", (w0, w0 + W)), R("FX", (w0, w0 + W))
-        mm([[(g, C(k), src(k)) for k in range(16)]])
-        if thr is None:
-            act(u, g, F.Relu, -32.0, 1.0 / 128)
+        if dead:
+            mm([[(g, C(k), src(k)) for k in range(16)]], False, False)
+            mm([[(g, NI, dead)]], True)
         else:
-            ts(u, g, thr, A.is_ge, 32.0, A.mult)
-        mm([[(z, R(M), u)]])
-        ts(x, z, zthr, A.is_le, fx, A.mult)
+            mm([[(g, C(k), src(k)) for k in range(16)]])
+        if first:
+            ts(u, g, 6000.0, A.is_ge, 1024.0, A.mult)
+            mm([[(z, R("M1"), u)]])
+            if dead:
+                ts(z, z, -63.5 * 1024, A.is_le, -2048.0, A.mult)
+                tt(x, z, u, A.add)
+            else:
+                ts(x, z, -63.5 * 1024, A.is_le, -1024.0, A.mult)
+        else:
+            ts(u, g, 16000.0, A.is_ge, 32.0, A.mult)
+            mm([[(z, R("M2"), u)]])
+            ts(x, z, -64.5 * 32, A.is_le, 4096.0, A.mult)
         for h in (1, 0):
             bk = nb()
             mm([[(R(bk, (j * W, j * W + W)), l, r) for l, r in terms(8 + 4 * h + j) + [(S(8 + 4 * h + j), x)]] for j in range(4)])
             act(R(SA, (4 * h, 4 * h + 4), (0, W)), R(bk, (0, 4 * W)))
-            gr = [[(R(P, 4 * h + j, (0, W)), l, r) for l, r in terms(4 * h + j) + [(S(4 * h + j), x)]] for j in range(4)]
-            mm(gr)
+            mm([[(R(P, 4 * h + j, (0, W)), l, r) for l, r in terms(4 * h + j) + [(S(4 * h + j), x)]] for j in range(4)])
 
-    def fits(W, terms, mlo, mhi, tail):
-        def fill(j, m):
-            b = nb()
-            mm([[(R(b, (i * W, i * W + W)), l, r) for l, r in terms(4 * j + i) + [(NI, m)]] for i in range(4)])
-            return R(b, (0, 4 * W))
+    def fits(W, terms, mode):
         for j in range(4):
-            e = fill(j, mlo)
+            b = nb()
+            mm([[(R(b, (i * W, i * W + W)), l, r) for l, r in terms(4 * j + i)] for i in range(4)])
+            e = R(b, (0, 4 * W))
             sa, sb = R("SGA", (4 * j, 4 * j + 4), (0, W)), R("SGB", (4 * j, 4 * j + 4), (0, W))
-            if tail in "ab":
-                act(sa, e, F.Abs)
-                if tail == "a":
-                    ts(sb, sa, 10.5, A.is_le, 2.0, A.mult)
-                else:
-                    act(sb, sa, F.Sign, 10.5, -1.0)
-                continue
-            act(sa, e, F.Sign, 10.5)
-            if mhi is not mlo:
-                e = fill(j, mhi)
-            if tail == "d":
-                ts(sb, e, 10.5, A.is_le, 2.0, A.mult)
+            if mode[j] == "v":
+                ts(sb, e, MAGIC, A.add, MAGIC, A.is_equal)
             else:
-                act(sb, e, F.Sign, 10.5, -1.0)
-        return [(C(k), R(s, k, (0, W))) for k in range(16) for s in (("SGB",) if tail in "ab" else ("SGA", "SGB"))], {"d": 39.0, "b": 7.0}.get(tail, 23.0)
+                act(sa, e, F.Abs)
+                if mode[j] == "a":
+                    ts(sb, sa, 15.75, A.is_le)
+                else:
+                    act(sb, sa, F.Sign, 15.75, -1.0)
+        return [(C(k), R("SGB", k, (0, W))) for k in range(16)]
 
     def total(e, tm, split):
         h = len(tm) - 4 if split else len(tm)
@@ -418,202 +442,228 @@ def build():
             mm([[(e, l, r) for l, r in tm[h:]]], True)
 
     def places(c0, n):
-        ts(R("DS", (0, n)), R("TRL", (256 + c0, 256 + c0 + n)), XN - 0.5, A.is_ge, -16384.0, A.mult)
         e = R(nb(), (0, n))
-        mm([[(e, ONES, R("LOC", (256 + c0, 256 + c0 + n))), (e, I, R("DS", (0, n)))]])
+        mm([[(e, ONES, R("LOC", (256 + c0, 256 + c0 + n))), (e, I, R("DD", (256 + c0, 256 + c0 + n)))]])
         ts(R("ASU", (0, n)), e, col("KC", 2), A.add, 0.0, A.max)
 
     par = [0]
     for u in range(4):
         lab[:] = ["list", u]
-        if u:
-            worklist("FC", "AC", 32, 8 * u, 192, "CL", *((8, 24) if u == 1 else (0, 32)))
-            e = R(nb(), (0, 192)); cl = R("CL", (0, 12))
-            mm([[(e, R("ONES16"), R("LW", (0, 192)))]])
-            ts(R("OOU"), e, col("KC", 1), A.add, 0.0, A.max)
-            cp(R("TRU"), IND(R("TRL"), cl))
-            lab[0] = "ab"
-            act(R("A0"), IND(R("TA"), cl)); act(R("B0"), IND(R("TB"), cl))
-            lab[0] = "more"
-            act(R("TRG"), IND(R("TRL"), cl))
-            act(R("LS"), R("LS0", (192, 384) if u == 2 else (0, 192)), F.Identity, col("BC", u))
-            cp(IND(R("LOC"), cl), R("LS"))
-            og, trg = "OG", ("TRG", 0)
-        else:
-            act(R("A0"), R("TA", (256, 448))); act(R("B0"), R("TB", (256, 448)))
-            act(R("LOC", (256, 448)), R("LS0", (0, 192)), F.Identity, col("BC", 0))
-            og, trg = "OB", ("TRL", 256)
-        places(0, 48)
-        ts(R("DE"), R(trg[0], (trg[1], trg[1] + 192)), XN - 0.5, A.is_ge, -64.0, A.mult)
-        order = list(range(NC1))[::-1] if u == 2 else list(range(NC1))
-        xg = []
-        for n, c in enumerate(order):
-            w0 = c * W1; lab[0] = "x%d" % n
+        ch, p0 = [], 0
+        for c0, l0, W in CH1[u]:
+            ch.append((c0, l0, W, p0)); p0 += W
+        nch = len(ch)
+        K = sum(W for c0, l0, W, p0 in ch if c0 is None)
+        act(R("LS"), R("LS0"), F.Identity, col("BC", u))
+        if u == 1:
+            ms(R("AC", (0, 8)), 1.0)
+            worklist("FC", "AC", 32, [(8, 12), (20, 24)], K, "CL", (12, 20))
+        elif u == 2:
+            worklist("FC", "AC", 32, [(16, 24), (28, 32), (0, 16)], K, "CL", (24, 28))
+        elif u == 3:
+            worklist("FC", "AC", 32, [(24, 32), (0, 24)], K, "CL", None, True)
+        src1, xg = [], []
+        for n, (c0, l0, W, p0) in enumerate(ch):
+            w = (p0, p0 + W)
+            if c0 is None:
+                lab[0] = "more"
+                cl = R("CL", (l0 // 16, (l0 + W) // 16))
+                cp(R("TRU", w), IND(R("TRL"), cl))
+                e = R(nb(), (0, W))
+                mm([[(e, R("ONES16"), R("LWB", (l0, l0 + W)))]])
+                ts(R("OOU", w), e, col("KC", 1), A.add, 0.0, A.max)
+                act(R("DE", w), IND(R("DD"), cl))
+                act(R("A0", w), IND(R("TA"), cl)); act(R("B0", w), IND(R("TZ"), cl))
+                cp(IND(R("LOC"), cl), R("LS", w))
+                src1.append((("TRU", p0), ("OG", 16 * p0), R("DE", w), cl))
+            else:
+                lab[0] = "fixed"
+                act(R("LOC", (256 + c0, 256 + c0 + W)), R("LS", w))
+                src1.append((("TR0", c0), ("OB", 16 * c0), R("DD", (256 + c0, 256 + c0 + W)) if u else None, None))
+            lab[0] = "x%d" % n
             for h in range(2):
-                a, b = w0 + h * W1 // 2, w0 + (h + 1) * W1 // 2
-                gx = (R("XG", (16 * a, 16 * b)), IND(R("XW", (256, 2064)), R("TRU", (a, b))))
-                xg.append(cp(*gx) if n == 0 and (u or h) else act(*gx))
-                if u:
-                    act(R("OG", (16 * a, 16 * b)), IND(R("OB"), R("OOU", (a, b))))
+                a, b = h * W // 2, (h + 1) * W // 2
+                tr = src1[n][0]
+                xg.append(move(GX[n > 0][h], R("XG", (16 * (p0 + a), 16 * (p0 + b))), IND(R("XW", (256, 2064)), R(tr[0], (tr[1] + a, tr[1] + b)))))
+                if c0 is None:
+                    act(R("OG", (16 * (p0 + a), 16 * (p0 + b))), IND(R("OB"), R("OOU", (p0 + a, p0 + b))))
 
         def onehot():
-            b1, b2, b3, top, few = nb(), nb(), nb(), (0, 96), (0, 32)
+            b1, b2, b3, few = nb(), nb(), nb(), (0, 32)
             lab[0] = "hot"
-            mm([[(R(b1, (128 * j, 128 * j + 128), p=top), R("A0" if j < 2 else "B0", (96 * (j % 2), 96 * (j % 2) + 96)), I)] for j in range(4)])
-            act(R("ABT", p=top), R(b1, p=top))
+            big, small = [[("T", 256), ("T", 384)], [("T", 448), ("", 128)], [("", 64), ("T", 640)], [("", 0), ("", 128)]][u]
+            gr = []
+            for j, (t, d) in enumerate((("TA", "A0"), ("TZ", "B0"))):
+                gr.append([(R(b1, (192 * j, 192 * j + 128)), R(t if big[0] else d, (big[1], big[1] + 128)), I)])
+                for h in range(2):
+                    gr.append([(R(b1, (192 * j + 128, 192 * j + 192), p=(64 * h, 64 * h + 64)), R(t if small[0] else d, (small[1], small[1] + 64)),
+                                R("IPM", (64 * h, 64 * h + 64)))])
+            mm(gr)
+            act(R("ABT"), R(b1, (0, 384)))
             for a in range(32):
-                ts(R("W2", (OAB + 256 * a, OAB + 256 * a + 256), p=top), R("ABT", (0, 256), p=top), float(a), A.is_equal)
-            c0 = 0 if OHM else 1; lab[0] = "hotb"
-            for b in range(c0, 33):
-                o, i_ = R("W2", (OBB + 256 * b, OBB + 256 * b + 256), p=top), R("ABT", (256, 512), p=top)
-                if b <= OHM:
-                    act(o, i_, F.Sign, 0.5 - b)
+                ts(R("W2", (OAB + 192 * a, OAB + 192 * a + 192)), R("ABT", (0, 192)), float(a), A.is_equal)
+            for n in range(16):
+                o, z = R("W2", (OBB + 192 * n, OBB + 192 * n + 192)), R("ABT", (192, 384))
+                if n < 15:
+                    ts(o, z, 2.0 ** (14 * n - 98), A.min)
                 else:
-                    ts(o, i_, b - 1.0, A.is_equal)
+                    cp(o, z)
             lab[0] = "flag"
             for g in range(8):
-                mm([[(R(b2, (33 * g + c0, 33 * g + 33), p=few), R("W2", (OAB + x, OAB + 8192, 256), p=top), R("W2", (OBB + 256 * c0 + x, OBB + 256 * 33, 256), p=top))
-                     for x in [128 * h + 16 * g + k for h in range(2) for k in range(16)]]])
-            if OHM:
-                act(R("CS", p=few), R(b2, (0, 264), p=few))
-                tt(R("FF", (0, 8), (0, OHM), p=few), R("CS", (0, 8), (0, OHM), p=few), R("CS", (0, 8), (1, OHM + 1), p=few), A.is_gt)
-                if OHM < 32:
-                    ts(R("FF", (0, 8), (OHM, 32), p=few), R("CS", (0, 8), (OHM + 1, 33), p=few), 0.5, A.is_gt)
-            else:
-                for g in range(8):
-                    act(R("FF", g, p=few), R(b2, (33 * g + 1, 33 * g + 33), p=few), F.Sign)
+                mm([[(R(b2, (16 * g, 16 * g + 16), p=few), R("W2", (OAB + x, OBB, 192)), R("W2", (OBB + x, P0, 192)))
+                     for x in list(range(16 * g, 16 * g + 16)) + list(range(128 + 8 * g, 136 + 8 * g))]])
+            tt(R("CI", p=few), R(b2, (0, 128), p=few), R("SCL", p=few), A.mult)
+            ts(R("CJ", (0, 8), (0, 32, 2), p=few), R("CI", p=few), 31, A.bitwise_and)
+            ts(R("CJ", (0, 8), (1, 32, 2), p=few), R("CI", p=few), 31 * 128, A.bitwise_and)
+            cp(R("FF", p=few), R("CJ", p=few))
             e = R(b3, (0, 64))
             gr = [(e, I, R("AT")), (e, I, R("FT"))] if u else [(e, R("SEL", (128, 256), p=few), R("ONE", (0, 64), p=few))]
             gr += [(R(b3, (h, 64, 2)), R("SEL", (240 * h + 112 - 16 * g, 240 * h + 240 - 16 * g), p=few), R("FF", g, p=few)) for g in range(8) for h in range(2)]
             mm([gr])
             ts(R("FT"), e, 1.75 if u else 0.5, A.is_ge)
-            worklist("FT", "AT", 64, 12 * u, 256, "TL", 0, 64)
+            worklist("FT", "AT", 64, [(12 * u, 64), (0, 12 * u)] if u else [(0, 64)], 256, "TL")
             tl = R("TL")
             cp(R("VCU"), IND(R("VC"), tl)); act(R("VLG"), IND(R("VL"), tl))
             lab[0] = "late"
-            cp(R("SOU"), IND(R("SO"), tl)); act(R("VCF"), IND(R("VC"), tl)); act(R("OX"), IND(R("XW", (0, 1280)), tl))
-            ts(R("EM"), R("VCF"), VE - 0.5, A.is_ge, -2.0 ** 35, A.mult)
-            for w0 in range(0, 256, 64):
-                lab[0] = "loc%d" % w0
-                act(R("SRC", (16 * w0, 16 * w0 + 1024)), IND(R("LOC"), R("VCU", (w0, w0 + 64))))
+            tt(R("TI", (0, 256)), IND(R("SO"), tl), R("DUMP2"), A.max)
+            ts(R("SOU"), R("TI", (0, 256)), -float(DB), A.add)
+            act(R("VCF"), IND(R("VC"), tl)); act(R("OX"), IND(R("XW", (0, 1280)), tl))
+            ts(R("EM"), R("VCF"), VE - 0.5, A.is_ge, -2.0 ** 50, A.mult)
+            for j, w0 in enumerate(range(0, 256, 64)):
+                lab[0] = "loc%d" % j
+                move(GL[j], R("SRC", (16 * w0, 16 * w0 + 1024)), IND(R("LOC"), R("VCU", (w0, w0 + 64))))
                 e = R(nb(), (0, 64))
                 mm([[(e, C(k), R("SRC", (16 * w0 + k, 16 * w0 + 1024, 16))) for k in range(16)] + [(e, I, R("VLG", (w0, w0 + 64)))]])
                 ts(R("ADU", (w0, w0 + 64)), e, 0.0, A.max)
 
         def send_b(done):
             lab[0] = "send"
-            act(R("BG", (0, 768)), IND(R("POOL", (784, OWN + 3072 * u + 16 * W1 * done)), R("ASU", (0, 48))))
+            places(0, 48)
+            act(R("BG", (0, 768)), IND(R("POOL", (784, OWN + 3072 * u + 16 * done)), R("ASU", (0, 48))))
             turn("BG", 0, "BS", u)
             send("BS", u, "POOL", 16, "ba%d" % u, extra=xg)
 
-        def terms1(c):
-            return lambda k: [(I, R("XG", (16 * W1 * c + k, 16 * W1 * (c + 1), 16))), (NI, R(og, (16 * W1 * c + k, 16 * W1 * (c + 1), 16)))]
+        def xk(n, k, a=0, b=None):
+            W, p0 = ch[n][2:]
+            return R("XG", (16 * (p0 + a) + k, 16 * (p0 + (b or W)), 16))
+
+        def ok(n, k, a=0, b=None):
+            o = src1[n][1]
+            return R(o[0], (o[1] + 16 * a + k, o[1] + 16 * (b or ch[n][2]), 16))
 
         def pre1(n):
-            c = order[n]; pr = (par[0] + n) % 2; lab[0] = "pre1%d" % n
-            stage("PB" if pr else "PA", "SA%d" % pr, c * W1, W1, terms1(c), lambda k: terms1(c)(k)[0][1], None if n and SMALL else 6000.0, "M1", -63.5 * 32, -1024.0)
+            W, p0 = ch[n][2:]; pr = (par[0] + n) % 2; lab[0] = "pre1%d" % n
+            stage("PB" if pr else "PA", "SA%d" % pr, p0, W, lambda k: [(I, xk(n, k)), (NI, ok(n, k))], lambda k: xk(n, k), True, src1[n][2])
 
         def post1(n):
-            c = order[n]; w = (c * W1, c * W1 + W1); tail = TAIL1[n == NC1 - 1]; lab[0] = "fit1%d" % n
-            pm, uu, ft, mk = R("PM", w), R("U", w), R("FIT", w), R("MR", w)
-            tm, thr = fits(W1, terms1(c), pm, pm, tail)
-            e = R(nb(), (0, W1))
-            total(e, [(NI, uu)] + tm, n == NC1 - 1)
-            ts(ft, e, thr, A.is_ge)
-            b = nb(); e, e2 = R(b, (0, W1)), R(b, (128, 128 + W1))
-            mm([[(e, R("OP32"), ft), (e, I, uu), (e, I, R("DE", w))], [(e2, R("OM32"), ft), (e2, NI, uu)]])
+            c0, l0, W, p0 = ch[n]; w = (p0, p0 + W); last = n == nch - 1; lab[0] = "fit1%d" % n
+            pm, uu, ft, mk, sa = R("PM", w), R("U", w), R("FIT", w), R("MR", w), "SA%d" % ((par[0] + n) % 2)
+            dead = src1[n][2]
+            tm = fits(W, lambda k: ([(I15, xk(n, k)), (NI15, ok(n, k))] if k < 8 else [(I15, R(sa, k - 8, (0, W)))]) + [(NI15, pm)], FIT1[last])
+            e = R(nb(), (0, W))
+            total(e, [(NI, uu)] + tm, last)
+            ts(ft, e, bound(FIT1[last], 0), A.is_ge)
+            b = nb(); e, e2 = R(b, (0, W)), R(b, (128, 128 + W))
+            mm([[(e, R("OP32"), ft), (e, R("IQ"), uu)] + ([(e, I, dead)] if dead else []), [(e2, R("OM32"), ft), (e2, NI, uu)]])
             ts(mk, e, 37.5, A.is_lt, 2048.0, A.mult)
-            ts(R("KL", w), e2, 5.5, A.is_ge, float(XN), A.mult)
-            base = OWN + 3072 * u + 16 * W1 * n; lab[0] = "pool%d" % n
-            for j in range(4):
-                b = nb()
-                mm([[(R(b, (i * W1, i * W1 + W1)), l, r) for l, r in ((NI, terms1(c)(4 * j + i)[1][1]), (NI, pm), (S(4 * j + i), mk))] for i in range(4)])
-                o, e = R("POOL", (base + 4 * j * W1, base + 4 * (j + 1) * W1)), R(b, (0, 4 * W1))
-                if n == NC1 - 1 and j % 2:
-                    ts(o, e, 255.0, A.add, 0.0, A.max)
-                else:
-                    act(o, e, F.Relu, 255.0)
-            if u:
-                tt(IND(R("TRL"), R("CL", (w[0] // 16, w[1] // 16))), R("TRG", w), R("KL", w), A.max)
+            ts(R("KL", w), e2, 5.5, A.is_ge, -DEAD, A.mult)
+            lab[0] = "pool%d" % n
+            for a in range(0, W, 64):
+                base = OWN + 3072 * u + 16 * (p0 + a)
+                for j in range(2):
+                    b = nb()
+                    mm([[(R(b, (i * 64, i * 64 + 64)), l, r) for l, r in ((NI, ok(n, 8 * j + i, a, a + 64)), (NI, R("PM", (p0 + a, p0 + a + 64))),
+                                                                          (S(8 * j + i), R("MR", (p0 + a, p0 + a + 64))))] for i in range(8)])
+                    o = R("POOL", (base + 512 * j, base + 512 * j + 512))
+                    if POOLQ[last][j] == "v":
+                        ts(o, R(b), 255.0, A.add, 0.0, A.max)
+                    else:
+                        act(o, R(b), F.Relu, 255.0)
+            lab[0] = "kill%d" % n
+            if c0 is None:
+                tt(IND(R("DD"), src1[n][3]), dead, R("KL", w), A.add)
             else:
-                tt(R("TRL", (256 + w[0], 256 + w[1])), R("TRL", (256 + w[0], 256 + w[1])), R("KL", w), A.max)
+                d = R("DD", (256 + c0, 256 + c0 + W))
+                tt(d, d, R("KL", w), A.add)
 
         pre1(0)
-        if u == 1:
+        if SENDB[u] == 0:
             send_b(0)
-        for n in range(NC1):
-            if n + 1 < NC1:
+        for n in range(nch):
+            if n + 1 < nch:
                 pre1(n + 1)
             pr = (par[0] + n) % 2
+            W, p0 = ch[n][2:]
             lab[0] = "med1%d" % n
-            median("PB" if pr else "PA", "SA%d" % pr, W1, R("PM", (order[n] * W1, order[n] * W1 + W1)), AS1[n > 0],
-                   [terms1(order[n])(k) + [(S(k), R("FX", (order[n] * W1, order[n] * W1 + W1)))] for k in range(8)])
+            median("PB" if pr else "PA", "SA%d" % pr, W, R("PM", (p0, p0 + W)), AS1[n > 0],
+                   [[(I, xk(n, k)), (NI, ok(n, k)), (S(k), R("FX", (p0, p0 + W)))] for k in range(8)])
             if n == 0:
                 onehot()
             post1(n)
-            if (u in (0, 2) and n == 0) or (u == 3 and n == NC1 - 1):
-                send_b(n + 1)
-        par[0] = (par[0] + NC1) % 2
+            if SENDB[u] == n + 1:
+                send_b(p0 + W)
+        par[0] = (par[0] + nch) % 2
 
         win = R("POOL", (0, OWN + 3072 * (u + 1)))
         st2 = [sum(CH2[:n]) for n in range(len(CH2))]
         for n, W in enumerate(CH2):
             for h in range(2):
                 a, b = st2[n] + h * W // 2, st2[n] + (h + 1) * W // 2; lab[0] = "b%d" % n
-                gx = (R("BG", (16 * a, 16 * b)), IND(win, R("ADU", (a, b))))
-                if n == 0 and h:
-                    cp(*gx)
-                else:
-                    act(*gx)
+                move(GB[n > 0][h], R("BG", (16 * a, 16 * b)), IND(win, R("ADU", (a, b))))
 
-        def terms2(n):
-            return lambda k: [(NI, R("BG", (16 * st2[n] + k, 16 * (st2[n] + CH2[n]), 16)))]
+        def bk(n, k, name="BG"):
+            return R(name, (16 * st2[n] + k, 16 * (st2[n] + CH2[n]), 16))
 
         def pre2(n):
             W, w0, pr = CH2[n], st2[n], (par[0] + n) % 2; lab[0] = "pre2%d" % n
-            stage("PB" if pr else "PA", "SA%d" % pr, w0, W, terms2(n), lambda k: terms2(n)(k)[0][1], 16000.0, "M2", -64.5 * 32, 4096.0)
+            stage("PB" if pr else "PA", "SA%d" % pr, w0, W, lambda k: [(NI, bk(n, k))], lambda k: bk(n, k), False, None)
             e = R(nb(), (0, W))
             mm([[(e, ONES, R("U", (w0, w0 + W)))]])
             ts(R("NH", (w0, w0 + W)), e, 13.5 * 32, A.is_ge, 512.0, A.mult)
+            lab[0] = "clip%d" % n
+            step = 512 if CLIP[n] == "a" else 1024
+            for a in range(16 * w0, 16 * (w0 + W), step):
+                w = (a, min(a + step, 16 * (w0 + W)))
+                if CLIP[n] == "a":
+                    act(R("SRC", w), R("BG", w), F.Relu, 255.0, -1.0)
+                else:
+                    ts(R("SRC", w), R("BG", w), 255.0, A.min)
+
+        lowv, highv = 1024.0 * 64.0 ** u, 32768.0 * 64.0 ** u
 
         def post2(n):
-            W, w0 = CH2[n], st2[n]; lab[0] = "fit2%d" % n
-            w = (w0, w0 + W); tail = TAIL2[n == len(CH2) - 1]
-            pm, mh, ml, tf = R("PM", w), R("MH", w), R("ML", w), terms2(n)
+            W, w0 = CH2[n], st2[n]; lab[0] = "new%d" % n
+            w = (w0, w0 + W); last = n == len(CH2) - 1
+            pm = R("PM", w)
             act(R("X0", w), pm, F.Relu, 255.0)
-            if tail in "ab":
-                for a in range(16 * w0, 16 * w[1], 512):
-                    act(R("SRC", (a, a + 512)), R("BG", (a, a + 512)), F.Relu, 255.0, -1.0)
-                ml = mh = R("X0", w)
-                tf = lambda k: [(I, R("SRC", (16 * w0 + k, 16 * w[1], 16)))]
+            if CLIP[n] == "a":
+                tf = lambda k: [(I15, bk(n, k, "SRC")), (NI15, R("X0", w))]
             else:
-                ts(mh, pm, -255.0, A.max)
-                ts(ml, pm, -244.5, A.is_le, -1024.0, A.mult)
-                tt(ml, ml, mh, A.add)
+                ts(R("X1", w), pm, -1.0, A.mult, 255.0, A.min)
+                tf = lambda k: [(NI15, bk(n, k, "SRC")), (I15, R("X1", w))]
             tt(R("XQ", w), R("X0", w), R("NH", w), A.max)
-            if SMALL:
-                e = R(nb(), (0, W))
-                mm([[(e, I, R("XQ", w)), (e, NI, R("OX", w))]])
-                act(R("NE", w), e, F.Abs)
-            else:
-                tt(R("NE", w), R("XQ", w), R("OX", w), A.not_equal)
+            e = R(nb(), (0, W))
+            mm([[(e, I, R("XQ", w)), (e, NI, R("OX", w))]])
+            act(R("NE", w), e, F.Abs)
             cp(IND(R("XW", (0, 1280)), R("TL", (w0 // 16, w[1] // 16))), R("XQ", w))
             e = R(nb(), (0, W))
             mm([[(e, R("ONESB"), R("NE", w)), (e, I, R("EM", w))]])
-            ts(R("AM", w), e, 1.0, A.max, 32.0 ** (u + 1), A.min)
-            tm, thr = fits(W, tf, ml, mh, tail)
+            ts(R("AM", w), e, lowv, A.max, highv, A.min)
+            lab[0] = "fit2%d" % n
+            tm = fits(W, tf, FIT2[last])
             e = R(nb(), (0, W))
-            total(e, [(I, R("U", w)), (I, R("NH", w))] + tm, n == len(CH2) - 1)
-            act(R("SN", w), e, F.Sign, -thr)
+            total(e, [(I, R("U", w)), (I, R("NH", w))] + tm, last)
+            act(R("SN", w), e, F.Sign, bound(FIT2[last], 1))
             tt(R("VA", w), R("SN", w), R("AM", w), A.mult)
             lab[0] = "back%d" % n
             for j in range(W // 32):
                 b = nb(); a = w0 + 32 * j
                 mm([[(R(b, (k, 512, 16)), S(k), R("VA", (a, a + 32)))] for k in range(16)])
                 act(R("SRC", (16 * a, 16 * a + 512)), R(b))
-                cp(IND(R("W2"), R("SOU", (a, a + 32))), R("SRC", (16 * a, 16 * a + 512)))
-            act(R("KL", w), R("SN", w), F.Identity, VE / 2.0, -VE / 2.0)
-            tt(IND(R("VC"), R("TL", (w0 // 16, w[1] // 16))), R("VCF", w), R("KL", w), A.max)
+                cp(IND(R("W2", (P0 + DB - 8192, P0 + 8192)), R("SOU", (a, a + 32))), R("SRC", (16 * a, 16 * a + 512)))
+            lab[0] = "empty%d" % n
+            act(R("KV", w), R("SN", w), F.Identity, VE / 2.0, -VE / 2.0)
+            tt(IND(R("VC"), R("TL", (w0 // 16, w[1] // 16))), R("VCF", w), R("KV", w), A.max)
 
         pre2(0)
         for n, W in enumerate(CH2):
@@ -622,57 +672,45 @@ def build():
             if u == 3 and n == 0:
                 lab[0] = "yb"
                 places(384, 128)
-                pw = R("POOL", (784, OWN + 4 * 3072))
-                act(R("TM1"), I, F.Identity, 0.0, 256.0)
                 for j in range(4):
-                    b, w, o = R(nb()), (512 * j, 512 * j + 512), R("ASU", (32 * j, 32 * j + 32))
-                    act(R("XG", w), IND(pw, o), F.Relu, 255.0, -1.0)
-                    act(R("OG", w), IND(pw, o), F.Sign, -1000.0)
-                    mm([[(b, I, R("XG", w)), (b, R("TM1"), R("OG", w))]])
-                    act(R("OB", w), b, F.Identity, 256.0)
+                    w = (512 * j, 512 * j + 512)
+                    act(R("OB", w), IND(R("POOL", (784, OWN + 4 * 3072)), R("ASU", (32 * j, 32 * j + 32))), F.Identity, 255.0, -1.0)
+                for j in range(2):
+                    w = (1024 * j, 1024 * j + 1024)
+                    ts(R("OG", w), R("OB", w), -600.0, A.is_le, 512.0, A.mult)
             pr = (par[0] + n) % 2
             lab[0] = "med2%d" % n
             median("PB" if pr else "PA", "SA%d" % pr, W, R("PM", (st2[n], st2[n] + W)), AS2[n > 0],
-                   [terms2(n)(k) + [(S(k), R("FX", (st2[n], st2[n] + W)))] for k in range(8)])
+                   [[(NI, bk(n, k)), (S(k), R("FX", (st2[n], st2[n] + W)))] for k in range(8)])
             post2(n)
         par[0] = (par[0] + len(CH2)) % 2
-        lab[0] = "end"
+        lab[0] = "turn"
         if u < 3:
             turn("XW", 256, "XS", u + 1)
             send("XS", u + 1, "XW", 1280, "xa%d" % (u + 1))
-        if TRED:
-            b = nb()
-            mm([[(R(b, (8 * j, 8 * j + 8)), R("W2", (128 * j, 128 * j + 128)), R("ONES", (0, 128, 16)))] for j in range(64)])
-            act(R("AB"), R(b), F.Abs, 0.0, 1.0 / (16 * 32.0 ** (u + 1)))
-            ts(R("ABT"), R(b), 0.0, A.is_lt, float(XN), A.mult)
-            e = R(nb(), (0, 32))
-            mm([[(e, I, R("AC")), (e, I, R("FC"))] + [(e, R("Z8", (120 - 8 * m, 248 - 8 * m)), R("AB", (8 * (m % 2) + m // 2, 512, 16))) for m in range(16)]])
-            ts(R("FC"), e, 1.75, A.is_ge)
-            b = nb()
-            for h in range(4):
-                mm([[(R(b, (c, 512, 8)), R("IP", (112 + 128 * c - 16 * g, 240 + 128 * c - 16 * g)), R("ABT", (g, 512, 8))) for g in range(8)] for c in (2 * h, 2 * h + 1)])
-            if u == 3:
-                cp(R("DS"), R(b, (384, 512)))
-                ts(R("DS"), R("DS"), 512.0, A.min)
-            tt(R("TRL", (256, 768)), R(b), R("TRL", (256, 768)), A.max)
-            continue
-        for j in (1, 0):
-            w = (256 * j, 256 * j + 256); e = R(nb(), (0, 256))
-            mm([[(e, C(k), R("W2", (4096 * j + k, 4096 * j + 4096, 16))) for k in range(16)]])
-            act(R("AB", w), e, F.Abs, 0.0, 1.0 / (16 * 32.0 ** (u + 1)))
-            ts(e, e, 0.0, A.is_lt, float(XN), A.mult)
-            if u == 3 and j:
-                ts(R("DS"), R(e[1], (128, 256)), 1.0, A.is_ge, 512.0, A.mult)
-            t = R("TRL", (256 + w[0], 256 + w[1]))
-            tt(t, e, t, A.max)
-        e = R(nb(), (0, 32))
-        mm([[(e, I, R("AC")), (e, I, R("FC"))] + [(e, C(m), R("AB", (m, 512, 16))) for m in range(16)]])
-        ts(R("FC"), e, 1.75, A.is_ge)
+        pieces = [[(192, 320, 0), (0, 192, 1), (320, 512, 0)], [(384, 448, 0), (0, 384, 1), (448, 512, 0)],
+                  [(256, 512, 1), (0, 256, 1)], [(384, 512, 1), (0, 384, 1)]][u]
+        for j, (a, b, flags) in enumerate(pieces):
+            lab[0] = "end%d" % j
+            e = R(nb(), (0, b - a))
+            mm([[(e, C(k), R("W2", (P0 + 16 * a + k, P0 + 16 * b, 16))) for k in range(16)]])
+            if flags:
+                act(R("AB", (a, b)), e, F.Abs, 0.0, 1.0 / (16 * highv))
+            if u == 3 and j == 0:
+                ts(R("DS"), e, -12.0 * lowv, A.is_le, 512.0, A.mult)
+            d = R("DD", (256 + a, 256 + b))
+            tt(d, e, d, A.min)
+        n = (12, 24, 32, 32)[u]
+        lab[0] = "flags"
+        e = R(nb(), (0, n))
+        mm([[(e, I, R("AC", (0, n))), (e, I, R("FC", (0, n)))] + [(e, C(m), R("AB", (m, 16 * n, 16))) for m in range(16)]])
+        ts(R("FC", (0, n)), e, 1.75, A.is_ge)
 
+    lab[0] = "out"
     dma("s", R("yx"), R("XW", (256, 1280)), 262144)
     for j in range(4):
         b, w = nb(), (512 * j, 512 * j + 512)
-        mm([[(R(b, (k, 512, 16)), S(k), R("DS", (32 * j, 32 * j + 32)))] for k in range(16)])
+        mm([[(R(b), I, R("OG", w))] + [(R(b, (k, 512, 16)), S(k), R("DS", (32 * j, 32 * j + 32))) for k in range(16)]])
         tt(R("BG", w), R(b), R("OB", w), A.max)
         if j % 2:
             dma("s", R("yb", (512 * j - 512, 512 * j + 512)), R("BG", (512 * j - 512, 512 * j + 512)), 262144)
@@ -685,14 +723,14 @@ def build():
     for j in range(2):
         b = nb()
         mm([[(R(b, p=g8), gi, R("XG", (512 * j, 512 * j + 512)))] + [(R(b, (m, 512, 16), p=g8), gm(m), R("FT", (32 * j, 32 * j + 32))) for m in range(16)]])
-        act(R("SO", (512 * j, 512 * j + 512), p=g8), R(b, p=g8))
-    dma("a", R("yt"), R("SO", (0, 1024), p=g8), 32768)
-    ts(R("AB"), R("TRL", (256, 768)), XN - 0.5, A.is_lt)
+        act(R("YF", (512 * j, 512 * j + 512), p=g8), R(b, p=g8))
+    dma("a", R("yt"), R("YF", p=g8), 32768)
+    ts(R("AB"), R("DD", (256, 768)), -0.5, A.is_ge)
     ts(R("AC"), R("FC"), 32.0, A.mult)
     b = nb()
     mm([[(R(b, p=g8), gi, R("AB"))] + [(R(b, (m, 512, 16), p=g8), gm(m), R("AC")) for m in range(16)]])
-    act(R("TA", (0, 512), p=g8), R(b, p=g8))
-    dma("a", R("yc"), R("TA", (0, 512), p=g8), 16384)
+    act(R("VC", (0, 512), p=g8), R(b, p=g8))
+    dma("a", R("yc"), R("VC", (0, 512), p=g8), 16384)
     return ops
 
 
@@ -802,6 +840,126 @@ def schedule(ops):
         if best[0] == was:
             FOUND.pop()
     end, st, bank = best
+    last = {}
+    for u in sorted(bank, key=lambda u: min(st[j] for j in unit[u])):
+        for d in last.get(bank[u], []):
+            for j in unit[u]:
+                ops[j]["deps"][d] = ops[j]["deps"].get(d, False) or ops[j]["q"] != ops[d]["q"] or ops[j]["q"] != "p"
+        last[bank[u]] = unit[u]
+    return sorted(range(n), key=lambda j: (st[j], j)), st, bank
+
+
+def graph(ops):
+    n = len(ops)
+    pre = [[(d, (ops[d]["lat"] + LAT) if w else 0.0) for d, w in o["deps"].items()] for o in ops]
+    suc = [[] for _ in range(n)]
+    unit = {}
+    for j in range(n):
+        if ops[j]["use"]:
+            unit.setdefault(ops[j]["use"], []).append(j)
+        for d, l in pre[j]:
+            suc[d].append((j, l))
+    G = {}
+    for back, ed in ((False, pre), (True, suc)):
+        gate = [set(d for d, l in ed[j]) for j in range(n)]
+        opens = [False] * n
+        for u, js in unit.items():
+            s = set(js)
+            js = js[::-1] if back else js
+            for j in js:
+                gate[js[0]] |= {d for d, l in ed[j] if d not in s}
+                if j != js[0]:
+                    gate[j].add(js[0])
+            opens[js[0]] = True
+        nx = [[] for _ in range(n)]
+        for j in range(n):
+            for d in gate[j]:
+                nx[d].append(j)
+        G[back] = (ed, [len(g) for g in gate], nx, opens)
+    return G, unit
+
+
+def sweep(ops, G, unit, key, back, delta):
+    ed, cnt, nx, opens = G[back]
+    n, cnt = len(ops), list(cnt)
+    cost, q, use = [o["cost"] for o in ops], [o["q"] for o in ops], [o["use"] for o in ops]
+    st, rdy, free = [0.0] * n, [0.0] * n, {x: 0.0 for x in q}
+    bfree = {b: 0.0 for b in BANKS}
+    bank, left, uend = {}, {u: len(js) for u, js in unit.items()}, {}
+    el = [j for j in range(n) if not cnt[j]]
+    while el:
+        tb = min(bfree.values())
+        best, bc, es = -1, 1e18, []
+        for j in el:
+            t, f = rdy[j], free[q[j]]
+            if f > t: t = f
+            if opens[j] and tb > t: t = tb
+            es.append(t)
+            if t + cost[j] < bc:
+                bc, best = t + cost[j], j
+        qq = q[best]
+        t0 = min(t for t, j in zip(es, el) if q[j] == qq)
+        lim = t0 + delta * (bc - t0)
+        pick, pk, pt = -1, 1e18, 0.0
+        for t, j in zip(es, el):
+            if q[j] == qq and t <= lim and key[j] < pk:
+                pick, pk, pt = j, key[j], t
+        j = pick
+        el.remove(j)
+        st[j] = pt
+        if qq is not None:
+            free[qq] = pt + cost[j]
+        u = use[j]
+        if u:
+            if opens[j]:
+                b = max((b for b in BANKS if bfree[b] <= pt), key=lambda b: bfree[b])
+                bank[u] = b; bfree[b] = 1e17; uend[u] = 0.0
+            uend[u] = max(uend[u], pt + cost[j])
+            left[u] -= 1
+            if not left[u]:
+                bfree[bank[u]] = uend[u] + LAT
+        for x in nx[j]:
+            cnt[x] -= 1
+            if not cnt[x]:
+                rdy[x] = max([st[d] + cost[d] + l for d, l in ed[x]] or [0.0])
+                el.append(x)
+    return max(st[j] + cost[j] + (0 if back else ops[j]["lat"]) for j in range(n)), st, bank
+
+
+def schedule(ops):
+    G, unit = graph(ops)
+    n, cost = len(ops), [o["cost"] for o in ops]
+    tail = [0.0] * n
+    for j in range(n - 1, -1, -1):
+        tail[j] = cost[j] + max([tail[x] + l for x, l in G[True][0][j]] or [ops[j]["lat"]])
+    best = None
+    for delta in (0.0, 0.3, 0.6, 1.0):
+        key = [-t for t in tail]
+        for it in range(SWEEPS):
+            r = sweep(ops, G, unit, key, False, delta)
+            if best is None or r[0] < best[0]:
+                best = r + (delta, key)
+            bk = sweep(ops, G, unit, [-r[1][j] - cost[j] for j in range(n)], True, delta)[1]
+            key = [-bk[j] - cost[j] for j in range(n)]
+    seed = [SEED]
+
+    def pick(a):
+        seed[0] = (seed[0] * 1103515245 + 12345) % 2147483648
+        return a[(seed[0] >> 8) % len(a)]
+    kinds = sorted({(o["tag"], o["rd"]) for o in ops})
+    for it in range(TRIES):
+        sh, every = {}, pick((1, 0, 0))
+        for _ in range(pick((1, 2))):
+            t, rd = pick(kinds)
+            v = pick((-1, 1)) * pick((300, 1000, 3000, 8000))
+            for x in range(4) if every else (rd,):
+                sh[(t, x)] = v
+        base = best[pick((4, 4, 1))]
+        key = [base[j] + sh.get((o["tag"], o["rd"]), 0) for j, o in enumerate(ops)]
+        r = sweep(ops, G, unit, key, False, best[3])
+        if r[0] < best[0]:
+            best = r + (best[3], key)
+    end, st, bank = best[:3]
     last = {}
     for u in sorted(bank, key=lambda u: min(st[j] for j in unit[u])):
         for d in last.get(bank[u], []):

import math
from concourse.bass import DstId, RemoteDMATransfer
from concourse.mybir import AluOpType as A, ActivationFunctionType as F

CH1 = [[(0, None, 64), (64, None, 128)],
       [(192, None, 128), (None, 0, 64)],
       [(384, None, 64), (None, 64, 64), (None, 0, 64)],
       [(None, 0, 64), (None, 64, 128)]]
SENDB = [1, 0, 2, 1]
CH2 = [96, 96, 64]
FIT1 = ("bbbb", "vbvb")
FIT2 = ("bbbb", "vbvb")
CLIP = "aaa"
GX = ("va", "aa")
GB = ("av", "aa")
GL = "aaaa"
POOLQ = ("aa", "av")
AS1 = (1, 1)
AS2 = (1, 1)
MOVES = []
FOUND = []
SWEEPS = 4
TRIES = 2000
SEED = 1
XN, VE = 1792, 816
OWN = 800
OAB, OBB, P0 = 0, 6144, 9216
DB = 3904
DEAD = 16384.0
MAGIC = 1.5 * 2.0 ** 28
LN2 = math.log(2.0)

bf, f4, i4, u2 = "bfloat16", "float32", "int32", "uint16"
hf = "float16"
WM = 128
SCRATCH = {}
for _n, _s, _d in [
    ("OB", [8192], bf), ("POOL", [OWN + 4 * 3072], bf), ("W2", [P0 + 8192], bf), ("XW", [2064], bf),
    ("XG", [3072], bf), ("OG", [3072], bf), ("BG", [4096], bf), ("SRC", [4096], bf),
    ("SGA", [16, WM], bf), ("SGB", [16, WM], bf), ("SA0", [8, WM], bf), ("SA1", [8, WM], bf), ("IH", [128], hf), ("NIH", [128], hf),
    ("SB0", [8, WM], hf), ("SC0", [8, WM], hf), ("SD0", [4, WM], hf), ("SB1", [8, WM], hf), ("SC1", [8, WM], hf), ("SD1", [4, WM], hf),
    ("CT", [512], i4), ("TV", [1024], i4), ("TI", [1024], i4), ("SO", [1280], i4), ("DUMP2", [256], i4), ("TRL", [768], i4),
    ("TA", [768], bf), ("TZ", [768], bf), ("DD", [768], bf), ("VC", [1280], f4), ("VL", [1280], bf), ("TR0", [448], u2),
    ("IDS", [1280], f4), ("LW", [2176], f4), ("LWB", [256], bf), ("LOC", [832], bf), ("LS0", [192], bf), ("LS", [192], bf),
    ("S", [2048], bf), ("ZC", [144], bf), ("SEL", [480], bf), ("PERM", [384], bf), ("ONE", [144], bf),
    ("I", [128], bf), ("NI", [128], bf), ("ONES", [128], bf), ("ONES16", [128], bf), ("ONESB", [128], bf),
    ("I15", [128], bf), ("NI15", [128], bf), ("IQ", [128], bf), ("IPM", [128], bf), ("SCL", [128], bf),
    ("TRI", [128], bf), ("RK", [128], bf), ("M1", [128], bf), ("M2", [128], bf), ("OP32", [128], bf), ("OM32", [128], bf),
    ("TM1", [128], bf), ("TM2", [128], bf),
    ("KI", [8], i4), ("KC", [8], f4), ("KT", [16], f4), ("MK", [16], f4), ("I16", [16], f4), ("BC", [4], f4), ("DUMP", [64], f4), ("ONEF", [64], f4),
    ("XS", [4 * 768], bf), ("BS", [4 * 768], bf),
    ("FC", [32], bf), ("AC", [32], bf), ("FT", [64], bf), ("AT", [64], bf), ("SCN", [64], f4), ("RP", [64], f4), ("RO", [64], f4),
    ("OFU", [64], u2), ("CL", [16], u2), ("TL", [16], u2), ("OOU", [192], u2), ("TRU", [192], u2),
    ("DE", [192], bf), ("U", [256], bf), ("FX", [256], bf), ("PM", [256], bf), ("FIT", [192], bf), ("MR", [192], bf), ("KL", [192], bf), ("KV", [256], f4),
    ("A0", [192], bf), ("B0", [192], bf), ("ABT", [384], bf), ("CI", [128], i4), ("CJ", [8, 32], i4), ("FF", [8, 32], bf),
    ("VCU", [256], u2), ("SOU", [256], u2), ("ADU", [256], u2), ("VCF", [256], f4), ("VLG", [256], bf), ("OX", [256], bf),
    ("EM", [256], bf), ("NH", [256], bf), ("X1", [256], bf), ("X0", [256], bf), ("XQ", [256], bf),
    ("NE", [256], bf), ("AM", [256], bf), ("SN", [256], bf), ("VA", [256], bf),
    ("AB", [512], bf), ("DS", [128], bf), ("ASU", [128], u2), ("YF", [1024], f4),
]:
    SCRATCH[_n] = ("sbuf", [128] + _s, _d)
SCRATCH["PA"] = ("psum", [128, 8, 128], f4)
SCRATCH["PB"] = ("psum", [128, 8, 128], f4)
BANKS = ("E0", "E1", "E2", "E3")
for _n in BANKS:
    SCRATCH[_n] = ("psum", [128, 512], f4)
NDMA = 12
SEMAPHORES = ["cv", "ca", "cp", "cg", "sent"] + ["xa%d" % u for u in range(4)] + ["ba%d" % u for u in range(4)] + ["d%d" % j for j in range(NDMA)]
QSEM = {"v": "cv", "a": "ca", "p": "cp", "g": "cg"}
LAT, GAT, SCA, PEC = 110.0, 1.56, 3.8, 0.5


def meta(n):
    return ("psum", [128, 512], f4) if n[0] == "#" else SCRATCH[n]


def R(name, *idx, p=None):
    return ("ref", name, tuple(slice(x[0], x[1], x[2] if len(x) > 2 else None) if isinstance(x, tuple) else x for x in idx), p)


def IND(win, off):
    return ("ind", win, off)


def spans(r):
    shp = meta(r[1])[1][1:]
    idx = list(r[2]) + [slice(None)] * (len(shp) - len(r[2]))
    rg = [range(*x.indices(n)) if isinstance(x, slice) else range(x, x + 1) for x, n in zip(idx, shp)]
    if len(shp) == 1:
        return [(rg[0][0], rg[0][-1] + 1)], len(rg[0])
    return [(a * shp[1] + rg[1][0], a * shp[1] + rg[1][-1] + 1) for a in rg[0]], len(rg[0]) * len(rg[1])


def is_ref(x):
    return isinstance(x, tuple) and len(x) > 0 and x[0] in ("ref", "ind")


def build():
    ops, acc, banks, ndma, uses, lab = [], {}, {}, [0], [0], ["start", 0]

    def add(q, calls, reads, writes, cost, kind="c", extra=(), lat=0.0, sem=None):
        me = len(ops)
        deps = {}
        for e in extra:
            deps[e] = True
        touched = set()
        for refs, wr in ((reads, False), (writes, True)):
            for r in refs:
                if r[1] not in SCRATCH and r[1][0] != "#":
                    continue
                lst = acc.setdefault(r[1], [])
                for lo, hi in spans(r)[0]:
                    for (a, b, o, w) in lst:
                        if a < hi and lo < b and o != me and (w or wr):
                            need = ops[o]["q"] != q or ops[o]["kind"] != "c" or kind != "c" or (w and not wr) or q != "p"
                            deps[o] = deps.get(o, False) or need
                    if wr:
                        lst[:] = [t for t in lst if not (lo <= t[0] and t[1] <= hi)]
                    lst.append((lo, hi, me, wr))
                    if meta(r[1])[0] == "psum":
                        for bk in range(lo // 512, (hi - 1) // 512 + 1):
                            touched.add((r[1], bk))
        for bk in touched:
            st = banks.setdefault(bk, [q, [], []])
            if st[0] != q:
                st[0], st[1], st[2] = q, [], st[1]
            for o in st[2]:
                deps[o] = True
            st[1].append(me)
        ops.append({"q": q, "calls": calls, "deps": deps, "cost": cost, "kind": kind, "lat": lat, "sem": sem, "tag": lab[0] + str(q), "rd": lab[1],
                    "use": max([b[0] for b in touched if b[0][0] == "#"] or [""])})
        return me

    def parts(out, ins):
        rd, wr = [], []
        for x in ins:
            if is_ref(x):
                rd += [x[1], x[2]] if x[0] == "ind" else [x]
        if out[0] == "ind":
            wr.append(out[1]); rd.append(out[2])
        else:
            wr.append(out)
        return rd, wr

    def vec(meth, out, *args):
        rd, wr = parts(out, args)
        full = [x for x in (out,) + args if is_ref(x) and x[0] == "ref" and spans(x)[1] > 1] or [out]
        n = max(spans(x)[1] for x in full)
        f = 0.5 if all(meta(x[1])[2] in (bf, u2, hf) for x in full) else 1.0
        if meth == "tensor_tensor":
            f = 1.0 if any(meta(x[1])[0] == "psum" for x in args[:2] if x[0] == "ref") else 2.0
        if out[0] == "ind":
            f = SCA
        elif any(is_ref(x) and x[0] == "ind" for x in args):
            f = GAT
        return add("v", [(meth, (out,) + args, {})], rd, wr, 60 + n * f)

    def tt(out, a, b, op): return vec("tensor_tensor", out, a, b, op)
    def ts(out, a, s1, o1, s2=None, o2=None):
        return vec("tensor_scalar", out, a, s1, s2, o1) if o2 is None else vec("tensor_scalar", out, a, s1, s2, o1, o2)
    def cp(out, a): return vec("tensor_copy", out, a)
    def ms(out, c): return vec("memset", out, c)

    def act(out, a, func=F.Identity, bias=0.0, scale=1.0):
        rd, wr = parts(out, (a, bias, scale))
        if out[0] == "ind":
            return add("a", [("activation", (out, a, func), {})], rd, wr, 90 + spans(a)[1] * SCA)
        return add("a", [("activation", (out, a, func), {"bias": bias, "scale": scale})], rd, wr,
                   90 + spans(out)[1] * (GAT if a[0] == "ind" else 1.0))

    def move(q, out, a): return cp(out, a) if q == "v" else act(out, a)

    def nb():
        uses[0] += 1
        return "#%d" % uses[0]

    def mm(groups, go_on=False, close=True):
        calls, rd, wr, cost = [], [], [], 40.0
        for gr in groups:
            for j, (o, l, r) in enumerate(gr):
                calls.append(("matmul", (o, l, r, j == 0 and not go_on, j == len(gr) - 1 and close), {}))
                rd += [l, r]; wr.append(o)
                cost += PEC * max(min(64, spans(l)[1]), spans(r)[1])
        return add("p", calls, rd, wr, cost)

    def gp(meth, out, *args, **kw):
        rd, wr = parts(out, args)
        return add("g", [(meth, (out,) + args, kw)], rd, wr, 200 + 2 * spans(out)[1])

    def iota(out, pat, base=0, cm=0):
        if SCRATCH[out[1]][2] == i4:
            return gp("iota", out, pat, base, cm)
        return gp("iota", out, pat, base, cm, allow_small_or_imprecise_dtypes=True)

    def fill(out, c): return iota(out, [[0, spans(out)[1]]], c)

    def asel(out, a, pat, op, base, cm=1): return gp("affine_select", out, a, pat, op, 0.0, base, cm)

    def dma(q, out, a, nbytes):
        j = ndma[0]; ndma[0] += 1
        return add(q, [("dma_start", (out, a), {})], [a], [out], 80.0, kind="d", lat=2400 + nbytes / 150.0, sem=("d%d" % j, 16))

    def send(src, u, dst, d0, sem, extra=()):
        s = add("g", [("send", (src, u, dst, d0, sem), {})], [R(src, (768 * u, 768 * u + 768))], [], 1200.0, kind="s", extra=extra, lat=4000.0)
        return add(None, [], [], [R(dst, (d0, d0 + 768))], 0.0, kind="r", extra=(s,), sem=(sem, 8))

    I, NI, ONES, I15, NI15 = R("I"), R("NI"), R("ONES"), R("I15"), R("NI15")
    def C(k): return R("ZC", (15 - k, 143 - k))
    def S(k): return R("S", (128 * k, 128 * k + 128))
    def col(name, j): return R(name, (j, j + 1))

    def turn(src, s0, dst, u):
        for bk, ds in ((nb(), (0, 1)), (nb(), (2,))):
            mm([[(R(bk, (256 * j, 256 * j + 256)), R("PERM", (128 * d, 128 * d + 128)), R(src, (s0 + 256 * d, s0 + 256 * d + 256)))] for j, d in enumerate(ds)])
            act(R(dst, (768 * u + 256 * ds[0], 768 * u + 256 * ds[-1] + 256)), R(bk, (0, 256 * len(ds))))

    dma("s", R("XW", (256, 1280)), R("x0"), 262144)
    dma("a", R("CT"), R("ct"), 262144)
    dma("s", R("OB", (0, 3072)), R("obs", (0, 3072)), 1310720)
    dma("a", R("TV"), R("tv"), 1835008)
    dma("s", R("OB", (3072, 8192)), R("obs", (3072, 8192)), 3145728)
    ms(R("ONE"), 1.0)
    one = R("ONE", (0, 128))
    asel(R("PERM", (0, 128)), one, [[-32, 4], [16, 2], [-1, 16]], A.is_equal, -16)
    asel(R("PERM", (128, 256)), one, [[-64, 2], [32, 2], [-1, 32]], A.is_equal, -32)
    asel(R("PERM", (256, 384)), one, [[-64, 2], [16, 4], [-1, 16]], A.is_equal, -48)
    turn("XW", 256, "XS", 0)
    send("XS", 0, "XW", 1280, "xa0")
    asel(I, one, [[-1, 128]], A.is_equal, 0)
    asel(R("IPM"), one, [[-8, 2], [-16, 8], [-1, 8]], A.is_equal, 0)
    asel(R("TM1"), one, [[-16, 8], [0, 16]], A.is_ge, 0)
    asel(ONES, R("TM1"), [[16, 8], [0, 16]], A.is_ge, 15, -1)
    asel(R("TRI"), ONES, [[1, 128]], A.is_ge, 0, -1)
    iota(R("KI", (0, 1)), [[0, 1]], 0, 1)
    iota(R("I16"), [[1, 16]])
    ts(R("KI", (4, 5)), R("KI", (0, 1)), 15, A.bitwise_and)
    cp(col("KC", 0), R("KI", (4, 5)))
    ts(R("MK"), R("I16"), col("KC", 0), A.is_equal)
    ts(col("KC", 1), col("KC", 0), -4352.0, A.add)
    ts(col("KC", 2), col("KC", 0), 64.0, A.mult, -784.0, A.add)
    ts(col("KC", 3), col("MK", 2), float(OWN), A.mult)
    ts(R("BC"), R("I16", (0, 4)), 3072.0, A.mult)
    ts(R("BC"), R("BC"), col("MK", 3), A.mult, col("KC", 3), A.add)
    modes = sorted(set(FIT1 + FIT2))
    for j, m in enumerate(modes):
        ms(col("KT", 2 * j), 11.5)
        for k in range(16):
            if m[k // 4] == "b" and len(set(m)) > 1:
                ts(col("KT", 2 * j), col("MK", k), -4.5, A.mult, col("KT", 2 * j), A.add)
        if len(set(m)) > 1:
            ts(col("KT", 2 * j + 1), col("KT", 2 * j), -1.0, A.mult)

    def bound(m, neg):
        if "b" in m and len(set(m)) > 1:
            return col("KT", 2 * modes.index(m) + neg)
        return (7.0 if "b" in m else 11.5) * (-1.0 if neg else 1.0)
    ms(R("ZC"), 0.0)
    cp(R("ZC", (15, 143, 16)), R("ONES", (0, 128, 16)))
    for k in range(16):
        act(S(k), ONES, F.Identity, 0.0, col("MK", k))
    ts(NI, I, -1.0, A.mult)
    cp(R("IH"), I); ts(R("NIH"), I, -1.0, A.mult)
    ts(I15, I, 1.5, A.mult); ts(NI15, I, -1.5, A.mult); ts(R("IQ"), I, 1.0 / 32, A.mult)
    ts(R("TM1"), R("TRI"), 2.0, A.mult)
    tt(R("TM1"), R("TM1"), ONES, A.subtract)
    ts(R("TM2"), I, -64.0, A.mult)
    tt(R("M1"), R("TM2"), R("TM1"), A.add)
    tt(R("M2"), R("TM2"), R("TM1"), A.subtract)
    ts(R("TM2"), I, 32.0, A.mult)
    tt(R("OP32"), ONES, R("TM2"), A.add)
    tt(R("OM32"), ONES, R("TM2"), A.subtract)
    ts(R("TM2"), I, -4096.0, A.mult)
    tt(R("TM1"), R("TRI"), ONES, A.subtract)
    tt(R("RK"), R("TM1"), R("TM2"), A.add)
    act(R("ONES16"), ONES, F.Identity, 0.0, 16.0)
    act(R("ONESB"), ONES, F.Identity, 0.0, 2.0 ** 34)
    fill(R("SEL"), 0)
    for h in range(2):
        asel(R("SEL", (240 * h + 112, 240 * h + 128), p=(0, 32)), R("ONE", (0, 16), p=(0, 32)), [[-1, 16]], A.is_equal, -16 * h)
    ms(R("ONEF"), 1.0)
    iota(R("DUMP"), [[16, 64]], 1024, 1)
    iota(R("DUMP2"), [[16, 256]], DB, 1)
    ts(R("TRL", (256, 768)), R("CT"), 4, A.logical_shift_right)
    cp(R("TR0", (0, 192)), R("TRL", (256, 448)))
    cp(R("TR0", (192, 448)), R("TRL", (448, 704)))
    ts(R("TI", (512, 1024)), R("CT"), 4, A.logical_shift_right, 31, A.bitwise_and)
    cp(R("TA", (256, 768)), R("TI", (512, 1024)))
    ts(R("TI", (0, 512)), R("CT"), 16384.0, A.add)
    ts(R("TI", (0, 512)), R("TI", (0, 512)), 9, A.logical_shift_right, 63, A.bitwise_and)
    cp(R("AB"), R("TI", (0, 512)))
    act(R("TZ", (256, 768)), R("AB"), F.Exp, -334.0 * LN2, 7.0 * LN2)
    iota(R("VCF", (0, 128)), [[0, 8], [-14, 16]], 110)
    act(R("SCL"), R("VCF", (0, 128)), F.Exp, 0.0, LN2)
    fill(R("TRL", (0, 256)), XN); fill(R("TA", (0, 256)), 0); fill(R("TZ", (0, 256)), 0); ms(R("DD"), 0.0)
    fill(R("XW", (0, 256)), 512); fill(R("XW", (2048, 2064)), 512)
    fill(R("POOL", (0, 16)), 2048); fill(R("POOL", (784, 800)), 2048)
    fill(R("LOC"), -1024)
    iota(R("LOC", (768, 816)), [[1, 48]], 1)
    iota(R("BG", (0, 1280)), [[16, 80], [0, 16]])
    iota(R("BG", (1280, 2560)), [[0, 80], [1, 16]], 16)
    iota(R("BG", (2560, 2752)), [[1024, 3], [0, 64]])
    iota(R("BG", (2752, 2944)), [[0, 3], [1, 64]])
    for a, n in ((0, 512), (512, 512), (1024, 256)):
        e = R(nb(), (0, n))
        mm([[(e, C(0), R("BG", (a, a + n))), (e, C(1), R("BG", (1280 + a, 1280 + a + n)))]])
        act(R("IDS", (a, a + n)), e, F.Identity, 0.0, 0.0625)
    e = R(nb(), (0, 192))
    mm([[(e, C(0), R("BG", (2560, 2752))), (e, C(1), R("BG", (2752, 2944)))]])
    act(R("LS0"), e, F.Identity, 0.0, 0.0625)
    lab[0] = "views"
    for j in range(2):
        e, v, t = R(nb()), R("TV", (512 * j, 512 * j + 512)), (256 + 512 * j, 768 + 512 * j)
        ti = R("TI", (512 * j, 512 * j + 512))
        ts(e, v, 8192.0, A.is_lt, 63.0, A.mult)
        act(R("AB"), e, F.Identity, 1.0)
        ts(ti, v, 15, A.bitwise_and)
        tt(R("VL", t), ti, R("AB"), A.mult)
        ts(ti, v, 8192.0, A.add)
        ts(R("SO", t), ti, 16383, A.bitwise_and)
        ts(ti, v, 4, A.logical_shift_right)
        ts(R("VC", t), ti, 256.0, A.add)
    fill(R("VC", (0, 256)), VE); fill(R("VL", (0, 256)), 0); fill(R("SO", (0, 256)), 0)
    lab[0] = "zero"
    for j in range(8):
        fill(R("W2", (P0 + 1024 * j, P0 + 1024 * j + 1024)), 0)
    lab[0] = "start"
    ms(R("FC"), 1.0); ms(R("AC", (0, 12)), 0.0); ms(R("AC", (12, 32)), 1.0)

    def worklist(fl, al, n, segs, K, out, fixed=None, turned=False):
        c0, c1 = min(s[0] for s in segs), max(s[1] for s in segs)
        w = (c0, c1)
        act(R("LW", (0, K)), R("IDS", (0, K)))
        if fixed:
            ms(R("SCN", fixed), 8000.0)
        b = nb()
        mm([[(R(b, w), ONES, R(fl, w))], [(R(b, (64 + c0, 64 + c1)), R("RK"), R(fl, w))]])
        for j, s in enumerate(segs):
            vec("tensor_tensor_scan", R("SCN", s), R("ONEF", s), R(b, s), col("SCN", segs[j - 1][1] - 1) if j and not turned else 4095.0, A.mult, A.add)
        tt(R("RP", w), R(b, (64 + c0, 64 + c1)), R("SCN", w), A.add)
        if turned:
            s, t = segs
            ts(col("KC", 4), col("SCN", s[1] - 1), -1.0, A.mult, K + 4094.5, A.add)
            ts(R("RO", s), R("RP", s), col("KC", 4), A.add, 0.5, A.add)
            tt(R("RO", s), R("RO", s), R("DUMP", s), A.min)
            tt(R("RO", t), R("RP", t), R("DUMP", t), A.min)
            cp(R("OFU", w), R("RO", w))
            ts(R(al, s), R("RP", s), K - 0.5, A.is_ge)
            ts(R(al, t), R("RP", t), col("KC", 4), A.is_ge)
            segs = segs[::-1]
        else:
            tt(R("RO", w), R("RP", w), R("DUMP", w), A.min)
            cp(R("OFU", w), R("RO", w))
            ts(R(al, w), R("RP", w), K - 0.5, A.is_ge)
            segs = sorted(segs)
            segs = [segs[0]] + segs[1:] if fixed else [w]
        if fixed:
            ms(R(al, fixed), 0.0)
        for s in segs:
            for c in range(s[0], s[1], 32):
                d = min(c + 32, s[1])
                act(IND(R("LW"), R("OFU", (c, d))), R("IDS", (256 + 16 * c, 256 + 16 * d)), F.Silu)
        m = K // 16
        act(R("LWB", (0, K)), R("LW", (0, K)))
        e = R(nb(), (0, m))
        mm([[(e, C(k), R("LWB", (k, K, 16))) for k in range(16)]])
        ts(R(out, (0, m)), e, -16.0, A.add)

    def median(P, SA, W, out, level, hist):
        def q(nm):
            return lambda a, b=None, s=None: R(nm, (a, a + 1 if b is None else b, s), (0, W))
        z = SA[2]
        p, a_, b_, c_, d_ = q(P), q(SA), q("SB" + z), q("SC" + z), q("SD" + z)
        lo, hi = A.min, A.max
        if level:
            def other(s0):
                mm([[(R(P, s, (0, W)), l, r) for l, r in hist[s] + [(I, R(SA, s, (0, W))), (R("NIH"), R("SB" + z, s, (0, W)))]] for s in range(s0, s0 + 4)])
            tt(b_(0, 4), p(0, 4), a_(0, 4), lo); other(0)
            tt(b_(4, 8), p(4, 8), a_(4, 8), hi); other(4)
        else:
            tt(b_(0, 4), p(0, 4), a_(0, 4), lo); tt(b_(4, 8), p(4, 8), a_(4, 8), hi)
            tt(p(0, 4), p(0, 4), a_(0, 4), hi); tt(p(4, 8), p(4, 8), a_(4, 8), lo)
        net = [
            (d_(0, 2), p(0, 2), b_(4, 6), lo), (c_(0, 2), p(2, 4), b_(6, 8), hi), (c_(6, 8), p(4, 6), b_(0, 2), lo), (d_(2, 4), p(6, 8), b_(2, 4), hi),
            (p(4, 6), p(4, 6), b_(0, 2), hi), (p(0, 2), p(0, 2), b_(4, 6), hi), (p(2, 4), p(2, 4), b_(6, 8), lo), (p(6, 8), p(6, 8), b_(2, 4), lo),
            (c_(2, 4), p(4, 6), d_(0, 2), lo), (c_(4, 6), p(2, 4), d_(2, 4), hi), (p(4, 6), p(4, 6), d_(0, 2), hi), (p(2, 4), p(2, 4), d_(2, 4), lo),
            (b_(0, 8, 2), p(0, 8, 2), c_(0, 8, 2), lo), (b_(1, 8, 2), p(1, 8, 2), c_(1, 8, 2), hi),
            (p(0, 8, 2), p(0, 8, 2), c_(0, 8, 2), hi), (p(1, 8, 2), p(1, 8, 2), c_(1, 8, 2), lo),
            (c_(2, 4), p(1, 8, 4), b_(0, 8, 4), lo), (d_(0, 4), p(0, 8, 2), b_(1, 8, 2), lo),
            (p(1, 8, 2), p(1, 8, 2), b_(0, 8, 2), hi), (p(2, 8, 4), p(2, 8, 4), b_(3, 8, 4), hi),
            (c_(0, 2), p(3, 8, 4), d_(1, 4, 2), hi), (p(0, 8, 4), p(1, 8, 4), d_(0, 3, 2), lo), (p(3), p(3), d_(1), lo),
            (b_(0), p(6), c_(0), hi), (b_(1), p(6), c_(0), lo), (b_(2, 4), p(0, 4, 2), c_(1, 4, 2), lo),
            (p(5), p(4), c_(2), lo), (p(7), p(4), c_(2), hi), (b_(2), p(3), b_(2), hi),
            (p(5, 8, 2), p(5, 8, 2), b_(0, 2), lo), (b_(4), p(5), b_(2), hi), (p(7), p(7), b_(3), hi), (out, p(7), b_(4), hi)]
        for o, x, y, f in net:
            tt(o, x, y, f)

    def stage(P, SA, w0, W, terms, src, first, dead):
        g, z, u, x = R(nb(), (0, W)), R(nb(), (0, W)), R("U", (w0, w0 + W)), R("FX", (w0, w0 + W))
        if dead:
            mm([[(g, C(k), src(k)) for k in range(16)]], False, False)
            mm([[(g, NI, dead)]], True)
        else:
            mm([[(g, C(k), src(k)) for k in range(16)]])
        if first:
            ts(u, g, 6000.0, A.is_ge, 1024.0, A.mult)
            mm([[(z, R("M1"), u)]])
            if dead:
                ts(z, z, -63.5 * 1024, A.is_le, -2048.0, A.mult)
                tt(x, z, u, A.add)
            else:
                ts(x, z, -63.5 * 1024, A.is_le, -1024.0, A.mult)
        else:
            ts(u, g, 16000.0, A.is_ge, 32.0, A.mult)
            mm([[(z, R("M2"), u)]])
            ts(x, z, -64.5 * 32, A.is_le, 4096.0, A.mult)
        for h in (1, 0):
            bk = nb()
            mm([[(R(bk, (j * W, j * W + W)), l, r) for l, r in terms(8 + 4 * h + j) + [(S(8 + 4 * h + j), x)]] for j in range(4)])
            act(R(SA, (4 * h, 4 * h + 4), (0, W)), R(bk, (0, 4 * W)))
            mm([[(R(P, 4 * h + j, (0, W)), l, r) for l, r in terms(4 * h + j) + [(S(4 * h + j), x)]] for j in range(4)])

    def fits(W, terms, mode):
        for j in range(4):
            b = nb()
            mm([[(R(b, (i * W, i * W + W)), l, r) for l, r in terms(4 * j + i)] for i in range(4)])
            e = R(b, (0, 4 * W))
            sa, sb = R("SGA", (4 * j, 4 * j + 4), (0, W)), R("SGB", (4 * j, 4 * j + 4), (0, W))
            if mode[j] == "v":
                ts(sb, e, MAGIC, A.add, MAGIC, A.is_equal)
            else:
                act(sa, e, F.Abs)
                if mode[j] == "a":
                    ts(sb, sa, 15.75, A.is_le)
                else:
                    act(sb, sa, F.Sign, 15.75, -1.0)
        return [(C(k), R("SGB", k, (0, W))) for k in range(16)]

    def total(e, tm, split):
        h = len(tm) - 4 if split else len(tm)
        mm([[(e, l, r) for l, r in tm[:h]]], False, not split)
        if split:
            mm([[(e, l, r) for l, r in tm[h:]]], True)

    def places(c0, n):
        e = R(nb(), (0, n))
        mm([[(e, ONES, R("LOC", (256 + c0, 256 + c0 + n))), (e, I, R("DD", (256 + c0, 256 + c0 + n)))]])
        ts(R("ASU", (0, n)), e, col("KC", 2), A.add, 0.0, A.max)

    par = [0]
    for u in range(4):
        lab[:] = ["list", u]
        ch, p0 = [], 0
        for c0, l0, W in CH1[u]:
            ch.append((c0, l0, W, p0)); p0 += W
        nch = len(ch)
        K = sum(W for c0, l0, W, p0 in ch if c0 is None)
        act(R("LS"), R("LS0"), F.Identity, col("BC", u))
        if u == 1:
            ms(R("AC", (0, 8)), 1.0)
            worklist("FC", "AC", 32, [(8, 12), (20, 24)], K, "CL", (12, 20))
        elif u == 2:
            worklist("FC", "AC", 32, [(16, 24), (28, 32), (0, 16)], K, "CL", (24, 28))
        elif u == 3:
            worklist("FC", "AC", 32, [(24, 32), (0, 24)], K, "CL", None, True)
        src1, xg = [], []
        for n, (c0, l0, W, p0) in enumerate(ch):
            w = (p0, p0 + W)
            if c0 is None:
                lab[0] = "more"
                cl = R("CL", (l0 // 16, (l0 + W) // 16))
                cp(R("TRU", w), IND(R("TRL"), cl))
                e = R(nb(), (0, W))
                mm([[(e, R("ONES16"), R("LWB", (l0, l0 + W)))]])
                ts(R("OOU", w), e, col("KC", 1), A.add, 0.0, A.max)
                act(R("DE", w), IND(R("DD"), cl))
                act(R("A0", w), IND(R("TA"), cl)); act(R("B0", w), IND(R("TZ"), cl))
                cp(IND(R("LOC"), cl), R("LS", w))
                src1.append((("TRU", p0), ("OG", 16 * p0), R("DE", w), cl))
            else:
                lab[0] = "fixed"
                act(R("LOC", (256 + c0, 256 + c0 + W)), R("LS", w))
                src1.append((("TR0", c0), ("OB", 16 * c0), R("DD", (256 + c0, 256 + c0 + W)) if u else None, None))
            lab[0] = "x%d" % n
            for h in range(2):
                a, b = h * W // 2, (h + 1) * W // 2
                tr = src1[n][0]
                xg.append(move(GX[n > 0][h], R("XG", (16 * (p0 + a), 16 * (p0 + b))), IND(R("XW", (256, 2064)), R(tr[0], (tr[1] + a, tr[1] + b)))))
                if c0 is None:
                    act(R("OG", (16 * (p0 + a), 16 * (p0 + b))), IND(R("OB"), R("OOU", (p0 + a, p0 + b))))

        def onehot():
            b1, b2, b3, few = nb(), nb(), nb(), (0, 32)
            lab[0] = "hot"
            big, small = [[("T", 256), ("T", 384)], [("T", 448), ("", 128)], [("", 64), ("T", 640)], [("", 0), ("", 128)]][u]
            gr = []
            for j, (t, d) in enumerate((("TA", "A0"), ("TZ", "B0"))):
                gr.append([(R(b1, (192 * j, 192 * j + 128)), R(t if big[0] else d, (big[1], big[1] + 128)), I)])
                for h in range(2):
                    gr.append([(R(b1, (192 * j + 128, 192 * j + 192), p=(64 * h, 64 * h + 64)), R(t if small[0] else d, (small[1], small[1] + 64)),
                                R("IPM", (64 * h, 64 * h + 64)))])
            mm(gr)
            act(R("ABT"), R(b1, (0, 384)))
            for a in range(32):
                ts(R("W2", (OAB + 192 * a, OAB + 192 * a + 192)), R("ABT", (0, 192)), float(a), A.is_equal)
            for n in range(16):
                o, z = R("W2", (OBB + 192 * n, OBB + 192 * n + 192)), R("ABT", (192, 384))
                if n < 15:
                    ts(o, z, 2.0 ** (14 * n - 98), A.min)
                else:
                    cp(o, z)
            lab[0] = "flag"
            for g in range(8):
                mm([[(R(b2, (16 * g, 16 * g + 16), p=few), R("W2", (OAB + x, OBB, 192)), R("W2", (OBB + x, P0, 192)))
                     for x in list(range(16 * g, 16 * g + 16)) + list(range(128 + 8 * g, 136 + 8 * g))]])
            tt(R("CI", p=few), R(b2, (0, 128), p=few), R("SCL", p=few), A.mult)
            ts(R("CJ", (0, 8), (0, 32, 2), p=few), R("CI", p=few), 31, A.bitwise_and)
            ts(R("CJ", (0, 8), (1, 32, 2), p=few), R("CI", p=few), 31 * 128, A.bitwise_and)
            cp(R("FF", p=few), R("CJ", p=few))
            e = R(b3, (0, 64))
            gr = [(e, I, R("AT")), (e, I, R("FT"))] if u else [(e, R("SEL", (128, 256), p=few), R("ONE", (0, 64), p=few))]
            gr += [(R(b3, (h, 64, 2)), R("SEL", (240 * h + 112 - 16 * g, 240 * h + 240 - 16 * g), p=few), R("FF", g, p=few)) for g in range(8) for h in range(2)]
            mm([gr])
            ts(R("FT"), e, 1.75 if u else 0.5, A.is_ge)
            worklist("FT", "AT", 64, [(12 * u, 64), (0, 12 * u)] if u else [(0, 64)], 256, "TL")
            tl = R("TL")
            cp(R("VCU"), IND(R("VC"), tl)); act(R("VLG"), IND(R("VL"), tl))
            lab[0] = "late"
            tt(R("TI", (0, 256)), IND(R("SO"), tl), R("DUMP2"), A.max)
            ts(R("SOU"), R("TI", (0, 256)), -float(DB), A.add)
            act(R("VCF"), IND(R("VC"), tl)); act(R("OX"), IND(R("XW", (0, 1280)), tl))
            ts(R("EM"), R("VCF"), VE - 0.5, A.is_ge, -2.0 ** 50, A.mult)
            for j, w0 in enumerate(range(0, 256, 64)):
                lab[0] = "loc%d" % j
                move(GL[j], R("SRC", (16 * w0, 16 * w0 + 1024)), IND(R("LOC"), R("VCU", (w0, w0 + 64))))
                e = R(nb(), (0, 64))
                mm([[(e, C(k), R("SRC", (16 * w0 + k, 16 * w0 + 1024, 16))) for k in range(16)] + [(e, I, R("VLG", (w0, w0 + 64)))]])
                ts(R("ADU", (w0, w0 + 64)), e, 0.0, A.max)

        def send_b(done):
            lab[0] = "send"
            places(0, 48)
            act(R("BG", (0, 768)), IND(R("POOL", (784, OWN + 3072 * u + 16 * done)), R("ASU", (0, 48))))
            turn("BG", 0, "BS", u)
            send("BS", u, "POOL", 16, "ba%d" % u, extra=xg)

        def xk(n, k, a=0, b=None):
            W, p0 = ch[n][2:]
            return R("XG", (16 * (p0 + a) + k, 16 * (p0 + (b or W)), 16))

        def ok(n, k, a=0, b=None):
            o = src1[n][1]
            return R(o[0], (o[1] + 16 * a + k, o[1] + 16 * (b or ch[n][2]), 16))

        def pre1(n):
            W, p0 = ch[n][2:]; pr = (par[0] + n) % 2; lab[0] = "pre1%d" % n
            stage("PB" if pr else "PA", "SA%d" % pr, p0, W, lambda k: [(I, xk(n, k)), (NI, ok(n, k))], lambda k: xk(n, k), True, src1[n][2])

        def post1(n):
            c0, l0, W, p0 = ch[n]; w = (p0, p0 + W); last = n == nch - 1; lab[0] = "fit1%d" % n
            pm, uu, ft, mk, sa = R("PM", w), R("U", w), R("FIT", w), R("MR", w), "SA%d" % ((par[0] + n) % 2)
            dead = src1[n][2]
            tm = fits(W, lambda k: ([(I15, xk(n, k)), (NI15, ok(n, k))] if k < 8 else [(I15, R(sa, k - 8, (0, W)))]) + [(NI15, pm)], FIT1[last])
            e = R(nb(), (0, W))
            total(e, [(NI, uu)] + tm, last)
            ts(ft, e, bound(FIT1[last], 0), A.is_ge)
            b = nb(); e, e2 = R(b, (0, W)), R(b, (128, 128 + W))
            mm([[(e, R("OP32"), ft), (e, R("IQ"), uu)] + ([(e, I, dead)] if dead else []), [(e2, R("OM32"), ft), (e2, NI, uu)]])
            ts(mk, e, 37.5, A.is_lt, 2048.0, A.mult)
            ts(R("KL", w), e2, 5.5, A.is_ge, -DEAD, A.mult)
            lab[0] = "pool%d" % n
            for a in range(0, W, 64):
                base = OWN + 3072 * u + 16 * (p0 + a)
                for j in range(2):
                    b = nb()
                    mm([[(R(b, (i * 64, i * 64 + 64)), l, r) for l, r in ((NI, ok(n, 8 * j + i, a, a + 64)), (NI, R("PM", (p0 + a, p0 + a + 64))),
                                                                          (S(8 * j + i), R("MR", (p0 + a, p0 + a + 64))))] for i in range(8)])
                    o = R("POOL", (base + 512 * j, base + 512 * j + 512))
                    if POOLQ[last][j] == "v":
                        ts(o, R(b), 255.0, A.add, 0.0, A.max)
                    else:
                        act(o, R(b), F.Relu, 255.0)
            lab[0] = "kill%d" % n
            if c0 is None:
                tt(IND(R("DD"), src1[n][3]), dead, R("KL", w), A.add)
            else:
                d = R("DD", (256 + c0, 256 + c0 + W))
                tt(d, d, R("KL", w), A.add)

        pre1(0)
        if SENDB[u] == 0:
            send_b(0)
        for n in range(nch):
            if n + 1 < nch:
                pre1(n + 1)
            pr = (par[0] + n) % 2
            W, p0 = ch[n][2:]
            lab[0] = "med1%d" % n
            median("PB" if pr else "PA", "SA%d" % pr, W, R("PM", (p0, p0 + W)), AS1[n > 0],
                   [[(I, xk(n, k)), (NI, ok(n, k)), (S(k), R("FX", (p0, p0 + W)))] for k in range(8)])
            if n == 0:
                onehot()
            post1(n)
            if SENDB[u] == n + 1:
                send_b(p0 + W)
        par[0] = (par[0] + nch) % 2

        win = R("POOL", (0, OWN + 3072 * (u + 1)))
        st2 = [sum(CH2[:n]) for n in range(len(CH2))]
        for n, W in enumerate(CH2):
            for h in range(2):
                a, b = st2[n] + h * W // 2, st2[n] + (h + 1) * W // 2; lab[0] = "b%d" % n
                move(GB[n > 0][h], R("BG", (16 * a, 16 * b)), IND(win, R("ADU", (a, b))))

        def bk(n, k, name="BG"):
            return R(name, (16 * st2[n] + k, 16 * (st2[n] + CH2[n]), 16))

        def pre2(n):
            W, w0, pr = CH2[n], st2[n], (par[0] + n) % 2; lab[0] = "pre2%d" % n
            stage("PB" if pr else "PA", "SA%d" % pr, w0, W, lambda k: [(NI, bk(n, k))], lambda k: bk(n, k), False, None)
            e = R(nb(), (0, W))
            mm([[(e, ONES, R("U", (w0, w0 + W)))]])
            ts(R("NH", (w0, w0 + W)), e, 13.5 * 32, A.is_ge, 512.0, A.mult)
            lab[0] = "clip%d" % n
            step = 512 if CLIP[n] == "a" else 1024
            for a in range(16 * w0, 16 * (w0 + W), step):
                w = (a, min(a + step, 16 * (w0 + W)))
                if CLIP[n] == "a":
                    act(R("SRC", w), R("BG", w), F.Relu, 255.0, -1.0)
                else:
                    ts(R("SRC", w), R("BG", w), 255.0, A.min)

        lowv, highv = 1024.0 * 64.0 ** u, 32768.0 * 64.0 ** u

        def post2(n):
            W, w0 = CH2[n], st2[n]; lab[0] = "new%d" % n
            w = (w0, w0 + W); last = n == len(CH2) - 1
            pm = R("PM", w)
            act(R("X0", w), pm, F.Relu, 255.0)
            if CLIP[n] == "a":
                tf = lambda k: [(I15, bk(n, k, "SRC")), (NI15, R("X0", w))]
            else:
                ts(R("X1", w), pm, -1.0, A.mult, 255.0, A.min)
                tf = lambda k: [(NI15, bk(n, k, "SRC")), (I15, R("X1", w))]
            tt(R("XQ", w), R("X0", w), R("NH", w), A.max)
            e = R(nb(), (0, W))
            mm([[(e, I, R("XQ", w)), (e, NI, R("OX", w))]])
            act(R("NE", w), e, F.Abs)
            cp(IND(R("XW", (0, 1280)), R("TL", (w0 // 16, w[1] // 16))), R("XQ", w))
            e = R(nb(), (0, W))
            mm([[(e, R("ONESB"), R("NE", w)), (e, I, R("EM", w))]])
            ts(R("AM", w), e, lowv, A.max, highv, A.min)
            lab[0] = "fit2%d" % n
            tm = fits(W, tf, FIT2[last])
            e = R(nb(), (0, W))
            total(e, [(I, R("U", w)), (I, R("NH", w))] + tm, last)
            act(R("SN", w), e, F.Sign, bound(FIT2[last], 1))
            tt(R("VA", w), R("SN", w), R("AM", w), A.mult)
            lab[0] = "back%d" % n
            for j in range(W // 32):
                b = nb(); a = w0 + 32 * j
                mm([[(R(b, (k, 512, 16)), S(k), R("VA", (a, a + 32)))] for k in range(16)])
                act(R("SRC", (16 * a, 16 * a + 512)), R(b))
                cp(IND(R("W2", (P0 + DB - 8192, P0 + 8192)), R("SOU", (a, a + 32))), R("SRC", (16 * a, 16 * a + 512)))
            lab[0] = "empty%d" % n
            act(R("KV", w), R("SN", w), F.Identity, VE / 2.0, -VE / 2.0)
            tt(IND(R("VC"), R("TL", (w0 // 16, w[1] // 16))), R("VCF", w), R("KV", w), A.max)

        pre2(0)
        for n, W in enumerate(CH2):
            if n + 1 < len(CH2):
                pre2(n + 1)
            if u == 3 and n == 0:
                lab[0] = "yb"
                places(384, 128)
                for j in range(4):
                    w = (512 * j, 512 * j + 512)
                    act(R("OB", w), IND(R("POOL", (784, OWN + 4 * 3072)), R("ASU", (32 * j, 32 * j + 32))), F.Identity, 255.0, -1.0)
                for j in range(2):
                    w = (1024 * j, 1024 * j + 1024)
                    ts(R("OG", w), R("OB", w), -600.0, A.is_le, 512.0, A.mult)
            pr = (par[0] + n) % 2
            lab[0] = "med2%d" % n
            median("PB" if pr else "PA", "SA%d" % pr, W, R("PM", (st2[n], st2[n] + W)), AS2[n > 0],
                   [[(NI, bk(n, k)), (S(k), R("FX", (st2[n], st2[n] + W)))] for k in range(8)])
            post2(n)
        par[0] = (par[0] + len(CH2)) % 2
        lab[0] = "turn"
        if u < 3:
            turn("XW", 256, "XS", u + 1)
            send("XS", u + 1, "XW", 1280, "xa%d" % (u + 1))
        pieces = [[(192, 320, 0), (0, 192, 1), (320, 512, 0)], [(384, 448, 0), (0, 384, 1), (448, 512, 0)],
                  [(256, 512, 1), (0, 256, 1)], [(384, 512, 1), (0, 384, 1)]][u]
        for j, (a, b, flags) in enumerate(pieces):
            lab[0] = "end%d" % j
            e = R(nb(), (0, b - a))
            mm([[(e, C(k), R("W2", (P0 + 16 * a + k, P0 + 16 * b, 16))) for k in range(16)]])
            if flags:
                act(R("AB", (a, b)), e, F.Abs, 0.0, 1.0 / (16 * highv))
            if u == 3 and j == 0:
                ts(R("DS"), e, -12.0 * lowv, A.is_le, 512.0, A.mult)
            d = R("DD", (256 + a, 256 + b))
            tt(d, e, d, A.min)
        n = (12, 24, 32, 32)[u]
        lab[0] = "flags"
        e = R(nb(), (0, n))
        mm([[(e, I, R("AC", (0, n))), (e, I, R("FC", (0, n)))] + [(e, C(m), R("AB", (m, 16 * n, 16))) for m in range(16)]])
        ts(R("FC", (0, n)), e, 1.75, A.is_ge)

    lab[0] = "out"
    dma("s", R("yx"), R("XW", (256, 1280)), 262144)
    for j in range(4):
        b, w = nb(), (512 * j, 512 * j + 512)
        mm([[(R(b), I, R("OG", w))] + [(R(b, (k, 512, 16)), S(k), R("DS", (32 * j, 32 * j + 32))) for k in range(16)]])
        tt(R("BG", w), R(b), R("OB", w), A.max)
        if j % 2:
            dma("s", R("yb", (512 * j - 512, 512 * j + 512)), R("BG", (512 * j - 512, 512 * j + 512)), 262144)
    e = R(nb(), (0, 64))
    mm([[(e, I, R("AT")), (e, I, R("FT"))]])
    ts(R("FT"), e, 1.75, A.is_ge, 32.0, A.mult)
    ts(R("XG", (0, 1024)), R("VC", (256, 1280)), VE - 0.5, A.is_lt)
    gi, g8 = R("ONES", (0, 128, 16)), (0, 8)
    def gm(m): return R("S", (128 * m, 128 * m + 128, 16))
    for j in range(2):
        b = nb()
        mm([[(R(b, p=g8), gi, R("XG", (512 * j, 512 * j + 512)))] + [(R(b, (m, 512, 16), p=g8), gm(m), R("FT", (32 * j, 32 * j + 32))) for m in range(16)]])
        act(R("YF", (512 * j, 512 * j + 512), p=g8), R(b, p=g8))
    dma("a", R("yt"), R("YF", p=g8), 32768)
    ts(R("AB"), R("DD", (256, 768)), -0.5, A.is_ge)
    ts(R("AC"), R("FC"), 32.0, A.mult)
    b = nb()
    mm([[(R(b, p=g8), gi, R("AB"))] + [(R(b, (m, 512, 16), p=g8), gm(m), R("AC")) for m in range(16)]])
    act(R("VC", (0, 512), p=g8), R(b, p=g8))
    dma("a", R("yc"), R("VC", (0, 512), p=g8), 16384)
    return ops


def schedule(ops):
    n = len(ops)
    cost = [o["cost"] for o in ops]
    pre = [[(d, (ops[d]["lat"] + LAT) if w else 0.0) for d, w in o["deps"].items()] for o in ops]
    suc = [[] for _ in range(n)]
    unit = {}
    for j in range(n):
        unit.setdefault(ops[j]["use"] or j, []).append(j)
        for d, l in pre[j]:
            suc[d].append((j, l))

    def gap(ln, t, c):
        k = len(ln)
        while k and ln[k - 1][1] > t:
            k -= 1
        while k < len(ln) and t + c > ln[k][0]:
            t = max(t, ln[k][1]); k += 1
        return t, k

    def sweep(key, edges, back):
        st, lanes, bank, left, nxt = [0.0] * n, {b: [] for b in BANKS}, {}, {}, {}
        for u, js in unit.items():
            before = {ops[d]["use"] or d for j in js for d, l in edges[j]} - {u}
            left[u] = len(before)
            for v in before:
                nxt.setdefault(v, []).append(u)
        uk = {u: min(key[j] for j in js) for u, js in unit.items()}
        ready = sorted((uk[u], unit[u][0], u) for u in unit if not left[u])
        done = 0

        def place(js, t0):
            got = []
            for j in js:
                t = max([st[d] + cost[d] + l for d, l in edges[j]] + [t0])
                if ops[j]["q"] is not None:
                    ln = lanes.setdefault(ops[j]["q"], [])
                    t, k = gap(ln, t, cost[j])
                    ln.insert(k, (t, t + cost[j])); got.append((ln, k))
                st[j] = t
            return got
        while ready:
            u = ready.pop(0)[2]
            js = unit[u][::-1] if back else unit[u]
            done += len(js)
            if isinstance(u, str):
                best = None
                for b in BANKS:
                    t0 = 0.0
                    while True:
                        for ln, k in place(js, t0)[::-1]:
                            ln.pop(k)
                        a, e = min(st[j] for j in js), max(st[j] + cost[j] for j in js) + LAT
                        t, k = gap(lanes[b], a, e - a)
                        if t == a:
                            break
                        t0 = t
                    if best is None or e < best[0]:
                        best = (e, b, t0, a, k)
                place(js, best[2])
                lanes[best[1]].insert(best[4], (best[3], best[0])); bank[u] = best[1]
            else:
                place(js, 0.0)
            for v in nxt.get(u, []):
                left[v] -= 1
                if not left[v]:
                    ready.append((uk[v], unit[v][0], v))
            ready.sort()
        assert done == n
        return st, bank

    tail = [0.0] * n
    for j in range(n - 1, -1, -1):
        tail[j] = cost[j] + max([tail[x] + l for x, l in suc[j]] or [ops[j]["lat"]])
    key = [-t for t in tail]
    best = None
    for it in range(2 * SWEEPS):
        if it == SWEEPS:
            key = list(range(n))
        st, bank = sweep(key, pre, False)
        end = max(st[j] + cost[j] + ops[j]["lat"] for j in range(n))
        if best is None or end < best[0]:
            best = (end, st, bank)
        bk = sweep([-st[j] - cost[j] for j in range(n)], suc, True)[0]
        key = [-bk[j] - cost[j] for j in range(n)]
    seed, tags = SEED, sorted({o["tag"] for o in ops})
    FOUND[:] = []
    for it in MOVES + list(range(SEED, SEED + TRIES)):
        sh, seed, was = {}, it * 2654435761 % 2147483648, best[0]
        FOUND.append(it)
        for _ in range(1 + it % 3):
            seed = (seed * 1103515245 + 12345) % 2147483648
            sh[tags[(seed >> 8) % len(tags)]] = ((seed >> 16) % 33 - 16) * (150 if it % 2 else 600)
        rd = it // 7 % 8
        key = [best[1][j] + (sh.get(ops[j]["tag"], 0) if rd > 3 or ops[j]["rd"] == rd else 0) for j in range(n)]
        for again in range(2):
            st, bank = sweep(key, pre, False)
            end = max(st[j] + cost[j] + ops[j]["lat"] for j in range(n))
            if end < best[0] - 20:
                best = (end, st, bank)
            if again or end > best[0] + 4000 or it % 4:
                break
            bk = sweep([-st[j] - cost[j] for j in range(n)], suc, True)[0]
            key = [-bk[j] - cost[j] for j in range(n)]
        if best[0] == was:
            FOUND.pop()
    end, st, bank = best
    last = {}
    for u in sorted(bank, key=lambda u: min(st[j] for j in unit[u])):
        for d in last.get(bank[u], []):
            for j in unit[u]:
                ops[j]["deps"][d] = ops[j]["deps"].get(d, False) or ops[j]["q"] != ops[d]["q"] or ops[j]["q"] != "p"
        last[bank[u]] = unit[u]
    return sorted(range(n), key=lambda j: (st[j], j)), st, bank


def graph(ops):
    n = len(ops)
    pre = [[(d, (ops[d]["lat"] + LAT) if w else 0.0) for d, w in o["deps"].items()] for o in ops]
    suc = [[] for _ in range(n)]
    unit = {}
    for j in range(n):
        if ops[j]["use"]:
            unit.setdefault(ops[j]["use"], []).append(j)
        for d, l in pre[j]:
            suc[d].append((j, l))
    G = {}
    for back, ed in ((False, pre), (True, suc)):
        gate = [set(d for d, l in ed[j]) for j in range(n)]
        opens = [False] * n
        for u, js in unit.items():
            s = set(js)
            js = js[::-1] if back else js
            for j in js:
                gate[js[0]] |= {d for d, l in ed[j] if d not in s}
                if j != js[0]:
                    gate[j].add(js[0])
            opens[js[0]] = True
        nx = [[] for _ in range(n)]
        for j in range(n):
            for d in gate[j]:
                nx[d].append(j)
        G[back] = (ed, [len(g) for g in gate], nx, opens)
    return G, unit


def sweep(ops, G, unit, key, back, delta):
    ed, cnt, nx, opens = G[back]
    n, cnt = len(ops), list(cnt)
    cost, q, use = [o["cost"] for o in ops], [o["q"] for o in ops], [o["use"] for o in ops]
    st, rdy, free = [0.0] * n, [0.0] * n, {x: 0.0 for x in q}
    bfree = {b: 0.0 for b in BANKS}
    bank, left, uend = {}, {u: len(js) for u, js in unit.items()}, {}
    el = [j for j in range(n) if not cnt[j]]
    while el:
        tb = min(bfree.values())
        best, bc, es = -1, 1e18, []
        for j in el:
            t, f = rdy[j], free[q[j]]
            if f > t: t = f
            if opens[j] and tb > t: t = tb
            es.append(t)
            if t + cost[j] < bc:
                bc, best = t + cost[j], j
        qq = q[best]
        t0 = min(t for t, j in zip(es, el) if q[j] == qq)
        lim = t0 + delta * (bc - t0)
        pick, pk, pt = -1, 1e18, 0.0
        for t, j in zip(es, el):
            if q[j] == qq and t <= lim and key[j] < pk:
                pick, pk, pt = j, key[j], t
        j = pick
        el.remove(j)
        st[j] = pt
        if qq is not None:
            free[qq] = pt + cost[j]
        u = use[j]
        if u:
            if opens[j]:
                b = max((b for b in BANKS if bfree[b] <= pt), key=lambda b: bfree[b])
                bank[u] = b; bfree[b] = 1e17; uend[u] = 0.0
            uend[u] = max(uend[u], pt + cost[j])
            left[u] -= 1
            if not left[u]:
                bfree[bank[u]] = uend[u] + LAT
        for x in nx[j]:
            cnt[x] -= 1
            if not cnt[x]:
                rdy[x] = max([st[d] + cost[d] + l for d, l in ed[x]] or [0.0])
                el.append(x)
    return max(st[j] + cost[j] + (0 if back else ops[j]["lat"]) for j in range(n)), st, bank


def schedule(ops):
    G, unit = graph(ops)
    n, cost = len(ops), [o["cost"] for o in ops]
    tail = [0.0] * n
    for j in range(n - 1, -1, -1):
        tail[j] = cost[j] + max([tail[x] + l for x, l in G[True][0][j]] or [ops[j]["lat"]])
    best = None
    for delta in (0.0, 0.3, 0.6, 1.0):
        key = [-t for t in tail]
        for it in range(SWEEPS):
            r = sweep(ops, G, unit, key, False, delta)
            if best is None or r[0] < best[0]:
                best = r + (delta, key)
            bk = sweep(ops, G, unit, [-r[1][j] - cost[j] for j in range(n)], True, delta)[1]
            key = [-bk[j] - cost[j] for j in range(n)]
    seed = [SEED]

    def pick(a):
        seed[0] = (seed[0] * 1103515245 + 12345) % 2147483648
        return a[(seed[0] >> 8) % len(a)]
    kinds = sorted({(o["tag"], o["rd"]) for o in ops})
    for it in range(TRIES):
        sh, every = {}, pick((1, 0, 0))
        for _ in range(pick((1, 2))):
            t, rd = pick(kinds)
            v = pick((-1, 1)) * pick((300, 1000, 3000, 8000))
            for x in range(4) if every else (rd,):
                sh[(t, x)] = v
        base = best[pick((4, 4, 1))]
        key = [base[j] + sh.get((o["tag"], o["rd"]), 0) for j, o in enumerate(ops)]
        r = sweep(ops, G, unit, key, False, best[3])
        if r[0] < best[0]:
            best = r + (best[3], key)
    end, st, bank = best[:3]
    last = {}
    for u in sorted(bank, key=lambda u: min(st[j] for j in unit[u])):
        for d in last.get(bank[u], []):
            for j in unit[u]:
                ops[j]["deps"][d] = ops[j]["deps"].get(d, False) or ops[j]["q"] != ops[d]["q"] or ops[j]["q"] != "p"
        last[bank[u]] = unit[u]
    return sorted(range(n), key=lambda j: (st[j], j)), st, bank


def plan():
    ops = build()
    order, start, bank = schedule(ops)
    cnt, known, snap, out = {}, {}, {}, []
    used = set()
    for o in ops:
        for d, w in o["deps"].items():
            if w and o["kind"] != "r":
                used.add(d)
    for j in order:
        o = ops[j]; q = o["q"]
        if o["kind"] == "r":
            snap[j] = {}
            continue
        kn = known.setdefault(q, {})
        waits = {}
        for d in sorted((d for d, w in o["deps"].items() if w), key=lambda d: -start[d]):
            s, v = ops[d]["sem"]
            if kn.get(s, 0) < v:
                waits[s] = max(waits.get(s, 0), v)
                kn[s] = v
                for s2, v2 in snap[d].items():
                    kn[s2] = max(kn.get(s2, 0), v2)
        if o["kind"] == "c" and j in used:
            cnt[q] = cnt.get(q, 0) + 1
            o["sem"] = (QSEM[q], cnt[q])
        snap[j] = dict(kn)
        out.append((q, waits, o["calls"], o["sem"], o["kind"]))
    fin = [(QSEM[q], c) for q, c in cnt.items()] + [o["sem"] for o in ops if o["kind"] in ("d", "r")]
    fin.append(("sent", 8 * sum(o["kind"] == "s" for o in ops)))
    return out, fin, bank


PLAN = []


def rank_program(g, core, T, topo):
    rank = T.rank_of(core)
    if rank is None:
        return
    if not PLAN:
        PLAN.append(plan())
    prog, fin, bank = PLAN[0]
    eng = {"v": g.vector, "a": g.scalar, "p": g.tensor, "s": g.sync, "g": g}

    def ap(x):
        if not is_ref(x):
            return x
        if x[0] == "ind":
            return ap(x[1]).indirect(ap(x[2]))
        t = T[bank.get(x[1], x[1])]
        return t[(slice(None) if x[3] is None else slice(x[3][0], x[3][1]),) + (x[2] or (slice(0, t.shape[1]),))]

    def send(src, u, dst, d0, sem):
        trs = []
        for d in range(1, 4):
            to = T.cores[rank ^ d]
            assert topo.may_write(core, to)
            e = topo.engines(core, to)
            use = (e[0:3:2], e[4:7:2], e[1:8:2])[d - 1]
            rid, pid, _ = topo.addr(to)
            a = 256 * (d - 1)
            trs.append(RemoteDMATransfer(dst_ids=[DstId(rid=rid, pnc=pid)], dma_engine_mask=sum(1 << x for x in use), remote_sem=T.sem[sem],
                                         src=T[src][:, 768 * u + a:768 * u + a + 256], dst=T[dst][:, d0 + a:d0 + a + 256]))
        g.remote_dma_fused(trs, local_sem=T.sem.sent)

    for q, waits, calls, sem, kind in prog:
        e = eng[q]
        for s, v in waits.items():
            e.wait_ge(T.sem[s], v)
        for meth, args, kw in calls:
            if meth == "send":
                send(*args)
                continue
            a = [ap(x) for x in args]
            k = {n: ap(x) for n, x in kw.items()}
            if meth == "matmul": r = e.matmul(*a)
            elif meth == "activation": r = e.activation(*a, **k)
            elif meth == "tensor_tensor": r = e.tensor_tensor(*a)
            elif meth == "tensor_scalar": r = e.tensor_scalar(*a)
            elif meth == "tensor_copy": r = e.tensor_copy(*a)
            elif meth == "memset": r = e.memset(*a)
            elif meth == "tensor_tensor_scan": r = e.tensor_tensor_scan(*a)
            elif meth == "iota": r = e.iota(*a, **k)
            elif meth == "affine_select": r = e.affine_select(*a)
            else: r = e.dma_start(*a)
        if kind == "d":
            r.then_inc(T.sem[sem[0]], 16)
        elif kind == "c" and sem is not None:
            r.then_inc(T.sem[sem[0]], 1)
    for s, v in fin:
        g.wait_ge(T.sem[s], v)
